import numpy as np
import ml_dtypes


def mxq(x, axis, fmt="e4m3"):
    dtype, down = {"e4m3": (ml_dtypes.float8_e4m3fn, 7), "e5m2": (ml_dtypes.float8_e5m2, 14)}[fmt]
    v = np.moveaxis(np.asarray(x, np.float32).astype(ml_dtypes.bfloat16).astype(np.float64), axis, -1)
    blocks = v.reshape(v.shape[:-1] + (-1, 32))
    amax = np.abs(blocks).max(-1, keepdims=True)
    byte = np.maximum(np.where(amax > 0, np.frexp(amax)[1] - 1 + 127, 0) - down, 1)
    scale = np.exp2(byte - 127.0)
    codes = (blocks / scale).astype(np.float32).astype(dtype).astype(np.float64)
    return np.moveaxis((codes * scale).reshape(v.shape), -1, axis)


WIDE = False


def mx_kscale(k):
    if not WIDE:
        return np.ones(k)
    levels = np.array([10, -10, 5, -5, 0])
    if k % 512:
        return np.exp2(np.random.permutation(np.resize(levels, k // 32))).repeat(32)
    a = np.empty((k // 512, 16))
    for p in range(k // 512):
        a[p, :8] = np.random.permutation(np.resize(levels, 8))
        for g in range(8):
            far = levels[np.abs(levels - a[p, g]) >= 10]
            a[p, g + 8] = far[np.random.randint(len(far))]
    return np.exp2(a.ravel()).repeat(32)


def f64(x):
    return np.asarray(x).astype(np.float64)


def striped(idx):
    return np.tile(idx.reshape(-1, 16).T, (8, 1)).astype(np.uint16)


def unstriped(offs):
    return offs[:16].T.reshape(-1).astype(np.int64)


E2M1 = np.array([0.0, 0.5, 1.0, 1.5, 2.0, 3.0, 4.0, 6.0, -0.0, -0.5, -1.0, -1.5, -2.0, -3.0, -4.0, -6.0])


def pack_weight(w, fmt):
    k, n = w.shape
    w = f64(np.asarray(w, np.float32).astype(ml_dtypes.bfloat16)).reshape(k // 32, 32, n)
    amax = np.abs(w).max(1)
    if fmt == "e4m3":
        byte = np.frexp(amax)[1] - 1 + 127 - 7
    else:
        mant, ex = np.frexp(amax / 6.0)
        byte = np.where(mant > 0.5, ex, ex - 1) + 127
    byte = np.clip(np.where(amax > 0, byte, 1), 1, 254)
    scaled = (w * np.exp2(127.0 - byte)[:, None, :]).reshape(k, n).astype(np.float32)
    by_word = np.ascontiguousarray(scaled.reshape(k // 512, 128, 4, n).transpose(0, 1, 3, 2))
    if fmt == "e4m3":
        words = by_word.astype(ml_dtypes.float8_e4m3fn).view(np.uint8)
    else:
        c = by_word.astype(ml_dtypes.float4_e2m1fn).view(np.uint8) & 0xF
        words = (c[..., 0::2] | (c[..., 1::2] << 4)).reshape(k // 512, 128, 2 * n)
    return np.ascontiguousarray(words), np.ascontiguousarray(byte.astype(np.uint8).reshape(k // 512, 16, n))


def unpack_weight(words, scales, fmt):
    g, _, n = scales.shape
    words = np.ascontiguousarray(words).reshape(g, 128, n, -1)
    if fmt == "e4m3":
        vals = words.view(ml_dtypes.float8_e4m3fn).astype(np.float64)
    else:
        nib = np.empty((g, 128, n, 4), np.uint8)
        nib[..., 0::2] = words & 0xF
        nib[..., 1::2] = words >> 4
        vals = E2M1[nib]
    vals = vals * np.repeat(np.exp2(scales.astype(np.float64) - 127.0), 8, axis=1)[..., None]
    return vals.transpose(0, 1, 3, 2).reshape(g * 512, n)


def gelu(v):
    return 0.5 * v * (1.0 + np.tanh(np.sqrt(2.0 / np.pi) * (v + 0.044715 * v**3)))


K, T, S, H, N = 512, 2048, 1024, 1024, 384

def setup_inputs():
    n = np.random.standard_normal
    s = mx_kscale(K)[:, None]
    u = mx_kscale(H)[:, None]
    tab_words, tab_scales = pack_weight(n((K, T)) * s, "e4m3")
    wr_words, wr_scales = pack_weight(n((K, H)) / np.sqrt(K) / s, "e2m1")
    wg_words, wg_scales = pack_weight(n((K, H)) / np.sqrt(K) / s * u.T, "e4m3")
    return {
        "tab_words": tab_words, "tab_scales": tab_scales,
        "offs": striped(np.random.permutation(T)[:S]),
        "offs2": striped(np.random.permutation(T)[:S]),
        "offs3": striped(np.random.permutation(T)[:S]),
        "ws": (n((K, H)) / np.sqrt(K) / s).astype(np.float32),
        "wr_words": wr_words, "wr_scales": wr_scales,
        "wg_words": wg_words, "wg_scales": wg_scales,
        "lo": (-0.9 * np.exp(0.3 * n(H))).astype(np.float32),
        "hi": (0.9 * np.exp(0.3 * n(H))).astype(np.float32),
        "wm": (n((H, N)) / np.sqrt(H) / u).astype(np.float32),
        "trim": (0.5 * n(N)).astype(np.float32),
    }

def reference(tab_words, tab_scales, offs, offs2, offs3, ws, wr_words, wr_scales, wg_words, wg_scales, lo, hi, wm, trim):
    v = unpack_weight(tab_words, tab_scales, "e4m3")[:, unstriped(offs)]
    v2 = unpack_weight(tab_words, tab_scales, "e4m3")[:, unstriped(offs2)]
    v3 = unpack_weight(tab_words, tab_scales, "e4m3")[:, unstriped(offs3)]
    wr = unpack_weight(wr_words, wr_scales, "e2m1")
    wg = unpack_weight(wg_words, wg_scales, "e4m3")
    a = mxq(f64(ws), 0, "e4m3").T @ v + wr.T @ v2
    c = np.maximum(np.minimum(a, f64(hi)[:, None]), f64(lo)[:, None])
    h = c * (wg.T @ v3)
    y = mxq(f64(wm), 0, "e4m3").T @ mxq(h, 0, "e4m3")
    return y + f64(trim)[:, None]

@@ -1,0 +1,308 @@
+from contextlib import ExitStack
+
+import concourse.mybir as mybir
+from concourse.masks import make_identity
+
+K, T, S, H, N = 512, 2048, 1024, 1024, 384
+FLOPS = 2 * S * H * (3 * K + N)
+
+F32 = mybir.dt.float32
+BF16 = mybir.dt.bfloat16
+I32 = mybir.dt.int32
+U32 = mybir.dt.uint32
+U16 = mybir.dt.uint16
+U8 = mybir.dt.uint8
+FP8X4 = mybir.dt.float8_e4m3fn_x4
+FP4X4 = mybir.dt.float4_e2m1fn_x4
+ALU = mybir.AluOpType
+ACT = mybir.ActivationFunctionType
+
+P = 128
+PACK = 4
+HALF = 512
+PASSES = H // HALF
+TILES = H // P
+CHUNK = 512
+CHUNKS = S // CHUNK
+UNIT = 128
+N_TILES = N // P
+GROUPS = ((0, 512), (512, 256), (768, 128), (896, 128))
+LO, HI, TRIM = 0, TILES, 2 * TILES
+
+
+def tile_list_scheduled_gain_mixing_kernel(
+    tc, tab_words, tab_scales, offs, offs2, offs3, ws, wr_words, wr_scales, wg_words, wg_scales, lo, hi, wm, trim, out
+):
+    nc = tc.nc
+    with ExitStack() as ctx:
+        keep = ctx.enter_context(tc.tile_pool(name="keep", bufs=1))
+        shared = ctx.enter_context(tc.tile_pool(name="shared", bufs=1))
+        psum = ctx.enter_context(tc.psum_pool(name="psum", bufs=1))
+
+        def held(name, shape, dtype):
+            return keep.tile(shape, dtype, name=name, align_bytes=64)
+
+        lists = [held("list%d" % i, [P, S // 16], U16) for i in range(3)]
+        table_words = held("table_words", [P, T], I32)
+        table_scales = held("table_scales", [P, T // 4], I32)
+        wr_raw_scales = held("wr_raw_scales", [P, H // 4], I32)
+        wg_raw_scales = held("wg_raw_scales", [P, H // 4], I32)
+        wr_raw = held("wr_raw", [P, H // 2], I32)
+        wg_raw = held("wg_raw", [P, H], I32)
+        ws_raw = [held("ws_raw%d" % b, [P, PACK, HALF], F32) for b in range(PASSES)]
+        wm_raw = [held("wm_raw%d" % b, [P, PACK, N], F32) for b in range(PASSES)]
+        rows = held("rows", [P, P], F32)
+        identity = held("identity", [P, P], F32)
+
+        nc.vector.memset(table_scales[:], 0)
+        nc.vector.memset(rows[:], 0.0)
+        nc.vector.memset(wr_raw_scales[:], 0)
+        nc.vector.memset(wg_raw_scales[:], 0)
+        make_identity(nc, identity[:])
+
+        def load_scale_rows(plane, scales):
+            for quadrant in range(4):
+                nc.sync.dma_start(
+                    plane[32 * quadrant : 32 * quadrant + 4, :],
+                    scales[0, 4 * quadrant : 4 * quadrant + 4, :].bitcast(I32),
+                )
+
+        def load_ws(b):
+            nc.sync.dma_start(ws_raw[b][:], ws[:, b * HALF : (b + 1) * HALF].rearrange("(p j) c -> p j c", j=PACK))
+
+        nc.sync.dma_start(lists[0][:], offs)
+        nc.sync.dma_start(lists[1][:], offs2)
+        load_scale_rows(table_scales, tab_scales)
+        nc.sync.dma_start(table_words[:], tab_words[0].rearrange("p n t -> p (n t)").bitcast(I32))
+        nc.sync.dma_start(lists[2][:], offs3)
+        load_ws(0)
+        for first, vector in ((LO, lo), (HI, hi)):
+            for b in range(PASSES):
+                nc.gpsimd.dma_start(
+                    rows[first + PACK * b : first + PACK * (b + 1), :].rearrange("t (q i) -> t q i", i=8),
+                    vector[b * HALF : (b + 1) * HALF].rearrange("(q t i) -> t q i", t=PACK, i=8),
+                )
+        nc.gpsimd.dma_start(rows[TRIM : TRIM + N_TILES, :], trim.rearrange("(n p) -> n p", p=P))
+        nc.sync.dma_start(wr_raw[:], wr_words[0].bitcast(I32))
+        load_scale_rows(wr_raw_scales, wr_scales)
+        load_ws(1)
+        nc.sync.dma_start(wg_raw[:], wg_words[0].rearrange("p n t -> p (n t)").bitcast(I32))
+        load_scale_rows(wg_raw_scales, wg_scales)
+        for b in range(PASSES):
+            wm_rows = wm[b * HALF : (b + 1) * HALF, :].rearrange("(q t i) n -> t q i n", t=PACK, i=8)
+            for t in range(PACK):
+                nc.sync.dma_start(wm_raw[b][:, t, :], wm_rows[t])
+
+        columns = held("columns", [P, 32], F32)
+
+        def reused(name, shape, dtype, offset):
+            return shared.tile(shape, dtype, name=name, align_bytes=64, offset=offset)
+
+        ws_grouped = [reused("ws_grouped%d" % b, [P, PACK, HALF], BF16, 4096 * b) for b in range(PASSES)]
+        picked_words = [
+            [held("words%d_0" % i, [P, CHUNK], U32), reused("words%d_1" % i, [P, CHUNK], U32, 2048 * i)]
+            for i in range(2)
+        ]
+        picked_words.append([reused("words2_%d" % c, [P, CHUNK], U32, 4096 + 2048 * c) for c in range(CHUNKS)])
+        picked_scales = [[held("scales%d_%d" % (i, c), [P, CHUNK], U8) for c in range(CHUNKS)] for i in range(3)]
+
+        def offsets(i, c):
+            return lists[i][:, c * CHUNK // 16 : (c + 1) * CHUNK // 16]
+
+        def gather_scales(i, c):
+            nc.vector.tensor_copy(picked_scales[i][c][:], table_scales[:].bitcast(U8).indirect(offsets(i, c)))
+
+        def gather_words(i, c):
+            nc.vector.tensor_copy(picked_words[i][c][:], table_words[:].bitcast(U32).indirect(offsets(i, c)))
+
+        def reorder_columns(name, raw, run):
+            moved = held(name, [P, raw.shape[1]], I32)
+            nc.vector.tensor_copy(
+                moved[:].rearrange("p (b t q e) -> p b t q e", b=PASSES, t=PACK, e=run),
+                raw[:].rearrange("p (b q t e) -> p b t q e", b=PASSES, t=PACK, e=run),
+            )
+            return moved
+
+        ws_codes = held("ws_codes", [P, H], U32)
+        ws_scales = held("ws_scales", [P, H], U8)
+
+        def round_ws(b):
+            source = ws_raw[b][:].rearrange("p j (q t h l) -> p t q h j l", t=PACK, h=2, l=4)
+            for t in range(PACK):
+                nc.scalar.copy(
+                    ws_grouped[b][:, t, :].rearrange("p (q h l j) -> p q h j l", h=2, l=4, j=PACK), source[:, t]
+                )
+
+        def quantize_ws(b):
+            cols = slice(b * HALF, (b + 1) * HALF)
+            nc.vector.quantize_mx(
+                out=ws_codes[:, cols].bitcast(FP8X4),
+                scales=ws_scales[:, cols],
+                in_=ws_grouped[b][:].rearrange("p t c -> p (t c)"),
+            )
+
+        wm_codes = held("wm_codes", [P, PASSES * N], U32)
+        wm_scales = held("wm_scales", [P, PASSES * N], U8)
+        wm_grouped = held("wm_grouped", [P, PASSES * N * PACK], BF16)
+
+        def round_wm(b):
+            nc.scalar.copy(
+                wm_grouped[:, b * N * PACK : (b + 1) * N * PACK].rearrange("p (h l t) -> p h t l", l=4, t=PACK),
+                wm_raw[b][:].rearrange("p t (h l) -> p h t l", l=4),
+            )
+
+        def quantize_wm():
+            for first, last in ((0, 512), (512, 768)):
+                nc.vector.quantize_mx(
+                    out=wm_codes[:, first:last].bitcast(FP8X4),
+                    scales=wm_scales[:, first:last],
+                    in_=wm_grouped[:, PACK * first : PACK * last],
+                )
+
+        clamped = [[held("clamped%d_%d" % (c, b), [P, PACK, CHUNK], F32) for b in range(PASSES)] for c in range(CHUNKS)]
+
+        demands = [[held("demand%d_%d" % (c, b), [P, PACK, CHUNK], F32) for b in range(PASSES)] for c in range(CHUNKS)]
+
+        def demand(c, b, wr_codes, wr_planes):
+            for t in range(PACK):
+                u = PACK * b + t
+                cols = slice(u * P, (u + 1) * P)
+                acc = psum.tile([P, CHUNK], F32, name="demand", tag="demand", bufs=2)
+                nc.tensor.matmul_mx(
+                    out=acc[:],
+                    lhsT=ws_codes[:, cols].bitcast(FP8X4),
+                    lhsT_scale=ws_scales[:, cols],
+                    rhs=picked_words[0][c][:].bitcast(FP8X4),
+                    rhs_scale=picked_scales[0][c][:],
+                    start=True,
+                    stop=False,
+                )
+                nc.tensor.matmul_mx(
+                    out=acc[:],
+                    lhsT=wr_codes[:].bitcast(U8)[:, 2 * u * P : 2 * (u + 1) * P].bitcast(FP4X4),
+                    lhsT_scale=wr_planes[:].bitcast(U8)[:, cols],
+                    rhs=picked_words[1][c][:].bitcast(FP8X4),
+                    rhs_scale=picked_scales[1][c][:],
+                    start=False,
+                    stop=True,
+                )
+                nc.scalar.copy(demands[c][b][:, t, :], acc[:])
+
+        def clamp(c, b):
+            for t in range(PACK):
+                u = PACK * b + t
+                nc.gpsimd.tensor_scalar(
+                    clamped[c][b][:, t, :],
+                    demands[c][b][:, t, :],
+                    columns[:, HI + u : HI + u + 1],
+                    columns[:, LO + u : LO + u + 1],
+                    ALU.min,
+                    ALU.max,
+                )
+
+        def gain_times_demand(h, first, j0, b, wg_codes, wg_planes):
+            c, at = divmod(j0, CHUNK)
+            gain = psum.tile([P, PACK, UNIT], F32, name="gain", tag="gain", bufs=3)
+            for t in range(PACK):
+                cols = slice((PACK * b + t) * P, (PACK * b + t + 1) * P)
+                nc.tensor.matmul_mx(
+                    out=gain[:, t, :],
+                    lhsT=wg_codes[:, cols].bitcast(FP8X4),
+                    lhsT_scale=wg_planes[:].bitcast(U8)[:, cols],
+                    rhs=picked_words[2][c][:, at : at + UNIT].bitcast(FP8X4),
+                    rhs_scale=picked_scales[2][c][:, at : at + UNIT],
+                    start=True,
+                    stop=True,
+                )
+            nc.vector.tensor_tensor(
+                h[:, b, PACK * (j0 - first) : PACK * (j0 - first + UNIT)].rearrange(
+                    "p (h l t) -> p h t l", l=4, t=PACK
+                ),
+                gain[:].rearrange("p t (h l) -> p h t l", l=4),
+                clamped[c][b][:, :, at : at + UNIT].rearrange("p t (h l) -> p h t l", l=4),
+                ALU.mult,
+            )
+
+        def quantize_h(g, h):
+            width = GROUPS[g][1]
+            h_codes = held("h_codes%d" % g, [P, PASSES * width], U32)
+            h_scales = held("h_scales%d" % g, [P, PASSES * width], U8)
+            nc.vector.quantize_mx(
+                out=h_codes[:].bitcast(FP8X4), scales=h_scales[:], in_=h[:].rearrange("p b c -> p (b c)")
+            )
+            return h_codes, h_scales
+
+        def mix(g, h_codes, h_scales):
+            first, width = GROUPS[g]
+            result = held("result%d" % g, [P, N_TILES, width], F32)
+            for n in range(N_TILES):
+                acc = psum.tile([P, width], F32, name="mix", tag="mix", bufs=3)
+                for b in range(PASSES):
+                    cols = slice(b * N + n * P, b * N + (n + 1) * P)
+                    nc.tensor.matmul_mx(
+                        out=acc[:],
+                        lhsT=wm_codes[:, cols].bitcast(FP8X4),
+                        lhsT_scale=wm_scales[:, cols],
+                        rhs=h_codes[:, b * width : (b + 1) * width].bitcast(FP8X4),
+                        rhs_scale=h_scales[:, b * width : (b + 1) * width],
+                        start=(b == 0),
+                        stop=(b == PASSES - 1),
+                    )
+                trim_column = columns[:, TRIM + n : TRIM + n + 1]
+                if g == len(GROUPS) - 1 and n == 1:
+                    nc.vector.tensor_scalar(result[:, n, :], acc[:], trim_column, None, ALU.add)
+                else:
+                    nc.scalar.activation(result[:, n, :], acc[:], ACT.Identity, bias=trim_column)
+            nc.sync.dma_start(out[:, first : first + width].rearrange("(n p) j -> p n j", p=P), result[:])
+
+        for i in range(2):
+            gather_scales(i, 0)
+        for i in range(2):
+            gather_words(i, 0)
+        for i in range(2):
+            gather_scales(i, 1)
+        for c in range(CHUNKS):
+            gather_scales(2, c)
+        round_ws(0)
+        rows_turned = psum.tile([P, P], F32, name="rows_turned", tag="mix", bufs=3)
+        nc.tensor.transpose(rows_turned[:], rows[:], identity[:])
+        nc.scalar.copy(columns[:], rows_turned[:, 0:32])
+        round_ws(1)
+        wr_codes = reorder_columns("wr_codes", wr_raw, 4)
+        wr_planes = reorder_columns("wr_planes", wr_raw_scales, 2)
+        quantize_ws(0)
+        quantize_ws(1)
+        for i in range(2):
+            gather_words(i, 1)
+        wg_codes = reorder_columns("wg_codes", wg_raw, 8)
+        wg_planes = reorder_columns("wg_planes", wg_raw_scales, 2)
+        for c in range(CHUNKS):
+            gather_words(2, c)
+        for c, b in ((0, 0), (0, 1), (1, 0)):
+            demand(c, b, wr_codes, wr_planes)
+            clamp(c, b)
+        round_wm(0)
+        round_wm(1)
+        demand(1, 1, wr_codes, wr_planes)
+        clamp(1, 1)
+
+        h = [held("h%d" % g, [P, PASSES, PACK * width], BF16) for g, (first, width) in enumerate(GROUPS)]
+
+        def units(g, b):
+            first, width = GROUPS[g]
+            for j0 in range(first, first + width, UNIT):
+                gain_times_demand(h[g], first, j0, b, wg_codes, wg_planes)
+
+        units(0, 0)
+        units(0, 1)
+        units(1, 0)
+        quantize_wm()
+        mix(0, *quantize_h(0, h[0]))
+        units(2, 0)
+        units(3, 0)
+        units(1, 1)
+        units(2, 1)
+        mix(1, *quantize_h(1, h[1]))
+        units(3, 1)
+        mix(2, *quantize_h(2, h[2]))
+        mix(3, *quantize_h(3, h[3]))

@@ -167,7 +167,7 @@ def tile_list_scheduled_gain_mixing_kernel(
             for t in range(PACK):
                 u = PACK * b + t
                 cols = slice(u * P, (u + 1) * P)
-                acc = psum.tile([P, CHUNK], F32, name="demand", tag="demand", bufs=2)
+                acc = psum.tile([P, CHUNK], F32, name="demand", tag="first", bufs=5)
                 nc.tensor.matmul_mx(
                     out=acc[:],
                     lhsT=ws_codes[:, cols].bitcast(FP8X4),
@@ -191,7 +191,7 @@ def tile_list_scheduled_gain_mixing_kernel(
         def clamp(c, b):
             for t in range(PACK):
                 u = PACK * b + t
-                nc.gpsimd.tensor_scalar(
+                nc.vector.tensor_scalar(
                     clamped[c][b][:, t, :],
                     demands[c][b][:, t, :],
                     columns[:, HI + u : HI + u + 1],
@@ -202,7 +202,7 @@ def tile_list_scheduled_gain_mixing_kernel(
 
         def gain_times_demand(h, first, j0, b, wg_codes, wg_planes):
             c, at = divmod(j0, CHUNK)
-            gain = psum.tile([P, PACK, UNIT], F32, name="gain", tag="gain", bufs=3)
+            gain = psum.tile([P, PACK, UNIT], F32, name="gain", tag="first", bufs=5)
             for t in range(PACK):
                 cols = slice((PACK * b + t) * P, (PACK * b + t + 1) * P)
                 nc.tensor.matmul_mx(
@@ -278,13 +278,12 @@ def tile_list_scheduled_gain_mixing_kernel(
         wg_planes = reorder_columns("wg_planes", wg_raw_scales, 2)
         for c in range(CHUNKS):
             gather_words(2, c)
-        for c, b in ((0, 0), (0, 1), (1, 0)):
-            demand(c, b, wr_codes, wr_planes)
-            clamp(c, b)
+        for c in range(CHUNKS):
+            for b in range(PASSES):
+                demand(c, b, wr_codes, wr_planes)
+                clamp(c, b)
         round_wm(0)
         round_wm(1)
-        demand(1, 1, wr_codes, wr_planes)
-        clamp(1, 1)
 
         h = [held("h%d" % g, [P, PASSES, PACK * width], BF16) for g, (first, width) in enumerate(GROUPS)]
 

@@ -42,6 +42,9 @@ def tile_list_scheduled_gain_mixing_kernel(
         def held(name, shape, dtype):
             return keep.tile(shape, dtype, name=name, align_bytes=64)
 
+        def reused(name, shape, dtype, offset):
+            return shared.tile(shape, dtype, name=name, align_bytes=64, offset=offset)
+
         lists = [held("list%d" % i, [P, S // 16], U16) for i in range(3)]
         table_words = held("table_words", [P, T], I32)
         table_scales = held("table_scales", [P, T // 4], I32)
@@ -49,13 +52,12 @@ def tile_list_scheduled_gain_mixing_kernel(
         wg_raw_scales = held("wg_raw_scales", [P, H // 4], I32)
         wr_raw = held("wr_raw", [P, H // 2], I32)
         wg_raw = held("wg_raw", [P, H], I32)
-        ws_raw = [held("ws_raw%d" % b, [P, PACK, HALF], F32) for b in range(PASSES)]
+        ws_raw = [reused("ws_raw%d" % b, [P, PACK, HALF], F32, 8192 * b) for b in range(PASSES)]
         wm_raw = [held("wm_raw%d" % b, [P, PACK, N], F32) for b in range(PASSES)]
         rows = held("rows", [P, P], F32)
         identity = held("identity", [P, P], F32)
 
-        nc.vector.memset(table_scales[:], 0)
-        nc.vector.memset(rows[:], 0.0)
+        nc.gpsimd.memset(rows[:], 0.0)
         nc.vector.memset(wr_raw_scales[:], 0)
         nc.vector.memset(wg_raw_scales[:], 0)
         make_identity(nc, identity[:])
@@ -70,22 +72,29 @@ def tile_list_scheduled_gain_mixing_kernel(
         def load_ws(b):
             nc.sync.dma_start(ws_raw[b][:], ws[:, b * HALF : (b + 1) * HALF].rearrange("(p j) c -> p j c", j=PACK))
 
-        nc.sync.dma_start(lists[0][:], offs)
-        nc.sync.dma_start(lists[1][:], offs2)
-        load_scale_rows(table_scales, tab_scales)
-        nc.sync.dma_start(table_words[:], tab_words[0].rearrange("p n t -> p (n t)").bitcast(I32))
-        nc.sync.dma_start(lists[2][:], offs3)
-        load_ws(0)
-        for first, vector in ((LO, lo), (HI, hi)):
+        def load_limits(queue, first, vector):
             for b in range(PASSES):
-                nc.gpsimd.dma_start(
+                queue.dma_start(
                     rows[first + PACK * b : first + PACK * (b + 1), :].rearrange("t (q i) -> t q i", i=8),
                     vector[b * HALF : (b + 1) * HALF].rearrange("(q t i) -> t q i", t=PACK, i=8),
                 )
+
+        load_limits(nc.gpsimd, LO, lo)
+        load_limits(nc.gpsimd, HI, hi)
         nc.gpsimd.dma_start(rows[TRIM : TRIM + N_TILES, :], trim.rearrange("(n p) -> n p", p=P))
-        nc.sync.dma_start(wr_raw[:], wr_words[0].bitcast(I32))
-        load_scale_rows(wr_raw_scales, wr_scales)
+        nc.sync.dma_start(lists[0][:], offs)
+        for quadrant in range(4):
+            nc.sync.dma_start(
+                table_scales[32 * quadrant : 32 * (quadrant + 1), :],
+                tab_scales[0, 4 * quadrant : 4 * quadrant + 4, :].bitcast(I32).unsqueeze(0).to_broadcast([8, 4, T // 4]),
+            )
+        nc.sync.dma_start(lists[1][:], offs2)
+        nc.sync.dma_start(table_words[:], tab_words[0].rearrange("p n t -> p (n t)").bitcast(I32))
+        load_ws(0)
         load_ws(1)
+        nc.sync.dma_start(wr_raw[:], wr_words[0].bitcast(I32))
+        nc.sync.dma_start(lists[2][:], offs3)
+        load_scale_rows(wr_raw_scales, wr_scales)
         nc.sync.dma_start(wg_raw[:], wg_words[0].rearrange("p n t -> p (n t)").bitcast(I32))
         load_scale_rows(wg_raw_scales, wg_scales)
         for b in range(PASSES):
@@ -93,18 +102,16 @@ def tile_list_scheduled_gain_mixing_kernel(
             for t in range(PACK):
                 nc.sync.dma_start(wm_raw[b][:, t, :], wm_rows[t])
 
-        columns = held("columns", [P, 32], F32)
+        columns = reused("columns", [P, 32], F32, 13312)
 
-        def reused(name, shape, dtype, offset):
-            return shared.tile(shape, dtype, name=name, align_bytes=64, offset=offset)
-
-        ws_grouped = [reused("ws_grouped%d" % b, [P, PACK, HALF], BF16, 4096 * b) for b in range(PASSES)]
-        picked_words = [
-            [held("words%d_0" % i, [P, CHUNK], U32), reused("words%d_1" % i, [P, CHUNK], U32, 2048 * i)]
+        ws_grouped = [reused("ws_grouped%d" % b, [P, PACK, HALF], BF16, 16384 + 4096 * b) for b in range(PASSES)]
+        picked_words = [[held("words%d_%d" % (i, c), [P, CHUNK], U32) for c in range(CHUNKS)] for i in range(2)]
+        picked_words.append([reused("words2_%d" % c, [P, CHUNK], U32, 8192 + 2048 * c) for c in range(CHUNKS)])
+        picked_scales = [
+            [held("scales%d_0" % i, [P, CHUNK], U8), reused("scales%d_1" % i, [P, CHUNK], U8, 512 * i)]
             for i in range(2)
         ]
-        picked_words.append([reused("words2_%d" % c, [P, CHUNK], U32, 4096 + 2048 * c) for c in range(CHUNKS)])
-        picked_scales = [[held("scales%d_%d" % (i, c), [P, CHUNK], U8) for c in range(CHUNKS)] for i in range(3)]
+        picked_scales.append([reused("scales2_%d" % c, [P, CHUNK], U8, 12288 + 512 * c) for c in range(CHUNKS)])
 
         def offsets(i, c):
             return lists[i][:, c * CHUNK // 16 : (c + 1) * CHUNK // 16]
@@ -115,8 +122,8 @@ def tile_list_scheduled_gain_mixing_kernel(
         def gather_words(i, c):
             nc.vector.tensor_copy(picked_words[i][c][:], table_words[:].bitcast(U32).indirect(offsets(i, c)))
 
-        def reorder_columns(name, raw, run):
-            moved = held(name, [P, raw.shape[1]], I32)
+        def reorder_columns(name, raw, run, offset):
+            moved = reused(name, [P, raw.shape[1]], I32, offset)
             nc.vector.tensor_copy(
                 moved[:].rearrange("p (b t q e) -> p b t q e", b=PASSES, t=PACK, e=run),
                 raw[:].rearrange("p (b q t e) -> p b t q e", b=PASSES, t=PACK, e=run),
@@ -191,7 +198,7 @@ def tile_list_scheduled_gain_mixing_kernel(
         def clamp(c, b):
             for t in range(PACK):
                 u = PACK * b + t
-                nc.vector.tensor_scalar(
+                nc.gpsimd.tensor_scalar(
                     clamped[c][b][:, t, :],
                     demands[c][b][:, t, :],
                     columns[:, HI + u : HI + u + 1],
@@ -257,27 +264,26 @@ def tile_list_scheduled_gain_mixing_kernel(
 
         for i in range(2):
             gather_scales(i, 0)
-        for i in range(2):
-            gather_words(i, 0)
-        for i in range(2):
-            gather_scales(i, 1)
         for c in range(CHUNKS):
-            gather_scales(2, c)
+            for i in range(2):
+                gather_words(i, c)
         round_ws(0)
         rows_turned = psum.tile([P, P], F32, name="rows_turned", tag="mix", bufs=3)
         nc.tensor.transpose(rows_turned[:], rows[:], identity[:])
-        nc.scalar.copy(columns[:], rows_turned[:, 0:32])
         round_ws(1)
-        wr_codes = reorder_columns("wr_codes", wr_raw, 4)
-        wr_planes = reorder_columns("wr_planes", wr_raw_scales, 2)
+        nc.scalar.copy(columns[:], rows_turned[:, 0:32])
+        wr_codes = reorder_columns("wr_codes", wr_raw, 4, 2048)
+        wr_planes = reorder_columns("wr_planes", wr_raw_scales, 2, 1024)
         quantize_ws(0)
         quantize_ws(1)
         for i in range(2):
-            gather_words(i, 1)
-        wg_codes = reorder_columns("wg_codes", wg_raw, 8)
-        wg_planes = reorder_columns("wg_planes", wg_raw_scales, 2)
-        for c in range(CHUNKS):
-            gather_words(2, c)
+            gather_scales(i, 1)
+        gather_scales(2, 0)
+        gather_words(2, 0)
+        wg_codes = reorder_columns("wg_codes", wg_raw, 8, 20480)
+        wg_planes = reorder_columns("wg_planes", wg_raw_scales, 2, 14336)
+        gather_scales(2, 1)
+        gather_words(2, 1)
         for c in range(CHUNKS):
             for b in range(PASSES):
                 demand(c, b, wr_codes, wr_planes)

@@ -57,6 +57,7 @@ def tile_list_scheduled_gain_mixing_kernel(
         rows = held("rows", [P, P], F32)
         identity = held("identity", [P, P], F32)
 
+        nc.vector.memset(table_scales[:], 0)
         nc.gpsimd.memset(rows[:], 0.0)
         nc.vector.memset(wr_raw_scales[:], 0)
         nc.vector.memset(wg_raw_scales[:], 0)
@@ -83,18 +84,14 @@ def tile_list_scheduled_gain_mixing_kernel(
         load_limits(nc.gpsimd, HI, hi)
         nc.gpsimd.dma_start(rows[TRIM : TRIM + N_TILES, :], trim.rearrange("(n p) -> n p", p=P))
         nc.sync.dma_start(lists[0][:], offs)
-        for quadrant in range(4):
-            nc.sync.dma_start(
-                table_scales[32 * quadrant : 32 * (quadrant + 1), :],
-                tab_scales[0, 4 * quadrant : 4 * quadrant + 4, :].bitcast(I32).unsqueeze(0).to_broadcast([8, 4, T // 4]),
-            )
         nc.sync.dma_start(lists[1][:], offs2)
+        nc.sync.dma_start(wr_raw[:], wr_words[0].bitcast(I32))
+        load_scale_rows(table_scales, tab_scales)
         nc.sync.dma_start(table_words[:], tab_words[0].rearrange("p n t -> p (n t)").bitcast(I32))
         load_ws(0)
         load_ws(1)
-        nc.sync.dma_start(wr_raw[:], wr_words[0].bitcast(I32))
-        nc.sync.dma_start(lists[2][:], offs3)
         load_scale_rows(wr_raw_scales, wr_scales)
+        nc.sync.dma_start(lists[2][:], offs3)
         nc.sync.dma_start(wg_raw[:], wg_words[0].rearrange("p n t -> p (n t)").bitcast(I32))
         load_scale_rows(wg_raw_scales, wg_scales)
         for b in range(PASSES):
@@ -105,31 +102,27 @@ def tile_list_scheduled_gain_mixing_kernel(
         columns = reused("columns", [P, 32], F32, 13312)
 
         ws_grouped = [reused("ws_grouped%d" % b, [P, PACK, HALF], BF16, 16384 + 4096 * b) for b in range(PASSES)]
-        picked_words = [[held("words%d_%d" % (i, c), [P, CHUNK], U32) for c in range(CHUNKS)] for i in range(2)]
-        picked_words.append([reused("words2_%d" % c, [P, CHUNK], U32, 8192 + 2048 * c) for c in range(CHUNKS)])
-        picked_scales = [
-            [held("scales%d_0" % i, [P, CHUNK], U8), reused("scales%d_1" % i, [P, CHUNK], U8, 512 * i)]
-            for i in range(2)
-        ]
-        picked_scales.append([reused("scales2_%d" % c, [P, CHUNK], U8, 12288 + 512 * c) for c in range(CHUNKS)])
+        picked_words = [held("words%d" % i, [P, S], U32) for i in range(2)]
+        picked_words.append(reused("words2", [P, S], U32, 8192))
+        picked_scales = [held("scales%d" % i, [P, S], U8) for i in range(2)]
+        picked_scales.append(reused("scales2", [P, S], U8, 12288))
 
-        def offsets(i, c):
-            return lists[i][:, c * CHUNK // 16 : (c + 1) * CHUNK // 16]
+        def gather_scales(i):
+            nc.vector.tensor_copy(picked_scales[i][:], table_scales[:].bitcast(U8).indirect(lists[i][:]))
 
-        def gather_scales(i, c):
-            nc.vector.tensor_copy(picked_scales[i][c][:], table_scales[:].bitcast(U8).indirect(offsets(i, c)))
+        def gather_words(i):
+            nc.vector.tensor_copy(picked_words[i][:], table_words[:].bitcast(U32).indirect(lists[i][:]))
 
-        def gather_words(i, c):
-            nc.vector.tensor_copy(picked_words[i][c][:], table_words[:].bitcast(U32).indirect(offsets(i, c)))
-
-        def reorder_columns(name, raw, run, offset):
-            moved = reused(name, [P, raw.shape[1]], I32, offset)
+        def reorder_columns(moved, raw, run):
             nc.vector.tensor_copy(
                 moved[:].rearrange("p (b t q e) -> p b t q e", b=PASSES, t=PACK, e=run),
                 raw[:].rearrange("p (b q t e) -> p b t q e", b=PASSES, t=PACK, e=run),
             )
-            return moved
 
+        wr_codes = held("wr_codes", [P, H // 2], I32)
+        wr_planes = reused("wr_planes", [P, H // 4], I32, 0)
+        wg_codes = reused("wg_codes", [P, H], I32, 20480)
+        wg_planes = reused("wg_planes", [P, H // 4], I32, 14336)
         ws_codes = held("ws_codes", [P, H], U32)
         ws_scales = held("ws_scales", [P, H], U8)
 
@@ -166,21 +159,22 @@ def tile_list_scheduled_gain_mixing_kernel(
                     in_=wm_grouped[:, PACK * first : PACK * last],
                 )
 
-        clamped = [[held("clamped%d_%d" % (c, b), [P, PACK, CHUNK], F32) for b in range(PASSES)] for c in range(CHUNKS)]
+        clamped = [held("clamped%d" % b, [P, PACK, S], F32) for b in range(PASSES)]
 
-        demands = [[held("demand%d_%d" % (c, b), [P, PACK, CHUNK], F32) for b in range(PASSES)] for c in range(CHUNKS)]
+        demands = [held("demand%d" % b, [P, PACK, S], F32) for b in range(PASSES)]
 
-        def demand(c, b, wr_codes, wr_planes):
-            for t in range(PACK):
-                u = PACK * b + t
-                cols = slice(u * P, (u + 1) * P)
+        def demand(u):
+            b, t = divmod(u, PACK)
+            cols = slice(u * P, (u + 1) * P)
+            for c in range(CHUNKS):
+                picks = slice(c * CHUNK, (c + 1) * CHUNK)
                 acc = psum.tile([P, CHUNK], F32, name="demand", tag="first", bufs=5)
                 nc.tensor.matmul_mx(
                     out=acc[:],
                     lhsT=ws_codes[:, cols].bitcast(FP8X4),
                     lhsT_scale=ws_scales[:, cols],
-                    rhs=picked_words[0][c][:].bitcast(FP8X4),
-                    rhs_scale=picked_scales[0][c][:],
+                    rhs=picked_words[0][:, picks].bitcast(FP8X4),
+                    rhs_scale=picked_scales[0][:, picks],
                     start=True,
                     stop=False,
                 )
@@ -188,27 +182,22 @@ def tile_list_scheduled_gain_mixing_kernel(
                     out=acc[:],
                     lhsT=wr_codes[:].bitcast(U8)[:, 2 * u * P : 2 * (u + 1) * P].bitcast(FP4X4),
                     lhsT_scale=wr_planes[:].bitcast(U8)[:, cols],
-                    rhs=picked_words[1][c][:].bitcast(FP8X4),
-                    rhs_scale=picked_scales[1][c][:],
+                    rhs=picked_words[1][:, picks].bitcast(FP8X4),
+                    rhs_scale=picked_scales[1][:, picks],
                     start=False,
                     stop=True,
                 )
-                nc.scalar.copy(demands[c][b][:, t, :], acc[:])
+                nc.scalar.copy(demands[b][:, t, picks], acc[:])
+            nc.vector.tensor_scalar(
+                clamped[b][:, t, :],
+                demands[b][:, t, :],
+                columns[:, HI + u : HI + u + 1],
+                columns[:, LO + u : LO + u + 1],
+                ALU.min,
+                ALU.max,
+            )
 
-        def clamp(c, b):
-            for t in range(PACK):
-                u = PACK * b + t
-                nc.gpsimd.tensor_scalar(
-                    clamped[c][b][:, t, :],
-                    demands[c][b][:, t, :],
-                    columns[:, HI + u : HI + u + 1],
-                    columns[:, LO + u : LO + u + 1],
-                    ALU.min,
-                    ALU.max,
-                )
-
-        def gain_times_demand(h, first, j0, b, wg_codes, wg_planes):
-            c, at = divmod(j0, CHUNK)
+        def gain_times_demand(h_tile, word, j0, b):
             gain = psum.tile([P, PACK, UNIT], F32, name="gain", tag="first", bufs=5)
             for t in range(PACK):
                 cols = slice((PACK * b + t) * P, (PACK * b + t + 1) * P)
@@ -216,98 +205,97 @@ def tile_list_scheduled_gain_mixing_kernel(
                     out=gain[:, t, :],
                     lhsT=wg_codes[:, cols].bitcast(FP8X4),
                     lhsT_scale=wg_planes[:].bitcast(U8)[:, cols],
-                    rhs=picked_words[2][c][:, at : at + UNIT].bitcast(FP8X4),
-                    rhs_scale=picked_scales[2][c][:, at : at + UNIT],
+                    rhs=picked_words[2][:, j0 : j0 + UNIT].bitcast(FP8X4),
+                    rhs_scale=picked_scales[2][:, j0 : j0 + UNIT],
                     start=True,
                     stop=True,
                 )
             nc.vector.tensor_tensor(
-                h[:, b, PACK * (j0 - first) : PACK * (j0 - first + UNIT)].rearrange(
-                    "p (h l t) -> p h t l", l=4, t=PACK
-                ),
+                h_tile[:, PACK * word : PACK * (word + UNIT)].rearrange("p (h l t) -> p h t l", l=4, t=PACK),
                 gain[:].rearrange("p t (h l) -> p h t l", l=4),
-                clamped[c][b][:, :, at : at + UNIT].rearrange("p t (h l) -> p h t l", l=4),
+                clamped[b][:, :, j0 : j0 + UNIT].rearrange("p t (h l) -> p h t l", l=4),
                 ALU.mult,
             )
 
-        def quantize_h(g, h):
-            width = GROUPS[g][1]
-            h_codes = held("h_codes%d" % g, [P, PASSES * width], U32)
-            h_scales = held("h_scales%d" % g, [P, PASSES * width], U8)
-            nc.vector.quantize_mx(
-                out=h_codes[:].bitcast(FP8X4), scales=h_scales[:], in_=h[:].rearrange("p b c -> p (b c)")
-            )
-            return h_codes, h_scales
+        h = [held("h%d" % g, [P, PASSES * PACK * width], BF16) for g, (first, width) in enumerate(GROUPS)]
+        h_codes = [held("h_codes%d" % g, [P, PASSES * width], U32) for g, (first, width) in enumerate(GROUPS)]
+        h_scales = [held("h_scales%d" % g, [P, PASSES * width], U8) for g, (first, width) in enumerate(GROUPS)]
 
-        def mix(g, h_codes, h_scales):
+        def units(g, b):
+            first, width = GROUPS[g]
+            for j0 in range(first, first + width, UNIT):
+                gain_times_demand(h[g], b * width + j0 - first, j0, b)
+
+        def quantize_h(g, first_pass, passes):
+            width = GROUPS[g][1]
+            start, stop = first_pass * width, (first_pass + passes) * width
+            nc.vector.quantize_mx(
+                out=h_codes[g][:, start:stop].bitcast(FP8X4),
+                scales=h_scales[g][:, start:stop],
+                in_=h[g][:, PACK * start : PACK * stop],
+            )
+
+        def mix(g):
             first, width = GROUPS[g]
             result = held("result%d" % g, [P, N_TILES, width], F32)
-            for n in range(N_TILES):
-                acc = psum.tile([P, width], F32, name="mix", tag="mix", bufs=3)
-                for b in range(PASSES):
+            sums = [psum.tile([P, width], F32, name="mix", tag="mix", bufs=3) for n in range(N_TILES)]
+            for b in range(PASSES):
+                for n in range(N_TILES):
                     cols = slice(b * N + n * P, b * N + (n + 1) * P)
                     nc.tensor.matmul_mx(
-                        out=acc[:],
+                        out=sums[n][:],
                         lhsT=wm_codes[:, cols].bitcast(FP8X4),
                         lhsT_scale=wm_scales[:, cols],
-                        rhs=h_codes[:, b * width : (b + 1) * width].bitcast(FP8X4),
-                        rhs_scale=h_scales[:, b * width : (b + 1) * width],
+                        rhs=h_codes[g][:, b * width : (b + 1) * width].bitcast(FP8X4),
+                        rhs_scale=h_scales[g][:, b * width : (b + 1) * width],
                         start=(b == 0),
                         stop=(b == PASSES - 1),
                     )
+            for n in range(N_TILES):
                 trim_column = columns[:, TRIM + n : TRIM + n + 1]
-                if g == len(GROUPS) - 1 and n == 1:
-                    nc.vector.tensor_scalar(result[:, n, :], acc[:], trim_column, None, ALU.add)
+                if g == len(GROUPS) - 1 and n != 1:
+                    nc.vector.tensor_scalar(result[:, n, :], sums[n][:], trim_column, None, ALU.add)
                 else:
-                    nc.scalar.activation(result[:, n, :], acc[:], ACT.Identity, bias=trim_column)
+                    nc.scalar.activation(result[:, n, :], sums[n][:], ACT.Identity, bias=trim_column)
             nc.sync.dma_start(out[:, first : first + width].rearrange("(n p) j -> p n j", p=P), result[:])
 
+        reorder_columns(wr_codes, wr_raw, 4)
         for i in range(2):
-            gather_scales(i, 0)
-        for c in range(CHUNKS):
-            for i in range(2):
-                gather_words(i, c)
+            gather_scales(i)
+        for i in range(2):
+            gather_words(i)
         round_ws(0)
         rows_turned = psum.tile([P, P], F32, name="rows_turned", tag="mix", bufs=3)
         nc.tensor.transpose(rows_turned[:], rows[:], identity[:])
         round_ws(1)
         nc.scalar.copy(columns[:], rows_turned[:, 0:32])
-        wr_codes = reorder_columns("wr_codes", wr_raw, 4, 2048)
-        wr_planes = reorder_columns("wr_planes", wr_raw_scales, 2, 1024)
+        reorder_columns(wr_planes, wr_raw_scales, 2)
         quantize_ws(0)
         quantize_ws(1)
-        for i in range(2):
-            gather_scales(i, 1)
-        gather_scales(2, 0)
-        gather_words(2, 0)
-        wg_codes = reorder_columns("wg_codes", wg_raw, 8, 20480)
-        wg_planes = reorder_columns("wg_planes", wg_raw_scales, 2, 14336)
-        gather_scales(2, 1)
-        gather_words(2, 1)
-        for c in range(CHUNKS):
-            for b in range(PASSES):
-                demand(c, b, wr_codes, wr_planes)
-                clamp(c, b)
+        gather_scales(2)
+        gather_words(2)
+        reorder_columns(wg_codes, wg_raw, 8)
+        reorder_columns(wg_planes, wg_raw_scales, 2)
+        for u in range(TILES):
+            demand(u)
         round_wm(0)
         round_wm(1)
-
-        h = [held("h%d" % g, [P, PASSES, PACK * width], BF16) for g, (first, width) in enumerate(GROUPS)]
-
-        def units(g, b):
-            first, width = GROUPS[g]
-            for j0 in range(first, first + width, UNIT):
-                gain_times_demand(h[g], first, j0, b, wg_codes, wg_planes)
 
         units(0, 0)
         units(0, 1)
         units(1, 0)
         quantize_wm()
-        mix(0, *quantize_h(0, h[0]))
-        units(2, 0)
-        units(3, 0)
+        quantize_h(0, 0, 2)
+        mix(0)
         units(1, 1)
+        units(2, 0)
+        quantize_h(1, 0, 2)
+        mix(1)
         units(2, 1)
-        mix(1, *quantize_h(1, h[1]))
+        units(3, 0)
+        quantize_h(2, 0, 2)
+        mix(2)
         units(3, 1)
-        mix(2, *quantize_h(2, h[2]))
-        mix(3, *quantize_h(3, h[3]))
+        quantize_h(3, 0, 1)
+        quantize_h(3, 1, 1)
+        mix(3)

@@ -26,7 +26,8 @@ CHUNK = 512
 CHUNKS = S // CHUNK
 UNIT = 128
 N_TILES = N // P
-GROUPS = ((0, 512), (512, 256), (768, 128), (896, 128))
+GROUPS = ((0, 256), (256, 256), (512, 256), (768, 128), (896, 128))
+VECTOR_CLAMPS = 5
 LO, HI, TRIM = 0, TILES, 2 * TILES
 
 
@@ -89,8 +90,8 @@ def tile_list_scheduled_gain_mixing_kernel(
         load_scale_rows(table_scales, tab_scales)
         nc.sync.dma_start(table_words[:], tab_words[0].rearrange("p n t -> p (n t)").bitcast(I32))
         load_ws(0)
-        load_ws(1)
         load_scale_rows(wr_raw_scales, wr_scales)
+        load_ws(1)
         nc.sync.dma_start(lists[2][:], offs3)
         nc.sync.dma_start(wg_raw[:], wg_words[0].rearrange("p n t -> p (n t)").bitcast(I32))
         load_scale_rows(wg_raw_scales, wg_scales)
@@ -102,16 +103,23 @@ def tile_list_scheduled_gain_mixing_kernel(
         columns = reused("columns", [P, 32], F32, 13312)
 
         ws_grouped = [reused("ws_grouped%d" % b, [P, PACK, HALF], BF16, 16384 + 4096 * b) for b in range(PASSES)]
-        picked_words = [held("words%d" % i, [P, S], U32) for i in range(2)]
-        picked_words.append(reused("words2", [P, S], U32, 8192))
+        demand_words = [
+            [held("words%d_0" % i, [P, CHUNK], U32), reused("words%d_1" % i, [P, CHUNK], U32, 2048 * (i + 1))]
+            for i in range(2)
+        ]
+        gain_words = reused("gain_words", [P, S], U32, 8192)
         picked_scales = [held("scales%d" % i, [P, S], U8) for i in range(2)]
         picked_scales.append(reused("scales2", [P, S], U8, 12288))
 
         def gather_scales(i):
             nc.vector.tensor_copy(picked_scales[i][:], table_scales[:].bitcast(U8).indirect(lists[i][:]))
 
-        def gather_words(i):
-            nc.vector.tensor_copy(picked_words[i][:], table_words[:].bitcast(U32).indirect(lists[i][:]))
+        def gather_words(picked, offsets):
+            nc.vector.tensor_copy(picked[:], table_words[:].bitcast(U32).indirect(offsets))
+
+        def gather_demand_words(c):
+            for i in range(2):
+                gather_words(demand_words[i][c], lists[i][:, c * CHUNK // 16 : (c + 1) * CHUNK // 16])
 
         def reorder_columns(moved, raw, run):
             nc.vector.tensor_copy(
@@ -159,36 +167,38 @@ def tile_list_scheduled_gain_mixing_kernel(
                     in_=wm_grouped[:, PACK * first : PACK * last],
                 )
 
-        clamped = [held("clamped%d" % b, [P, PACK, S], F32) for b in range(PASSES)]
+        demands = [reused("demand0", [P, PACK, S], F32, 24576), held("demand1", [P, PACK, S], F32)]
+        clamped = [held("clamped0", [P, PACK, S], F32), reused("clamped1", [P, PACK, S], F32, 24576)]
 
-        demands = [held("demand%d" % b, [P, PACK, S], F32) for b in range(PASSES)]
-
-        def demand(u):
+        def demand(u, c):
             b, t = divmod(u, PACK)
             cols = slice(u * P, (u + 1) * P)
-            for c in range(CHUNKS):
-                picks = slice(c * CHUNK, (c + 1) * CHUNK)
-                acc = psum.tile([P, CHUNK], F32, name="demand", tag="first", bufs=5)
-                nc.tensor.matmul_mx(
-                    out=acc[:],
-                    lhsT=ws_codes[:, cols].bitcast(FP8X4),
-                    lhsT_scale=ws_scales[:, cols],
-                    rhs=picked_words[0][:, picks].bitcast(FP8X4),
-                    rhs_scale=picked_scales[0][:, picks],
-                    start=True,
-                    stop=False,
-                )
-                nc.tensor.matmul_mx(
-                    out=acc[:],
-                    lhsT=wr_codes[:].bitcast(U8)[:, 2 * u * P : 2 * (u + 1) * P].bitcast(FP4X4),
-                    lhsT_scale=wr_planes[:].bitcast(U8)[:, cols],
-                    rhs=picked_words[1][:, picks].bitcast(FP8X4),
-                    rhs_scale=picked_scales[1][:, picks],
-                    start=False,
-                    stop=True,
-                )
-                nc.scalar.copy(demands[b][:, t, picks], acc[:])
-            nc.vector.tensor_scalar(
+            picks = slice(c * CHUNK, (c + 1) * CHUNK)
+            acc = psum.tile([P, CHUNK], F32, name="demand", tag="first", bufs=5)
+            nc.tensor.matmul_mx(
+                out=acc[:],
+                lhsT=ws_codes[:, cols].bitcast(FP8X4),
+                lhsT_scale=ws_scales[:, cols],
+                rhs=demand_words[0][c][:].bitcast(FP8X4),
+                rhs_scale=picked_scales[0][:, picks],
+                start=True,
+                stop=False,
+            )
+            nc.tensor.matmul_mx(
+                out=acc[:],
+                lhsT=wr_codes[:].bitcast(U8)[:, 2 * u * P : 2 * (u + 1) * P].bitcast(FP4X4),
+                lhsT_scale=wr_planes[:].bitcast(U8)[:, cols],
+                rhs=demand_words[1][c][:].bitcast(FP8X4),
+                rhs_scale=picked_scales[1][:, picks],
+                start=False,
+                stop=True,
+            )
+            nc.scalar.copy(demands[b][:, t, picks], acc[:])
+
+        def clamp(u):
+            b, t = divmod(u, PACK)
+            engine = nc.vector if u < VECTOR_CLAMPS else nc.gpsimd
+            engine.tensor_scalar(
                 clamped[b][:, t, :],
                 demands[b][:, t, :],
                 columns[:, HI + u : HI + u + 1],
@@ -205,7 +215,7 @@ def tile_list_scheduled_gain_mixing_kernel(
                     out=gain[:, t, :],
                     lhsT=wg_codes[:, cols].bitcast(FP8X4),
                     lhsT_scale=wg_planes[:].bitcast(U8)[:, cols],
-                    rhs=picked_words[2][:, j0 : j0 + UNIT].bitcast(FP8X4),
+                    rhs=gain_words[:, j0 : j0 + UNIT].bitcast(FP8X4),
                     rhs_scale=picked_scales[2][:, j0 : j0 + UNIT],
                     start=True,
                     stop=True,
@@ -238,22 +248,25 @@ def tile_list_scheduled_gain_mixing_kernel(
         def mix(g):
             first, width = GROUPS[g]
             result = held("result%d" % g, [P, N_TILES, width], F32)
-            sums = [psum.tile([P, width], F32, name="mix", tag="mix", bufs=3) for n in range(N_TILES)]
-            for b in range(PASSES):
-                for n in range(N_TILES):
-                    cols = slice(b * N + n * P, b * N + (n + 1) * P)
-                    nc.tensor.matmul_mx(
-                        out=sums[n][:],
-                        lhsT=wm_codes[:, cols].bitcast(FP8X4),
-                        lhsT_scale=wm_scales[:, cols],
-                        rhs=h_codes[g][:, b * width : (b + 1) * width].bitcast(FP8X4),
-                        rhs_scale=h_scales[g][:, b * width : (b + 1) * width],
-                        start=(b == 0),
-                        stop=(b == PASSES - 1),
-                    )
+            tag, bufs = ("first", 5) if g == len(GROUPS) - 2 else ("mix", 3)
+            sums = [psum.tile([P, width], F32, name="mix", tag=tag, bufs=bufs) for n in range(N_TILES)]
+            steps = [(n, b) for n in range(N_TILES) for b in range(PASSES)]
+            if g >= len(GROUPS) - 2:
+                steps = sorted(steps, key=lambda step: step[1])
+            for n, b in steps:
+                cols = slice(b * N + n * P, b * N + (n + 1) * P)
+                nc.tensor.matmul_mx(
+                    out=sums[n][:],
+                    lhsT=wm_codes[:, cols].bitcast(FP8X4),
+                    lhsT_scale=wm_scales[:, cols],
+                    rhs=h_codes[g][:, b * width : (b + 1) * width].bitcast(FP8X4),
+                    rhs_scale=h_scales[g][:, b * width : (b + 1) * width],
+                    start=(b == 0),
+                    stop=(b == PASSES - 1),
+                )
             for n in range(N_TILES):
                 trim_column = columns[:, TRIM + n : TRIM + n + 1]
-                if g == len(GROUPS) - 1 and n != 1:
+                if g >= len(GROUPS) - 2 and (g + n) % 2 == 1:
                     nc.vector.tensor_scalar(result[:, n, :], sums[n][:], trim_column, None, ALU.add)
                 else:
                     nc.scalar.activation(result[:, n, :], sums[n][:], ACT.Identity, bias=trim_column)
@@ -262,8 +275,7 @@ def tile_list_scheduled_gain_mixing_kernel(
         reorder_columns(wr_codes, wr_raw, 4)
         for i in range(2):
             gather_scales(i)
-        for i in range(2):
-            gather_words(i)
+        gather_demand_words(0)
         round_ws(0)
         rows_turned = psum.tile([P, P], F32, name="rows_turned", tag="mix", bufs=3)
         nc.tensor.transpose(rows_turned[:], rows[:], identity[:])
@@ -271,31 +283,39 @@ def tile_list_scheduled_gain_mixing_kernel(
         nc.scalar.copy(columns[:], rows_turned[:, 0:32])
         reorder_columns(wr_planes, wr_raw_scales, 2)
         quantize_ws(0)
+        gather_demand_words(1)
         quantize_ws(1)
         gather_scales(2)
-        gather_words(2)
+        gather_words(gain_words, lists[2][:])
         reorder_columns(wg_codes, wg_raw, 8)
         reorder_columns(wg_planes, wg_raw_scales, 2)
+        for u in range(PACK):
+            demand(u, 0)
         for u in range(TILES):
-            demand(u)
+            if u >= PACK:
+                demand(u, 0)
+            demand(u, 1)
+            clamp(u)
         round_wm(0)
         round_wm(1)
 
-        units(0, 0)
+        for g in range(len(GROUPS)):
+            units(g, 0)
         units(0, 1)
-        units(1, 0)
         quantize_wm()
-        quantize_h(0, 0, 2)
+        quantize_h(0, 0, PASSES)
         mix(0)
         units(1, 1)
-        units(2, 0)
-        quantize_h(1, 0, 2)
+        quantize_h(3, 0, 1)
+        quantize_h(1, 0, PASSES)
         mix(1)
         units(2, 1)
-        units(3, 0)
-        quantize_h(2, 0, 2)
+        quantize_h(4, 0, 1)
+        quantize_h(2, 0, PASSES)
         mix(2)
         units(3, 1)
-        quantize_h(3, 0, 1)
+        units(4, 1)
         quantize_h(3, 1, 1)
+        quantize_h(4, 1, 1)
         mix(3)
+        mix(4)

@@ -27,8 +27,9 @@ CHUNKS = S // CHUNK
 UNIT = 128
 N_TILES = N // P
 GROUPS = ((0, 256), (256, 256), (512, 256), (768, 128), (896, 128))
-VECTOR_CLAMPS = 5
-LO, HI, TRIM = 0, TILES, 2 * TILES
+VECTOR_CLAMPS = 8
+LO, HI, TRIM = 0, PACK, 2 * PACK
+ROWS = 16
 
 
 def tile_list_scheduled_gain_mixing_kernel(
@@ -55,14 +56,13 @@ def tile_list_scheduled_gain_mixing_kernel(
         wg_raw = held("wg_raw", [P, H], I32)
         ws_raw = [reused("ws_raw%d" % b, [P, PACK, HALF], F32, 8192 * b) for b in range(PASSES)]
         wm_raw = [held("wm_raw%d" % b, [P, PACK, N], F32) for b in range(PASSES)]
-        rows = held("rows", [P, P], F32)
+        rows = held("rows", [P, PASSES * P], F32)
         identity = held("identity", [P, P], F32)
 
         nc.vector.memset(table_scales[:], 0)
         nc.gpsimd.memset(rows[:], 0.0)
         nc.vector.memset(wr_raw_scales[:], 0)
         nc.vector.memset(wg_raw_scales[:], 0)
-        make_identity(nc, identity[:])
 
         def load_scale_rows(plane, scales):
             for quadrant in range(4):
@@ -74,25 +74,25 @@ def tile_list_scheduled_gain_mixing_kernel(
         def load_ws(b):
             nc.sync.dma_start(ws_raw[b][:], ws[:, b * HALF : (b + 1) * HALF].rearrange("(p j) c -> p j c", j=PACK))
 
-        def load_limits(queue, first, vector):
-            for b in range(PASSES):
-                queue.dma_start(
-                    rows[first + PACK * b : first + PACK * (b + 1), :].rearrange("t (q i) -> t q i", i=8),
-                    vector[b * HALF : (b + 1) * HALF].rearrange("(q t i) -> t q i", t=PACK, i=8),
-                )
+        def load_limits(first, vector):
+            nc.gpsimd.dma_start(
+                rows[first : first + PACK, :].rearrange("t (q i) -> t q i", i=8),
+                vector.rearrange("(q t i) -> t q i", t=PACK, i=8),
+            )
 
-        load_limits(nc.gpsimd, LO, lo)
-        load_limits(nc.gpsimd, HI, hi)
-        nc.gpsimd.dma_start(rows[TRIM : TRIM + N_TILES, :], trim.rearrange("(n p) -> n p", p=P))
+        load_limits(LO, lo)
+        load_limits(HI, hi)
+        nc.gpsimd.dma_start(rows[TRIM : TRIM + N_TILES, 0:P], trim.rearrange("(n p) -> n p", p=P))
+        make_identity(nc, identity[:])
         nc.sync.dma_start(lists[0][:], offs)
         nc.sync.dma_start(lists[1][:], offs2)
         nc.sync.dma_start(wr_raw[:], wr_words[0].bitcast(I32))
         load_scale_rows(table_scales, tab_scales)
-        nc.sync.dma_start(table_words[:], tab_words[0].rearrange("p n t -> p (n t)").bitcast(I32))
+        nc.sync.dma_start(lists[2][:], offs3)
         load_ws(0)
+        nc.sync.dma_start(table_words[:], tab_words[0].rearrange("p n t -> p (n t)").bitcast(I32))
         load_scale_rows(wr_raw_scales, wr_scales)
         load_ws(1)
-        nc.sync.dma_start(lists[2][:], offs3)
         nc.sync.dma_start(wg_raw[:], wg_words[0].rearrange("p n t -> p (n t)").bitcast(I32))
         load_scale_rows(wg_raw_scales, wg_scales)
         for b in range(PASSES):
@@ -100,16 +100,15 @@ def tile_list_scheduled_gain_mixing_kernel(
             for t in range(PACK):
                 nc.sync.dma_start(wm_raw[b][:, t, :], wm_rows[t])
 
-        columns = reused("columns", [P, 32], F32, 13312)
+        columns = reused("columns", [P, PASSES, ROWS], F32, 12288)
 
-        ws_grouped = [reused("ws_grouped%d" % b, [P, PACK, HALF], BF16, 16384 + 4096 * b) for b in range(PASSES)]
+        ws_grouped = [reused("ws_grouped%d" % b, [P, PACK, HALF], BF16, 32768 + 4096 * b) for b in range(PASSES)]
         demand_words = [
-            [held("words%d_0" % i, [P, CHUNK], U32), reused("words%d_1" % i, [P, CHUNK], U32, 2048 * (i + 1))]
+            [held("words%d_0" % i, [P, CHUNK], U32), reused("words%d_1" % i, [P, CHUNK], U32, 8192 + 2048 * i)]
             for i in range(2)
         ]
-        gain_words = reused("gain_words", [P, S], U32, 8192)
-        picked_scales = [held("scales%d" % i, [P, S], U8) for i in range(2)]
-        picked_scales.append(reused("scales2", [P, S], U8, 12288))
+        gain_words = reused("gain_words", [P, S], U32, 36864)
+        picked_scales = [held("scales%d" % i, [P, S], U8) for i in range(3)]
 
         def gather_scales(i):
             nc.vector.tensor_copy(picked_scales[i][:], table_scales[:].bitcast(U8).indirect(lists[i][:]))
@@ -128,9 +127,9 @@ def tile_list_scheduled_gain_mixing_kernel(
             )
 
         wr_codes = held("wr_codes", [P, H // 2], I32)
-        wr_planes = reused("wr_planes", [P, H // 4], I32, 0)
-        wg_codes = reused("wg_codes", [P, H], I32, 20480)
-        wg_planes = reused("wg_planes", [P, H // 4], I32, 14336)
+        wr_planes = held("wr_planes", [P, H // 4], I32)
+        wg_codes = reused("wg_codes", [P, H], I32, 32768)
+        wg_planes = reused("wg_planes", [P, H // 4], I32, 12544)
         ws_codes = held("ws_codes", [P, H], U32)
         ws_scales = held("ws_scales", [P, H], U8)
 
@@ -151,7 +150,7 @@ def tile_list_scheduled_gain_mixing_kernel(
 
         wm_codes = held("wm_codes", [P, PASSES * N], U32)
         wm_scales = held("wm_scales", [P, PASSES * N], U8)
-        wm_grouped = held("wm_grouped", [P, PASSES * N * PACK], BF16)
+        wm_grouped = reused("wm_grouped", [P, PASSES * N * PACK], BF16, 6144)
 
         def round_wm(b):
             nc.scalar.copy(
@@ -167,8 +166,8 @@ def tile_list_scheduled_gain_mixing_kernel(
                     in_=wm_grouped[:, PACK * first : PACK * last],
                 )
 
-        demands = [reused("demand0", [P, PACK, S], F32, 24576), held("demand1", [P, PACK, S], F32)]
-        clamped = [held("clamped0", [P, PACK, S], F32), reused("clamped1", [P, PACK, S], F32, 24576)]
+        demands = [reused("demand0", [P, PACK, S], F32, 15360), held("demand1", [P, PACK, S], F32)]
+        clamped = [held("clamped0", [P, PACK, S], F32), held("clamped1", [P, PACK, S], F32)]
 
         def demand(u, c):
             b, t = divmod(u, PACK)
@@ -201,8 +200,8 @@ def tile_list_scheduled_gain_mixing_kernel(
             engine.tensor_scalar(
                 clamped[b][:, t, :],
                 demands[b][:, t, :],
-                columns[:, HI + u : HI + u + 1],
-                columns[:, LO + u : LO + u + 1],
+                columns[:, b, HI + t : HI + t + 1],
+                columns[:, b, LO + t : LO + t + 1],
                 ALU.min,
                 ALU.max,
             )
@@ -265,7 +264,7 @@ def tile_list_scheduled_gain_mixing_kernel(
                     stop=(b == PASSES - 1),
                 )
             for n in range(N_TILES):
-                trim_column = columns[:, TRIM + n : TRIM + n + 1]
+                trim_column = columns[:, 0, TRIM + n : TRIM + n + 1]
                 if g >= len(GROUPS) - 2 and (g + n) % 2 == 1:
                     nc.vector.tensor_scalar(result[:, n, :], sums[n][:], trim_column, None, ALU.add)
                 else:
@@ -273,19 +272,19 @@ def tile_list_scheduled_gain_mixing_kernel(
             nc.sync.dma_start(out[:, first : first + width].rearrange("(n p) j -> p n j", p=P), result[:])
 
         reorder_columns(wr_codes, wr_raw, 4)
-        for i in range(2):
+        for i in range(3):
             gather_scales(i)
-        gather_demand_words(0)
         round_ws(0)
-        rows_turned = psum.tile([P, P], F32, name="rows_turned", tag="mix", bufs=3)
-        nc.tensor.transpose(rows_turned[:], rows[:], identity[:])
-        round_ws(1)
-        nc.scalar.copy(columns[:], rows_turned[:, 0:32])
-        reorder_columns(wr_planes, wr_raw_scales, 2)
         quantize_ws(0)
-        gather_demand_words(1)
+        gather_demand_words(0)
+        rows_turned = psum.tile([P, PASSES, P], F32, name="rows_turned", tag="mix", bufs=3)
+        for b in range(PASSES):
+            nc.tensor.transpose(rows_turned[:, b, :], rows[:, b * P : (b + 1) * P], identity[:])
+        round_ws(1)
+        nc.scalar.copy(columns[:], rows_turned[:, :, 0:ROWS])
+        reorder_columns(wr_planes, wr_raw_scales, 2)
         quantize_ws(1)
-        gather_scales(2)
+        gather_demand_words(1)
         gather_words(gain_words, lists[2][:])
         reorder_columns(wg_codes, wg_raw, 8)
         reorder_columns(wg_planes, wg_raw_scales, 2)

@@ -27,9 +27,10 @@ CHUNKS = S // CHUNK
 UNIT = 128
 N_TILES = N // P
 GROUPS = ((0, 256), (256, 256), (512, 256), (768, 128), (896, 128))
-VECTOR_CLAMPS = 8
 LO, HI, TRIM = 0, PACK, 2 * PACK
 ROWS = 16
+QUARTER = 256
+EARLY_UNITS = 3
 
 
 def tile_list_scheduled_gain_mixing_kernel(
@@ -53,8 +54,13 @@ def tile_list_scheduled_gain_mixing_kernel(
         wr_raw_scales = held("wr_raw_scales", [P, H // 4], I32)
         wg_raw_scales = held("wg_raw_scales", [P, H // 4], I32)
         wr_raw = held("wr_raw", [P, H // 2], I32)
-        wg_raw = held("wg_raw", [P, H], I32)
-        ws_raw = [reused("ws_raw%d" % b, [P, PACK, HALF], F32, 8192 * b) for b in range(PASSES)]
+        wg_raw = reused("wg_raw", [P, H], I32, 32768)
+        ws_raw = [
+            held("ws_raw0", [P, PACK, QUARTER], F32),
+            reused("ws_raw1", [P, PACK, QUARTER], F32, 4096),
+            held("ws_raw2", [P, PACK, QUARTER], F32),
+            reused("ws_raw3", [P, PACK, QUARTER], F32, 12288),
+        ]
         wm_raw = [held("wm_raw%d" % b, [P, PACK, N], F32) for b in range(PASSES)]
         rows = held("rows", [P, PASSES * P], F32)
         identity = held("identity", [P, P], F32)
@@ -71,8 +77,9 @@ def tile_list_scheduled_gain_mixing_kernel(
                     scales[0, 4 * quadrant : 4 * quadrant + 4, :].bitcast(I32),
                 )
 
-        def load_ws(b):
-            nc.sync.dma_start(ws_raw[b][:], ws[:, b * HALF : (b + 1) * HALF].rearrange("(p j) c -> p j c", j=PACK))
+        def load_ws(k):
+            columns_of_ws = ws[:, k * QUARTER : (k + 1) * QUARTER]
+            nc.sync.dma_start(ws_raw[k][:], columns_of_ws.rearrange("(p j) c -> p j c", j=PACK))
 
         def load_limits(first, vector):
             nc.gpsimd.dma_start(
@@ -88,11 +95,13 @@ def tile_list_scheduled_gain_mixing_kernel(
         nc.sync.dma_start(lists[1][:], offs2)
         nc.sync.dma_start(wr_raw[:], wr_words[0].bitcast(I32))
         load_scale_rows(table_scales, tab_scales)
-        nc.sync.dma_start(lists[2][:], offs3)
-        load_ws(0)
         nc.sync.dma_start(table_words[:], tab_words[0].rearrange("p n t -> p (n t)").bitcast(I32))
-        load_scale_rows(wr_raw_scales, wr_scales)
+        load_ws(0)
         load_ws(1)
+        load_scale_rows(wr_raw_scales, wr_scales)
+        load_ws(2)
+        load_ws(3)
+        nc.sync.dma_start(lists[2][:], offs3)
         nc.sync.dma_start(wg_raw[:], wg_words[0].rearrange("p n t -> p (n t)").bitcast(I32))
         load_scale_rows(wg_raw_scales, wg_scales)
         for b in range(PASSES):
@@ -100,15 +109,16 @@ def tile_list_scheduled_gain_mixing_kernel(
             for t in range(PACK):
                 nc.sync.dma_start(wm_raw[b][:, t, :], wm_rows[t])
 
-        columns = reused("columns", [P, PASSES, ROWS], F32, 12288)
+        columns = reused("columns", [P, PASSES, ROWS], F32, 12352)
 
-        ws_grouped = [reused("ws_grouped%d" % b, [P, PACK, HALF], BF16, 32768 + 4096 * b) for b in range(PASSES)]
+        ws_grouped = [held("ws_grouped%d" % b, [P, PACK, HALF], BF16) for b in range(PASSES)]
         demand_words = [
-            [held("words%d_0" % i, [P, CHUNK], U32), reused("words%d_1" % i, [P, CHUNK], U32, 8192 + 2048 * i)]
+            [held("words%d_0" % i, [P, CHUNK], U32), reused("words%d_1" % i, [P, CHUNK], U32, 4096 + 2048 * i)]
             for i in range(2)
         ]
-        gain_words = reused("gain_words", [P, S], U32, 36864)
-        picked_scales = [held("scales%d" % i, [P, S], U8) for i in range(3)]
+        gain_words = reused("gain_words", [P, S], U32, 8256)
+        picked_scales = [held("scales%d" % i, [P, S], U8) for i in range(2)]
+        picked_scales.append(reused("scales2", [P, S], U8, 12544))
 
         def gather_scales(i):
             nc.vector.tensor_copy(picked_scales[i][:], table_scales[:].bitcast(U8).indirect(lists[i][:]))
@@ -128,17 +138,17 @@ def tile_list_scheduled_gain_mixing_kernel(
 
         wr_codes = held("wr_codes", [P, H // 2], I32)
         wr_planes = held("wr_planes", [P, H // 4], I32)
-        wg_codes = reused("wg_codes", [P, H], I32, 32768)
-        wg_planes = reused("wg_planes", [P, H // 4], I32, 12544)
+        wg_codes = held("wg_codes", [P, H], I32)
+        wg_planes = held("wg_planes", [P, H // 4], I32)
         ws_codes = held("ws_codes", [P, H], U32)
         ws_scales = held("ws_scales", [P, H], U8)
 
-        def round_ws(b):
-            source = ws_raw[b][:].rearrange("p j (q t h l) -> p t q h j l", t=PACK, h=2, l=4)
+        def round_ws(k):
+            b, half = divmod(k, 2)
+            source = ws_raw[k][:].rearrange("p j (q t h l) -> p t q h j l", t=PACK, h=2, l=4)
             for t in range(PACK):
-                nc.scalar.copy(
-                    ws_grouped[b][:, t, :].rearrange("p (q h l j) -> p q h j l", h=2, l=4, j=PACK), source[:, t]
-                )
+                target = ws_grouped[b][:, t, half * QUARTER : (half + 1) * QUARTER]
+                nc.scalar.copy(target.rearrange("p (q h l j) -> p q h j l", h=2, l=4, j=PACK), source[:, t])
 
         def quantize_ws(b):
             cols = slice(b * HALF, (b + 1) * HALF)
@@ -148,9 +158,9 @@ def tile_list_scheduled_gain_mixing_kernel(
                 in_=ws_grouped[b][:].rearrange("p t c -> p (t c)"),
             )
 
-        wm_codes = held("wm_codes", [P, PASSES * N], U32)
+        wm_codes = reused("wm_codes", [P, PASSES * N], U32, 45056)
         wm_scales = held("wm_scales", [P, PASSES * N], U8)
-        wm_grouped = reused("wm_grouped", [P, PASSES * N * PACK], BF16, 6144)
+        wm_grouped = reused("wm_grouped", [P, PASSES * N * PACK], BF16, 2048)
 
         def round_wm(b):
             nc.scalar.copy(
@@ -166,11 +176,10 @@ def tile_list_scheduled_gain_mixing_kernel(
                     in_=wm_grouped[:, PACK * first : PACK * last],
                 )
 
-        demands = [reused("demand0", [P, PACK, S], F32, 15360), held("demand1", [P, PACK, S], F32)]
-        clamped = [held("clamped0", [P, PACK, S], F32), held("clamped1", [P, PACK, S], F32)]
+        demands = [reused("demand0", [P, TILES, CHUNK], F32, 14336), reused("demand1", [P, TILES, CHUNK], F32, 36864)]
+        clamped = [held("clamped0", [P, TILES, CHUNK], F32), reused("clamped1", [P, TILES, CHUNK], F32, 20480)]
 
         def demand(u, c):
-            b, t = divmod(u, PACK)
             cols = slice(u * P, (u + 1) * P)
             picks = slice(c * CHUNK, (c + 1) * CHUNK)
             acc = psum.tile([P, CHUNK], F32, name="demand", tag="first", bufs=5)
@@ -192,21 +201,20 @@ def tile_list_scheduled_gain_mixing_kernel(
                 start=False,
                 stop=True,
             )
-            nc.scalar.copy(demands[b][:, t, picks], acc[:])
+            nc.scalar.copy(demands[c][:, u, :], acc[:])
 
-        def clamp(u):
+        def clamp(engine, u, c):
             b, t = divmod(u, PACK)
-            engine = nc.vector if u < VECTOR_CLAMPS else nc.gpsimd
             engine.tensor_scalar(
-                clamped[b][:, t, :],
-                demands[b][:, t, :],
+                clamped[c][:, u, :],
+                demands[c][:, u, :],
                 columns[:, b, HI + t : HI + t + 1],
                 columns[:, b, LO + t : LO + t + 1],
                 ALU.min,
                 ALU.max,
             )
 
-        def gain_times_demand(h_tile, word, j0, b):
+        def gain_unit(j0, b):
             gain = psum.tile([P, PACK, UNIT], F32, name="gain", tag="first", bufs=5)
             for t in range(PACK):
                 cols = slice((PACK * b + t) * P, (PACK * b + t + 1) * P)
@@ -219,21 +227,29 @@ def tile_list_scheduled_gain_mixing_kernel(
                     start=True,
                     stop=True,
                 )
+            return gain
+
+        def multiply(gain, h_tile, word, j0, b):
+            c, within = divmod(j0, CHUNK)
             nc.vector.tensor_tensor(
                 h_tile[:, PACK * word : PACK * (word + UNIT)].rearrange("p (h l t) -> p h t l", l=4, t=PACK),
                 gain[:].rearrange("p t (h l) -> p h t l", l=4),
-                clamped[b][:, :, j0 : j0 + UNIT].rearrange("p t (h l) -> p h t l", l=4),
+                clamped[c][:, PACK * b : PACK * (b + 1), within : within + UNIT].rearrange("p t (h l) -> p h t l", l=4),
                 ALU.mult,
             )
 
         h = [held("h%d" % g, [P, PASSES * PACK * width], BF16) for g, (first, width) in enumerate(GROUPS)]
-        h_codes = [held("h_codes%d" % g, [P, PASSES * width], U32) for g, (first, width) in enumerate(GROUPS)]
+        h_codes = [
+            reused("h_codes%d" % g, [P, PASSES * width], U32, 36864 + 4 * PASSES * first)
+            for g, (first, width) in enumerate(GROUPS)
+        ]
         h_scales = [held("h_scales%d" % g, [P, PASSES * width], U8) for g, (first, width) in enumerate(GROUPS)]
 
         def units(g, b):
             first, width = GROUPS[g]
             for j0 in range(first, first + width, UNIT):
-                gain_times_demand(h[g], b * width + j0 - first, j0, b)
+                gain = early[j0 // UNIT] if b == 0 and j0 < EARLY_UNITS * UNIT else gain_unit(j0, b)
+                multiply(gain, h[g], b * width + j0 - first, j0, b)
 
         def quantize_h(g, first_pass, passes):
             width = GROUPS[g][1]
@@ -272,43 +288,48 @@ def tile_list_scheduled_gain_mixing_kernel(
             nc.sync.dma_start(out[:, first : first + width].rearrange("(n p) j -> p n j", p=P), result[:])
 
         reorder_columns(wr_codes, wr_raw, 4)
-        for i in range(3):
+        for i in range(2):
             gather_scales(i)
-        round_ws(0)
-        quantize_ws(0)
         gather_demand_words(0)
+        for k in range(4):
+            round_ws(k)
+        reorder_columns(wr_planes, wr_raw_scales, 2)
+        quantize_ws(0)
+        gather_demand_words(1)
+        quantize_ws(1)
+        gather_scales(2)
+        gather_words(gain_words, lists[2][:])
+        reorder_columns(wg_planes, wg_raw_scales, 2)
+        reorder_columns(wg_codes, wg_raw, 8)
         rows_turned = psum.tile([P, PASSES, P], F32, name="rows_turned", tag="mix", bufs=3)
         for b in range(PASSES):
             nc.tensor.transpose(rows_turned[:, b, :], rows[:, b * P : (b + 1) * P], identity[:])
-        round_ws(1)
-        nc.scalar.copy(columns[:], rows_turned[:, :, 0:ROWS])
-        reorder_columns(wr_planes, wr_raw_scales, 2)
-        quantize_ws(1)
-        gather_demand_words(1)
-        gather_words(gain_words, lists[2][:])
-        reorder_columns(wg_codes, wg_raw, 8)
-        reorder_columns(wg_planes, wg_raw_scales, 2)
-        for u in range(PACK):
-            demand(u, 0)
         for u in range(TILES):
-            if u >= PACK:
-                demand(u, 0)
+            demand(u, 0)
+            if u == 0:
+                nc.scalar.copy(columns[:], rows_turned[:, :, 0:ROWS])
+            clamp(nc.vector, u, 0)
+        early = []
+        for u in range(TILES):
+            if u == TILES - EARLY_UNITS:
+                early = [gain_unit(k * UNIT, 0) for k in range(EARLY_UNITS)]
             demand(u, 1)
-            clamp(u)
+            clamp(nc.gpsimd, u, 1)
         round_wm(0)
         round_wm(1)
 
-        for g in range(len(GROUPS)):
+        for b in range(PASSES):
+            units(0, b)
+            units(1, b)
+        for g in range(2, len(GROUPS)):
             units(g, 0)
-        units(0, 1)
         quantize_wm()
         quantize_h(0, 0, PASSES)
-        mix(0)
-        units(1, 1)
-        quantize_h(3, 0, 1)
         quantize_h(1, 0, PASSES)
+        mix(0)
         mix(1)
         units(2, 1)
+        quantize_h(3, 0, 1)
         quantize_h(4, 0, 1)
         quantize_h(2, 0, PASSES)
         mix(2)

@@ -54,7 +54,7 @@ def tile_list_scheduled_gain_mixing_kernel(
         wr_raw_scales = held("wr_raw_scales", [P, H // 4], I32)
         wg_raw_scales = held("wg_raw_scales", [P, H // 4], I32)
         wr_raw = held("wr_raw", [P, H // 2], I32)
-        wg_raw = reused("wg_raw", [P, H], I32, 32768)
+        wg_raw = held("wg_raw", [P, H], I32)
         ws_raw = [
             held("ws_raw0", [P, PACK, QUARTER], F32),
             reused("ws_raw1", [P, PACK, QUARTER], F32, 4096),
@@ -158,7 +158,7 @@ def tile_list_scheduled_gain_mixing_kernel(
                 in_=ws_grouped[b][:].rearrange("p t c -> p (t c)"),
             )
 
-        wm_codes = reused("wm_codes", [P, PASSES * N], U32, 45056)
+        wm_codes = reused("wm_codes", [P, PASSES * N], U32, 38912)
         wm_scales = held("wm_scales", [P, PASSES * N], U8)
         wm_grouped = reused("wm_grouped", [P, PASSES * N * PACK], BF16, 2048)
 
@@ -176,10 +176,13 @@ def tile_list_scheduled_gain_mixing_kernel(
                     in_=wm_grouped[:, PACK * first : PACK * last],
                 )
 
-        demands = [reused("demand0", [P, TILES, CHUNK], F32, 14336), reused("demand1", [P, TILES, CHUNK], F32, 36864)]
-        clamped = [held("clamped0", [P, TILES, CHUNK], F32), reused("clamped1", [P, TILES, CHUNK], F32, 20480)]
+        demand0 = reused("demand0", [P, PACK, S], F32, 14336)
+        demand1 = [reused("demand1_%d" % c, [P, PACK, CHUNK], F32, 30720 + 10240 * c) for c in range(CHUNKS)]
+        clamped0 = held("clamped0", [P, PACK, S], F32)
+        clamped1 = [held("clamped1_0", [P, PACK, CHUNK], F32), reused("clamped1_1", [P, PACK, CHUNK], F32, 28672)]
 
         def demand(u, c):
+            b, t = divmod(u, PACK)
             cols = slice(u * P, (u + 1) * P)
             picks = slice(c * CHUNK, (c + 1) * CHUNK)
             acc = psum.tile([P, CHUNK], F32, name="demand", tag="first", bufs=5)
@@ -201,13 +204,13 @@ def tile_list_scheduled_gain_mixing_kernel(
                 start=False,
                 stop=True,
             )
-            nc.scalar.copy(demands[c][:, u, :], acc[:])
+            nc.scalar.copy(demand0[:, t, picks] if b == 0 else demand1[c][:, t, :], acc[:])
 
-        def clamp(engine, u, c):
+        def clamp(engine, u, target, source):
             b, t = divmod(u, PACK)
             engine.tensor_scalar(
-                clamped[c][:, u, :],
-                demands[c][:, u, :],
+                target[:, t, :],
+                source[:, t, :],
                 columns[:, b, HI + t : HI + t + 1],
                 columns[:, b, LO + t : LO + t + 1],
                 ALU.min,
@@ -231,17 +234,18 @@ def tile_list_scheduled_gain_mixing_kernel(
 
         def multiply(gain, h_tile, word, j0, b):
             c, within = divmod(j0, CHUNK)
+            source = clamped0[:, :, j0 : j0 + UNIT] if b == 0 else clamped1[c][:, :, within : within + UNIT]
             nc.vector.tensor_tensor(
                 h_tile[:, PACK * word : PACK * (word + UNIT)].rearrange("p (h l t) -> p h t l", l=4, t=PACK),
+                source.rearrange("p t (h l) -> p h t l", l=4),
                 gain[:].rearrange("p t (h l) -> p h t l", l=4),
-                clamped[c][:, PACK * b : PACK * (b + 1), within : within + UNIT].rearrange("p t (h l) -> p h t l", l=4),
                 ALU.mult,
             )
 
         h = [held("h%d" % g, [P, PASSES * PACK * width], BF16) for g, (first, width) in enumerate(GROUPS)]
+        h_offsets = (41984, 44032, 49152, 46080, 47104)
         h_codes = [
-            reused("h_codes%d" % g, [P, PASSES * width], U32, 36864 + 4 * PASSES * first)
-            for g, (first, width) in enumerate(GROUPS)
+            reused("h_codes%d" % g, [P, PASSES * width], U32, h_offsets[g]) for g, (first, width) in enumerate(GROUPS)
         ]
         h_scales = [held("h_scales%d" % g, [P, PASSES * width], U8) for g, (first, width) in enumerate(GROUPS)]
 
@@ -308,13 +312,17 @@ def tile_list_scheduled_gain_mixing_kernel(
             demand(u, 0)
             if u == 0:
                 nc.scalar.copy(columns[:], rows_turned[:, :, 0:ROWS])
-            clamp(nc.vector, u, 0)
+            if u >= PACK:
+                clamp(nc.vector, u, clamped1[0], demand1[0])
         early = []
         for u in range(TILES):
             if u == TILES - EARLY_UNITS:
                 early = [gain_unit(k * UNIT, 0) for k in range(EARLY_UNITS)]
             demand(u, 1)
-            clamp(nc.gpsimd, u, 1)
+            if u < PACK:
+                clamp(nc.vector, u, clamped0, demand0)
+            else:
+                clamp(nc.gpsimd, u, clamped1[1], demand1[1])
         round_wm(0)
         round_wm(1)
 

@@ -29,8 +29,7 @@ N_TILES = N // P
 GROUPS = ((0, 256), (256, 256), (512, 256), (768, 128), (896, 128))
 LO, HI, TRIM = 0, PACK, 2 * PACK
 ROWS = 16
-QUARTER = 256
-EARLY_UNITS = 3
+AHEAD = 3
 
 
 def tile_list_scheduled_gain_mixing_kernel(
@@ -55,12 +54,7 @@ def tile_list_scheduled_gain_mixing_kernel(
         wg_raw_scales = held("wg_raw_scales", [P, H // 4], I32)
         wr_raw = held("wr_raw", [P, H // 2], I32)
         wg_raw = held("wg_raw", [P, H], I32)
-        ws_raw = [
-            held("ws_raw0", [P, PACK, QUARTER], F32),
-            reused("ws_raw1", [P, PACK, QUARTER], F32, 4096),
-            held("ws_raw2", [P, PACK, QUARTER], F32),
-            reused("ws_raw3", [P, PACK, QUARTER], F32, 12288),
-        ]
+        ws_raw = [reused("ws_raw%d" % b, [P, PACK, HALF], F32, 12288 * b) for b in range(PASSES)]
         wm_raw = [held("wm_raw%d" % b, [P, PACK, N], F32) for b in range(PASSES)]
         rows = held("rows", [P, PASSES * P], F32)
         identity = held("identity", [P, P], F32)
@@ -77,9 +71,8 @@ def tile_list_scheduled_gain_mixing_kernel(
                     scales[0, 4 * quadrant : 4 * quadrant + 4, :].bitcast(I32),
                 )
 
-        def load_ws(k):
-            columns_of_ws = ws[:, k * QUARTER : (k + 1) * QUARTER]
-            nc.sync.dma_start(ws_raw[k][:], columns_of_ws.rearrange("(p j) c -> p j c", j=PACK))
+        def load_ws(b):
+            nc.sync.dma_start(ws_raw[b][:], ws[:, b * HALF : (b + 1) * HALF].rearrange("(p j) c -> p j c", j=PACK))
 
         def load_limits(first, vector):
             nc.gpsimd.dma_start(
@@ -97,10 +90,8 @@ def tile_list_scheduled_gain_mixing_kernel(
         load_scale_rows(table_scales, tab_scales)
         nc.sync.dma_start(table_words[:], tab_words[0].rearrange("p n t -> p (n t)").bitcast(I32))
         load_ws(0)
-        load_ws(1)
         load_scale_rows(wr_raw_scales, wr_scales)
-        load_ws(2)
-        load_ws(3)
+        load_ws(1)
         nc.sync.dma_start(lists[2][:], offs3)
         nc.sync.dma_start(wg_raw[:], wg_words[0].rearrange("p n t -> p (n t)").bitcast(I32))
         load_scale_rows(wg_raw_scales, wg_scales)
@@ -109,26 +100,19 @@ def tile_list_scheduled_gain_mixing_kernel(
             for t in range(PACK):
                 nc.sync.dma_start(wm_raw[b][:, t, :], wm_rows[t])
 
-        columns = reused("columns", [P, PASSES, ROWS], F32, 12352)
+        columns = reused("columns", [P, PASSES, ROWS], F32, 16448)
 
         ws_grouped = [held("ws_grouped%d" % b, [P, PACK, HALF], BF16) for b in range(PASSES)]
-        demand_words = [
-            [held("words%d_0" % i, [P, CHUNK], U32), reused("words%d_1" % i, [P, CHUNK], U32, 4096 + 2048 * i)]
-            for i in range(2)
-        ]
+        demand_words = [held("words%d" % i, [P, S], U32) for i in range(2)]
         gain_words = reused("gain_words", [P, S], U32, 8256)
         picked_scales = [held("scales%d" % i, [P, S], U8) for i in range(2)]
-        picked_scales.append(reused("scales2", [P, S], U8, 12544))
+        picked_scales.append(reused("scales2", [P, S], U8, 0))
 
         def gather_scales(i):
             nc.vector.tensor_copy(picked_scales[i][:], table_scales[:].bitcast(U8).indirect(lists[i][:]))
 
         def gather_words(picked, offsets):
             nc.vector.tensor_copy(picked[:], table_words[:].bitcast(U32).indirect(offsets))
-
-        def gather_demand_words(c):
-            for i in range(2):
-                gather_words(demand_words[i][c], lists[i][:, c * CHUNK // 16 : (c + 1) * CHUNK // 16])
 
         def reorder_columns(moved, raw, run):
             nc.vector.tensor_copy(
@@ -138,29 +122,29 @@ def tile_list_scheduled_gain_mixing_kernel(
 
         wr_codes = held("wr_codes", [P, H // 2], I32)
         wr_planes = held("wr_planes", [P, H // 4], I32)
-        wg_codes = held("wg_codes", [P, H], I32)
-        wg_planes = held("wg_planes", [P, H // 4], I32)
-        ws_codes = held("ws_codes", [P, H], U32)
+        wg_codes = reused("wg_codes", [P, H], I32, 12352)
+        wg_planes = reused("wg_planes", [P, H // 4], I32, 16640)
+        ws_codes = [reused("ws_codes0", [P, HALF], U32, 63488), held("ws_codes1", [P, HALF], U32)]
         ws_scales = held("ws_scales", [P, H], U8)
 
-        def round_ws(k):
-            b, half = divmod(k, 2)
-            source = ws_raw[k][:].rearrange("p j (q t h l) -> p t q h j l", t=PACK, h=2, l=4)
+        def round_ws(b):
+            source = ws_raw[b][:].rearrange("p j (q t h l) -> p t q h j l", t=PACK, h=2, l=4)
             for t in range(PACK):
-                target = ws_grouped[b][:, t, half * QUARTER : (half + 1) * QUARTER]
-                nc.scalar.copy(target.rearrange("p (q h l j) -> p q h j l", h=2, l=4, j=PACK), source[:, t])
+                nc.scalar.copy(
+                    ws_grouped[b][:, t, :].rearrange("p (q h l j) -> p q h j l", h=2, l=4, j=PACK), source[:, t]
+                )
 
         def quantize_ws(b):
             cols = slice(b * HALF, (b + 1) * HALF)
             nc.vector.quantize_mx(
-                out=ws_codes[:, cols].bitcast(FP8X4),
+                out=ws_codes[b][:].bitcast(FP8X4),
                 scales=ws_scales[:, cols],
                 in_=ws_grouped[b][:].rearrange("p t c -> p (t c)"),
             )
 
-        wm_codes = reused("wm_codes", [P, PASSES * N], U32, 38912)
+        wm_codes = reused("wm_codes", [P, PASSES * N], U32, 34816)
         wm_scales = held("wm_scales", [P, PASSES * N], U8)
-        wm_grouped = reused("wm_grouped", [P, PASSES * N * PACK], BF16, 2048)
+        wm_grouped = reused("wm_grouped", [P, PASSES * N * PACK], BF16, 63488)
 
         def round_wm(b):
             nc.scalar.copy(
@@ -176,10 +160,10 @@ def tile_list_scheduled_gain_mixing_kernel(
                     in_=wm_grouped[:, PACK * first : PACK * last],
                 )
 
-        demand0 = reused("demand0", [P, PACK, S], F32, 14336)
-        demand1 = [reused("demand1_%d" % c, [P, PACK, CHUNK], F32, 30720 + 10240 * c) for c in range(CHUNKS)]
+        demand0 = reused("demand0", [P, PACK, S], F32, 18432)
+        demand1 = [reused("demand1_0", [P, PACK, CHUNK], F32, 36864), held("demand1_1", [P, PACK, CHUNK], F32)]
         clamped0 = held("clamped0", [P, PACK, S], F32)
-        clamped1 = [held("clamped1_0", [P, PACK, CHUNK], F32), reused("clamped1_1", [P, PACK, CHUNK], F32, 28672)]
+        clamped1 = [reused("clamped1_%d" % c, [P, PACK, CHUNK], F32, 18432 + 22528 * c) for c in range(CHUNKS)]
 
         def demand(u, c):
             b, t = divmod(u, PACK)
@@ -188,9 +172,9 @@ def tile_list_scheduled_gain_mixing_kernel(
             acc = psum.tile([P, CHUNK], F32, name="demand", tag="first", bufs=5)
             nc.tensor.matmul_mx(
                 out=acc[:],
-                lhsT=ws_codes[:, cols].bitcast(FP8X4),
+                lhsT=ws_codes[b][:, t * P : (t + 1) * P].bitcast(FP8X4),
                 lhsT_scale=ws_scales[:, cols],
-                rhs=demand_words[0][c][:].bitcast(FP8X4),
+                rhs=demand_words[0][:, picks].bitcast(FP8X4),
                 rhs_scale=picked_scales[0][:, picks],
                 start=True,
                 stop=False,
@@ -199,7 +183,7 @@ def tile_list_scheduled_gain_mixing_kernel(
                 out=acc[:],
                 lhsT=wr_codes[:].bitcast(U8)[:, 2 * u * P : 2 * (u + 1) * P].bitcast(FP4X4),
                 lhsT_scale=wr_planes[:].bitcast(U8)[:, cols],
-                rhs=demand_words[1][c][:].bitcast(FP8X4),
+                rhs=demand_words[1][:, picks].bitcast(FP8X4),
                 rhs_scale=picked_scales[1][:, picks],
                 start=False,
                 stop=True,
@@ -243,17 +227,31 @@ def tile_list_scheduled_gain_mixing_kernel(
             )
 
         h = [held("h%d" % g, [P, PASSES * PACK * width], BF16) for g, (first, width) in enumerate(GROUPS)]
-        h_offsets = (41984, 44032, 49152, 46080, 47104)
+        h_offsets = (49152, 51200, 53248, 37888, 38912)
         h_codes = [
             reused("h_codes%d" % g, [P, PASSES * width], U32, h_offsets[g]) for g, (first, width) in enumerate(GROUPS)
         ]
         h_scales = [held("h_scales%d" % g, [P, PASSES * width], U8) for g, (first, width) in enumerate(GROUPS)]
 
-        def units(g, b):
+        places = [(g, j0) for g, (first, width) in enumerate(GROUPS) for j0 in range(first, first + width, UNIT)]
+        order = [(b, g, j0) for b in range(PASSES) for g, j0 in places]
+        gains = []
+
+        def queue_gain():
+            if len(gains) < len(order):
+                b, g, j0 = order[len(gains)]
+                gains.append(gain_unit(j0, b))
+
+        def product(k):
+            b, g, j0 = order[k]
             first, width = GROUPS[g]
-            for j0 in range(first, first + width, UNIT):
-                gain = early[j0 // UNIT] if b == 0 and j0 < EARLY_UNITS * UNIT else gain_unit(j0, b)
-                multiply(gain, h[g], b * width + j0 - first, j0, b)
+            multiply(gains[k], h[g], b * width + j0 - first, j0, b)
+            queue_gain()
+
+        def units(g):
+            for k in range(len(places), len(order)):
+                if order[k][1] == g:
+                    product(k)
 
         def quantize_h(g, first_pass, passes):
             width = GROUPS[g][1]
@@ -294,55 +292,54 @@ def tile_list_scheduled_gain_mixing_kernel(
         reorder_columns(wr_codes, wr_raw, 4)
         for i in range(2):
             gather_scales(i)
-        gather_demand_words(0)
-        for k in range(4):
-            round_ws(k)
+        for i in range(2):
+            gather_words(demand_words[i], lists[i][:])
+        round_ws(0)
+        round_ws(1)
         reorder_columns(wr_planes, wr_raw_scales, 2)
         quantize_ws(0)
-        gather_demand_words(1)
-        quantize_ws(1)
         gather_scales(2)
+        quantize_ws(1)
         gather_words(gain_words, lists[2][:])
         reorder_columns(wg_planes, wg_raw_scales, 2)
         reorder_columns(wg_codes, wg_raw, 8)
         rows_turned = psum.tile([P, PASSES, P], F32, name="rows_turned", tag="mix", bufs=3)
         for b in range(PASSES):
             nc.tensor.transpose(rows_turned[:, b, :], rows[:, b * P : (b + 1) * P], identity[:])
-        for u in range(TILES):
+        for t in range(PACK):
+            demand(t, 0)
+        nc.scalar.copy(columns[:], rows_turned[:, :, 0:ROWS])
+        for t in range(PACK):
+            demand(t, 1)
+            clamp(nc.vector, t, clamped0, demand0)
+        for u in range(PACK, TILES):
             demand(u, 0)
-            if u == 0:
-                nc.scalar.copy(columns[:], rows_turned[:, :, 0:ROWS])
-            if u >= PACK:
-                clamp(nc.vector, u, clamped1[0], demand1[0])
-        early = []
-        for u in range(TILES):
-            if u == TILES - EARLY_UNITS:
-                early = [gain_unit(k * UNIT, 0) for k in range(EARLY_UNITS)]
-            demand(u, 1)
-            if u < PACK:
-                clamp(nc.vector, u, clamped0, demand0)
-            else:
-                clamp(nc.gpsimd, u, clamped1[1], demand1[1])
+            clamp(nc.gpsimd, u, clamped1[0], demand1[0])
+            if u == PACK:
+                for k in range(AHEAD):
+                    queue_gain()
         round_wm(0)
         round_wm(1)
-
-        for b in range(PASSES):
-            units(0, b)
-            units(1, b)
-        for g in range(2, len(GROUPS)):
-            units(g, 0)
+        for k in range(len(places)):
+            product(k)
+            if k % 2 == 1:
+                demand(PACK + k // 2, 1)
+        units(0)
         quantize_wm()
         quantize_h(0, 0, PASSES)
-        quantize_h(1, 0, PASSES)
         mix(0)
-        mix(1)
-        units(2, 1)
+        for u in range(PACK, TILES):
+            clamp(nc.vector, u, clamped1[1], demand1[1])
+        units(1)
         quantize_h(3, 0, 1)
+        quantize_h(1, 0, PASSES)
+        mix(1)
+        units(2)
         quantize_h(4, 0, 1)
         quantize_h(2, 0, PASSES)
         mix(2)
-        units(3, 1)
-        units(4, 1)
+        units(3)
+        units(4)
         quantize_h(3, 1, 1)
         quantize_h(4, 1, 1)
         mix(3)

@@ -50,7 +50,7 @@ def tile_list_scheduled_gain_mixing_kernel(
         lists = [held("list%d" % i, [P, S // 16], U16) for i in range(3)]
         table_words = held("table_words", [P, T], I32)
         table_scales = held("table_scales", [P, T // 4], I32)
-        wr_raw_scales = held("wr_raw_scales", [P, H // 4], I32)
+        wr_raw_scales = reused("wr_raw_scales", [P, H // 4], I32, 71680)
         wg_raw_scales = held("wg_raw_scales", [P, H // 4], I32)
         wr_raw = held("wr_raw", [P, H // 2], I32)
         wg_raw = held("wg_raw", [P, H], I32)
@@ -102,11 +102,11 @@ def tile_list_scheduled_gain_mixing_kernel(
 
         columns = reused("columns", [P, PASSES, ROWS], F32, 16448)
 
-        ws_grouped = [held("ws_grouped%d" % b, [P, PACK, HALF], BF16) for b in range(PASSES)]
-        demand_words = [held("words%d" % i, [P, S], U32) for i in range(2)]
-        gain_words = reused("gain_words", [P, S], U32, 8256)
+        ws_grouped = [reused("ws_grouped%d" % b, [P, PACK, HALF], BF16, 81920 + 4096 * b) for b in range(PASSES)]
+        demand_words = [reused("words0", [P, S], U32, 71680), held("words1", [P, S], U32)]
+        gain_words = reused("gain_words", [P, S], U32, 86016)
         picked_scales = [held("scales%d" % i, [P, S], U8) for i in range(2)]
-        picked_scales.append(reused("scales2", [P, S], U8, 0))
+        picked_scales.append(reused("scales2", [P, S], U8, 81920))
 
         def gather_scales(i):
             nc.vector.tensor_copy(picked_scales[i][:], table_scales[:].bitcast(U8).indirect(lists[i][:]))
@@ -124,7 +124,7 @@ def tile_list_scheduled_gain_mixing_kernel(
         wr_planes = held("wr_planes", [P, H // 4], I32)
         wg_codes = reused("wg_codes", [P, H], I32, 12352)
         wg_planes = reused("wg_planes", [P, H // 4], I32, 16640)
-        ws_codes = [reused("ws_codes0", [P, HALF], U32, 63488), held("ws_codes1", [P, HALF], U32)]
+        ws_codes = [held("ws_codes%d" % b, [P, HALF], U32) for b in range(PASSES)]
         ws_scales = held("ws_scales", [P, H], U8)
 
         def round_ws(b):
@@ -144,7 +144,7 @@ def tile_list_scheduled_gain_mixing_kernel(
 
         wm_codes = reused("wm_codes", [P, PASSES * N], U32, 34816)
         wm_scales = held("wm_scales", [P, PASSES * N], U8)
-        wm_grouped = reused("wm_grouped", [P, PASSES * N * PACK], BF16, 63488)
+        wm_grouped = reused("wm_grouped", [P, PASSES * N * PACK], BF16, 71680)
 
         def round_wm(b):
             nc.scalar.copy(
@@ -161,30 +161,31 @@ def tile_list_scheduled_gain_mixing_kernel(
                 )
 
         demand0 = reused("demand0", [P, PACK, S], F32, 18432)
-        demand1 = [reused("demand1_0", [P, PACK, CHUNK], F32, 36864), held("demand1_1", [P, PACK, CHUNK], F32)]
+        demand1 = [held("demand1_0", [P, PACK, CHUNK], F32), reused("demand1_1", [P, PACK, CHUNK], F32, 36864)]
         clamped0 = held("clamped0", [P, PACK, S], F32)
-        clamped1 = [reused("clamped1_%d" % c, [P, PACK, CHUNK], F32, 18432 + 22528 * c) for c in range(CHUNKS)]
+        clamped1 = [reused("clamped1_%d" % c, [P, PACK, CHUNK], F32, 18432 + 8192 * c) for c in range(CHUNKS)]
 
         def demand(u, c):
             b, t = divmod(u, PACK)
             cols = slice(u * P, (u + 1) * P)
             picks = slice(c * CHUNK, (c + 1) * CHUNK)
-            acc = psum.tile([P, CHUNK], F32, name="demand", tag="first", bufs=5)
-            nc.tensor.matmul_mx(
-                out=acc[:],
-                lhsT=ws_codes[b][:, t * P : (t + 1) * P].bitcast(FP8X4),
-                lhsT_scale=ws_scales[:, cols],
-                rhs=demand_words[0][:, picks].bitcast(FP8X4),
-                rhs_scale=picked_scales[0][:, picks],
-                start=True,
-                stop=False,
-            )
+            tag, bufs = ("mix", 3) if b == 0 and c == 1 and t > 0 else ("first", 5)
+            acc = psum.tile([P, CHUNK], F32, name="demand", tag=tag, bufs=bufs)
             nc.tensor.matmul_mx(
                 out=acc[:],
                 lhsT=wr_codes[:].bitcast(U8)[:, 2 * u * P : 2 * (u + 1) * P].bitcast(FP4X4),
                 lhsT_scale=wr_planes[:].bitcast(U8)[:, cols],
                 rhs=demand_words[1][:, picks].bitcast(FP8X4),
                 rhs_scale=picked_scales[1][:, picks],
+                start=True,
+                stop=False,
+            )
+            nc.tensor.matmul_mx(
+                out=acc[:],
+                lhsT=ws_codes[b][:, t * P : (t + 1) * P].bitcast(FP8X4),
+                lhsT_scale=ws_scales[:, cols],
+                rhs=demand_words[0][:, picks].bitcast(FP8X4),
+                rhs_scale=picked_scales[0][:, picks],
                 start=False,
                 stop=True,
             )
@@ -227,7 +228,7 @@ def tile_list_scheduled_gain_mixing_kernel(
             )
 
         h = [held("h%d" % g, [P, PASSES * PACK * width], BF16) for g, (first, width) in enumerate(GROUPS)]
-        h_offsets = (49152, 51200, 53248, 37888, 38912)
+        h_offsets = (37888, 39936, 49152, 41984, 43008)
         h_codes = [
             reused("h_codes%d" % g, [P, PASSES * width], U32, h_offsets[g]) for g, (first, width) in enumerate(GROUPS)
         ]
@@ -292,17 +293,17 @@ def tile_list_scheduled_gain_mixing_kernel(
         reorder_columns(wr_codes, wr_raw, 4)
         for i in range(2):
             gather_scales(i)
-        for i in range(2):
-            gather_words(demand_words[i], lists[i][:])
+        gather_words(demand_words[1], lists[1][:])
+        reorder_columns(wr_planes, wr_raw_scales, 2)
+        gather_words(demand_words[0], lists[0][:])
         round_ws(0)
         round_ws(1)
-        reorder_columns(wr_planes, wr_raw_scales, 2)
         quantize_ws(0)
         gather_scales(2)
         quantize_ws(1)
-        gather_words(gain_words, lists[2][:])
         reorder_columns(wg_planes, wg_raw_scales, 2)
         reorder_columns(wg_codes, wg_raw, 8)
+        gather_words(gain_words, lists[2][:])
         rows_turned = psum.tile([P, PASSES, P], F32, name="rows_turned", tag="mix", bufs=3)
         for b in range(PASSES):
             nc.tensor.transpose(rows_turned[:, b, :], rows[:, b * P : (b + 1) * P], identity[:])
@@ -312,29 +313,25 @@ def tile_list_scheduled_gain_mixing_kernel(
         for t in range(PACK):
             demand(t, 1)
             clamp(nc.vector, t, clamped0, demand0)
-        for u in range(PACK, TILES):
-            demand(u, 0)
-            clamp(nc.gpsimd, u, clamped1[0], demand1[0])
-            if u == PACK:
-                for k in range(AHEAD):
-                    queue_gain()
+        for c in range(CHUNKS):
+            for u in range(PACK, TILES):
+                demand(u, c)
+                clamp(nc.gpsimd, u, clamped1[c], demand1[c])
         round_wm(0)
         round_wm(1)
+        for k in range(AHEAD):
+            queue_gain()
         for k in range(len(places)):
             product(k)
-            if k % 2 == 1:
-                demand(PACK + k // 2, 1)
         units(0)
+        units(1)
         quantize_wm()
         quantize_h(0, 0, PASSES)
-        mix(0)
-        for u in range(PACK, TILES):
-            clamp(nc.vector, u, clamped1[1], demand1[1])
-        units(1)
-        quantize_h(3, 0, 1)
         quantize_h(1, 0, PASSES)
+        mix(0)
         mix(1)
         units(2)
+        quantize_h(3, 0, 1)
         quantize_h(4, 0, 1)
         quantize_h(2, 0, PASSES)
         mix(2)

@@ -53,10 +53,10 @@ def tile_list_scheduled_gain_mixing_kernel(
         wr_raw_scales = reused("wr_raw_scales", [P, H // 4], I32, 71680)
         wg_raw_scales = held("wg_raw_scales", [P, H // 4], I32)
         wr_raw = held("wr_raw", [P, H // 2], I32)
-        wg_raw = held("wg_raw", [P, H], I32)
+        wg_raw = reused("wg_raw", [P, H], I32, 90112)
         ws_raw = [reused("ws_raw%d" % b, [P, PACK, HALF], F32, 12288 * b) for b in range(PASSES)]
         wm_raw = [held("wm_raw%d" % b, [P, PACK, N], F32) for b in range(PASSES)]
-        rows = held("rows", [P, PASSES * P], F32)
+        rows = reused("rows", [P, PASSES * P], F32, 20480)
         identity = held("identity", [P, P], F32)
 
         nc.vector.memset(table_scales[:], 0)
@@ -102,14 +102,18 @@ def tile_list_scheduled_gain_mixing_kernel(
 
         columns = reused("columns", [P, PASSES, ROWS], F32, 16448)
 
-        ws_grouped = [reused("ws_grouped%d" % b, [P, PACK, HALF], BF16, 81920 + 4096 * b) for b in range(PASSES)]
+        ws_grouped = [reused("ws_grouped%d" % b, [P, PACK, HALF], BF16, 81408 + 4608 * b) for b in range(PASSES)]
         demand_words = [reused("words0", [P, S], U32, 71680), held("words1", [P, S], U32)]
-        gain_words = reused("gain_words", [P, S], U32, 86016)
+        gain_words = reused("gain_words", [P, S], U32, 85504)
         picked_scales = [held("scales%d" % i, [P, S], U8) for i in range(2)]
-        picked_scales.append(reused("scales2", [P, S], U8, 81920))
+        gain_scales = [reused("scales2_0", [P, CHUNK], U8, 81920), reused("scales2_1", [P, CHUNK], U8, 85504 + 4096)]
 
         def gather_scales(i):
             nc.vector.tensor_copy(picked_scales[i][:], table_scales[:].bitcast(U8).indirect(lists[i][:]))
+
+        def gather_gain_scales(c):
+            offsets = lists[2][:, c * CHUNK // 16 : (c + 1) * CHUNK // 16]
+            nc.vector.tensor_copy(gain_scales[c][:], table_scales[:].bitcast(U8).indirect(offsets))
 
         def gather_words(picked, offsets):
             nc.vector.tensor_copy(picked[:], table_words[:].bitcast(U32).indirect(offsets))
@@ -142,7 +146,7 @@ def tile_list_scheduled_gain_mixing_kernel(
                 in_=ws_grouped[b][:].rearrange("p t c -> p (t c)"),
             )
 
-        wm_codes = reused("wm_codes", [P, PASSES * N], U32, 34816)
+        wm_codes = reused("wm_codes", [P, PASSES * N], U32, 38912)
         wm_scales = held("wm_scales", [P, PASSES * N], U8)
         wm_grouped = reused("wm_grouped", [P, PASSES * N * PACK], BF16, 71680)
 
@@ -160,10 +164,10 @@ def tile_list_scheduled_gain_mixing_kernel(
                     in_=wm_grouped[:, PACK * first : PACK * last],
                 )
 
-        demand0 = reused("demand0", [P, PACK, S], F32, 18432)
-        demand1 = [held("demand1_0", [P, PACK, CHUNK], F32), reused("demand1_1", [P, PACK, CHUNK], F32, 36864)]
-        clamped0 = held("clamped0", [P, PACK, S], F32)
-        clamped1 = [reused("clamped1_%d" % c, [P, PACK, CHUNK], F32, 18432 + 8192 * c) for c in range(CHUNKS)]
+        demand0 = [reused("demand0_%d" % c, [P, PACK, CHUNK], F32, 18432 + 8192 * c) for c in range(CHUNKS)]
+        demand1 = [held("demand1_0", [P, PACK, CHUNK], F32), reused("demand1_1", [P, PACK, CHUNK], F32, 40960)]
+        clamped0 = [reused("clamped0_0", [P, PACK, CHUNK], F32, 90112), held("clamped0_1", [P, PACK, CHUNK], F32)]
+        clamped1 = [reused("clamped1_%d" % c, [P, PACK, CHUNK], F32, 22528 + 8192 * c) for c in range(CHUNKS)]
 
         def demand(u, c):
             b, t = divmod(u, PACK)
@@ -189,7 +193,7 @@ def tile_list_scheduled_gain_mixing_kernel(
                 start=False,
                 stop=True,
             )
-            nc.scalar.copy(demand0[:, t, picks] if b == 0 else demand1[c][:, t, :], acc[:])
+            nc.scalar.copy((demand0, demand1)[b][c][:, t, :], acc[:])
 
         def clamp(engine, u, target, source):
             b, t = divmod(u, PACK)
@@ -211,7 +215,7 @@ def tile_list_scheduled_gain_mixing_kernel(
                     lhsT=wg_codes[:, cols].bitcast(FP8X4),
                     lhsT_scale=wg_planes[:].bitcast(U8)[:, cols],
                     rhs=gain_words[:, j0 : j0 + UNIT].bitcast(FP8X4),
-                    rhs_scale=picked_scales[2][:, j0 : j0 + UNIT],
+                    rhs_scale=gain_scales[j0 // CHUNK][:, j0 % CHUNK : j0 % CHUNK + UNIT],
                     start=True,
                     stop=True,
                 )
@@ -219,7 +223,7 @@ def tile_list_scheduled_gain_mixing_kernel(
 
         def multiply(gain, h_tile, word, j0, b):
             c, within = divmod(j0, CHUNK)
-            source = clamped0[:, :, j0 : j0 + UNIT] if b == 0 else clamped1[c][:, :, within : within + UNIT]
+            source = (clamped0, clamped1)[b][c][:, :, within : within + UNIT]
             nc.vector.tensor_tensor(
                 h_tile[:, PACK * word : PACK * (word + UNIT)].rearrange("p (h l t) -> p h t l", l=4, t=PACK),
                 source.rearrange("p t (h l) -> p h t l", l=4),
@@ -228,14 +232,15 @@ def tile_list_scheduled_gain_mixing_kernel(
             )
 
         h = [held("h%d" % g, [P, PASSES * PACK * width], BF16) for g, (first, width) in enumerate(GROUPS)]
-        h_offsets = (37888, 39936, 49152, 41984, 43008)
+        h_offsets = (41984, 44032, 53248, 46080, 47104)
         h_codes = [
             reused("h_codes%d" % g, [P, PASSES * width], U32, h_offsets[g]) for g, (first, width) in enumerate(GROUPS)
         ]
         h_scales = [held("h_scales%d" % g, [P, PASSES * width], U8) for g, (first, width) in enumerate(GROUPS)]
 
         places = [(g, j0) for g, (first, width) in enumerate(GROUPS) for j0 in range(first, first + width, UNIT)]
-        order = [(b, g, j0) for b in range(PASSES) for g, j0 in places]
+        middle = CHUNK // UNIT
+        order = [(0, g, j0) for g, j0 in places[middle:] + places[:middle]] + [(1, g, j0) for g, j0 in places]
         gains = []
 
         def queue_gain():
@@ -299,35 +304,42 @@ def tile_list_scheduled_gain_mixing_kernel(
         round_ws(0)
         round_ws(1)
         quantize_ws(0)
-        gather_scales(2)
+        gather_gain_scales(0)
         quantize_ws(1)
         reorder_columns(wg_planes, wg_raw_scales, 2)
         reorder_columns(wg_codes, wg_raw, 8)
+        gather_gain_scales(1)
         gather_words(gain_words, lists[2][:])
         rows_turned = psum.tile([P, PASSES, P], F32, name="rows_turned", tag="mix", bufs=3)
         for b in range(PASSES):
             nc.tensor.transpose(rows_turned[:, b, :], rows[:, b * P : (b + 1) * P], identity[:])
-        for t in range(PACK):
-            demand(t, 0)
         nc.scalar.copy(columns[:], rows_turned[:, :, 0:ROWS])
         for t in range(PACK):
+            demand(t, 0)
+        for t in range(PACK):
+            clamp(nc.gpsimd, t, clamped0[0], demand0[0])
+        for t in range(PACK):
             demand(t, 1)
-            clamp(nc.vector, t, clamped0, demand0)
-        for c in range(CHUNKS):
-            for u in range(PACK, TILES):
-                demand(u, c)
-                clamp(nc.gpsimd, u, clamped1[c], demand1[c])
-        round_wm(0)
-        round_wm(1)
+            clamp(nc.vector, t, clamped0[1], demand0[1])
+        for u in range(PACK, TILES):
+            demand(u, 0)
+            clamp(nc.gpsimd, u, clamped1[0], demand1[0])
+        demand(PACK, 1)
+        clamp(nc.gpsimd, PACK, clamped1[1], demand1[1])
         for k in range(AHEAD):
             queue_gain()
         for k in range(len(places)):
+            if k % 2 == 0 and PACK + 1 + k // 2 < TILES:
+                demand(PACK + 1 + k // 2, 1)
+                clamp(nc.gpsimd, PACK + 1 + k // 2, clamped1[1], demand1[1])
             product(k)
+        round_wm(0)
+        round_wm(1)
         units(0)
         units(1)
-        quantize_wm()
         quantize_h(0, 0, PASSES)
         quantize_h(1, 0, PASSES)
+        quantize_wm()
         mix(0)
         mix(1)
         units(2)

@@ -165,9 +165,9 @@ def tile_list_scheduled_gain_mixing_kernel(
                 )
 
         demand0 = [reused("demand0_%d" % c, [P, PACK, CHUNK], F32, 18432 + 8192 * c) for c in range(CHUNKS)]
-        demand1 = [held("demand1_0", [P, PACK, CHUNK], F32), reused("demand1_1", [P, PACK, CHUNK], F32, 40960)]
+        demand1 = [reused("demand1_%d" % c, [P, PACK, CHUNK], F32, (57344, 40960)[c]) for c in range(CHUNKS)]
         clamped0 = [reused("clamped0_0", [P, PACK, CHUNK], F32, 90112), held("clamped0_1", [P, PACK, CHUNK], F32)]
-        clamped1 = [reused("clamped1_%d" % c, [P, PACK, CHUNK], F32, 22528 + 8192 * c) for c in range(CHUNKS)]
+        clamped1 = [held("clamped1_0", [P, PACK, CHUNK], F32), reused("clamped1_1", [P, PACK, CHUNK], F32, 57344)]
 
         def demand(u, c):
             b, t = divmod(u, PACK)
@@ -323,7 +323,7 @@ def tile_list_scheduled_gain_mixing_kernel(
             clamp(nc.vector, t, clamped0[1], demand0[1])
         for u in range(PACK, TILES):
             demand(u, 0)
-            clamp(nc.gpsimd, u, clamped1[0], demand1[0])
+            clamp(nc.vector, u, clamped1[0], demand1[0])
         demand(PACK, 1)
         clamp(nc.gpsimd, PACK, clamped1[1], demand1[1])
         for k in range(AHEAD):
@@ -338,9 +338,9 @@ def tile_list_scheduled_gain_mixing_kernel(
         units(0)
         units(1)
         quantize_h(0, 0, PASSES)
-        quantize_h(1, 0, PASSES)
         quantize_wm()
         mix(0)
+        quantize_h(1, 0, PASSES)
         mix(1)
         units(2)
         quantize_h(3, 0, 1)

@@ -30,6 +30,7 @@ GROUPS = ((0, 256), (256, 256), (512, 256), (768, 128), (896, 128))
 LO, HI, TRIM = 0, PACK, 2 * PACK
 ROWS = 16
 AHEAD = 3
+SHARE = 2
 
 
 def tile_list_scheduled_gain_mixing_kernel(
@@ -165,9 +166,19 @@ def tile_list_scheduled_gain_mixing_kernel(
                 )
 
         demand0 = [reused("demand0_%d" % c, [P, PACK, CHUNK], F32, 18432 + 8192 * c) for c in range(CHUNKS)]
-        demand1 = [reused("demand1_%d" % c, [P, PACK, CHUNK], F32, (57344, 40960)[c]) for c in range(CHUNKS)]
+        demand1_vector = reused("demand1_vector", [P, SHARE, CHUNK], F32, 57344)
+        demand1_gpsimd = held("demand1_gpsimd", [P, PACK - SHARE, CHUNK], F32)
+        demand1_last = reused("demand1_last", [P, PACK, CHUNK], F32, 40960)
         clamped0 = [reused("clamped0_0", [P, PACK, CHUNK], F32, 90112), held("clamped0_1", [P, PACK, CHUNK], F32)]
         clamped1 = [held("clamped1_0", [P, PACK, CHUNK], F32), reused("clamped1_1", [P, PACK, CHUNK], F32, 57344)]
+
+        def demand_rows(u, c):
+            b, t = divmod(u, PACK)
+            if b == 0:
+                return demand0[c][:, t, :]
+            if c == 1:
+                return demand1_last[:, t, :]
+            return demand1_vector[:, t, :] if t < SHARE else demand1_gpsimd[:, t - SHARE, :]
 
         def demand(u, c):
             b, t = divmod(u, PACK)
@@ -193,13 +204,13 @@ def tile_list_scheduled_gain_mixing_kernel(
                 start=False,
                 stop=True,
             )
-            nc.scalar.copy((demand0, demand1)[b][c][:, t, :], acc[:])
+            nc.scalar.copy(demand_rows(u, c), acc[:])
 
-        def clamp(engine, u, target, source):
+        def clamp(engine, u, c):
             b, t = divmod(u, PACK)
             engine.tensor_scalar(
-                target[:, t, :],
-                source[:, t, :],
+                (clamped0, clamped1)[b][c][:, t, :],
+                demand_rows(u, c),
                 columns[:, b, HI + t : HI + t + 1],
                 columns[:, b, LO + t : LO + t + 1],
                 ALU.min,
@@ -317,30 +328,33 @@ def tile_list_scheduled_gain_mixing_kernel(
         for t in range(PACK):
             demand(t, 0)
         for t in range(PACK):
-            clamp(nc.gpsimd, t, clamped0[0], demand0[0])
+            clamp(nc.gpsimd, t, 0)
         for t in range(PACK):
             demand(t, 1)
-            clamp(nc.vector, t, clamped0[1], demand0[1])
-        for u in range(PACK, TILES):
+            clamp(nc.vector, t, 1)
+        for u in range(PACK, PACK + SHARE):
             demand(u, 0)
-            clamp(nc.vector, u, clamped1[0], demand1[0])
+            clamp(nc.vector, u, 0)
         demand(PACK, 1)
-        clamp(nc.gpsimd, PACK, clamped1[1], demand1[1])
+        clamp(nc.gpsimd, PACK, 1)
+        for u in range(PACK + SHARE, TILES):
+            demand(u, 0)
+            clamp(nc.gpsimd, u, 0)
         for k in range(AHEAD):
             queue_gain()
         for k in range(len(places)):
             if k % 2 == 0 and PACK + 1 + k // 2 < TILES:
                 demand(PACK + 1 + k // 2, 1)
-                clamp(nc.gpsimd, PACK + 1 + k // 2, clamped1[1], demand1[1])
+                clamp(nc.gpsimd, PACK + 1 + k // 2, 1)
             product(k)
         round_wm(0)
         round_wm(1)
         units(0)
         units(1)
         quantize_h(0, 0, PASSES)
+        quantize_h(1, 0, PASSES)
         quantize_wm()
         mix(0)
-        quantize_h(1, 0, PASSES)
         mix(1)
         units(2)
         quantize_h(3, 0, 1)

@@ -76,22 +76,22 @@ def tile_list_scheduled_gain_mixing_kernel(
             nc.sync.dma_start(ws_raw[b][:], ws[:, b * HALF : (b + 1) * HALF].rearrange("(p j) c -> p j c", j=PACK))
 
         def load_limits(first, vector):
-            nc.gpsimd.dma_start(
+            nc.sync.dma_start(
                 rows[first : first + PACK, :].rearrange("t (q i) -> t q i", i=8),
                 vector.rearrange("(q t i) -> t q i", t=PACK, i=8),
             )
 
-        load_limits(LO, lo)
-        load_limits(HI, hi)
-        nc.gpsimd.dma_start(rows[TRIM : TRIM + N_TILES, 0:P], trim.rearrange("(n p) -> n p", p=P))
         make_identity(nc, identity[:])
         nc.sync.dma_start(lists[0][:], offs)
         nc.sync.dma_start(lists[1][:], offs2)
         nc.sync.dma_start(wr_raw[:], wr_words[0].bitcast(I32))
         load_scale_rows(table_scales, tab_scales)
         nc.sync.dma_start(table_words[:], tab_words[0].rearrange("p n t -> p (n t)").bitcast(I32))
-        load_ws(0)
         load_scale_rows(wr_raw_scales, wr_scales)
+        load_ws(0)
+        load_limits(LO, lo)
+        load_limits(HI, hi)
+        nc.sync.dma_start(rows[TRIM : TRIM + N_TILES, 0:P], trim.rearrange("(n p) -> n p", p=P))
         load_ws(1)
         nc.sync.dma_start(lists[2][:], offs3)
         nc.sync.dma_start(wg_raw[:], wg_words[0].rearrange("p n t -> p (n t)").bitcast(I32))

@@ -27,8 +27,8 @@ CHUNKS = S // CHUNK
 UNIT = 128
 N_TILES = N // P
 GROUPS = ((0, 256), (256, 256), (512, 256), (768, 128), (896, 128))
-LO, HI, TRIM = 0, PACK, 2 * PACK
-ROWS = 16
+LO, HI = 0, PACK
+ROWS = 8
 AHEAD = 3
 SHARE = 2
 
@@ -66,11 +66,9 @@ def tile_list_scheduled_gain_mixing_kernel(
         nc.vector.memset(wg_raw_scales[:], 0)
 
         def load_scale_rows(plane, scales):
-            for quadrant in range(4):
-                nc.sync.dma_start(
-                    plane[32 * quadrant : 32 * quadrant + 4, :],
-                    scales[0, 4 * quadrant : 4 * quadrant + 4, :].bitcast(I32),
-                )
+            by_row = scales[0].rearrange("(q r) n -> r q n", r=4)
+            for r in range(4):
+                nc.sync.dma_start(plane[r:P:32, :], by_row[r].bitcast(I32))
 
         def load_ws(b):
             nc.sync.dma_start(ws_raw[b][:], ws[:, b * HALF : (b + 1) * HALF].rearrange("(p j) c -> p j c", j=PACK))
@@ -91,7 +89,6 @@ def tile_list_scheduled_gain_mixing_kernel(
         load_ws(0)
         load_limits(LO, lo)
         load_limits(HI, hi)
-        nc.sync.dma_start(rows[TRIM : TRIM + N_TILES, 0:P], trim.rearrange("(n p) -> n p", p=P))
         load_ws(1)
         nc.sync.dma_start(lists[2][:], offs3)
         nc.sync.dma_start(wg_raw[:], wg_words[0].rearrange("p n t -> p (n t)").bitcast(I32))
@@ -100,6 +97,9 @@ def tile_list_scheduled_gain_mixing_kernel(
             wm_rows = wm[b * HALF : (b + 1) * HALF, :].rearrange("(q t i) n -> t q i n", t=PACK, i=8)
             for t in range(PACK):
                 nc.sync.dma_start(wm_raw[b][:, t, :], wm_rows[t])
+        trims = held("trims", [P, N_TILES], F32)
+        with nc.allow_non_contiguous_dma(reason="one trim value for each partition and output tile"):
+            nc.sync.dma_start(trims[:], trim.rearrange("(n p) -> p n", p=P))
 
         columns = reused("columns", [P, PASSES, ROWS], F32, 16448)
 
@@ -299,7 +299,7 @@ def tile_list_scheduled_gain_mixing_kernel(
                     stop=(b == PASSES - 1),
                 )
             for n in range(N_TILES):
-                trim_column = columns[:, 0, TRIM + n : TRIM + n + 1]
+                trim_column = trims[:, n : n + 1]
                 if g >= len(GROUPS) - 2 and (g + n) % 2 == 1:
                     nc.vector.tensor_scalar(result[:, n, :], sums[n][:], trim_column, None, ALU.add)
                 else:

@@ -26,7 +26,7 @@ CHUNK = 512
 CHUNKS = S // CHUNK
 UNIT = 128
 N_TILES = N // P
-GROUPS = ((0, 256), (256, 256), (512, 256), (768, 128), (896, 128))
+GROUPS = ((0, 256), (256, 256), (512, 256), (768, 256))
 LO, HI = 0, PACK
 ROWS = 8
 AHEAD = 3
@@ -51,16 +51,16 @@ def tile_list_scheduled_gain_mixing_kernel(
         lists = [held("list%d" % i, [P, S // 16], U16) for i in range(3)]
         table_words = held("table_words", [P, T], I32)
         table_scales = held("table_scales", [P, T // 4], I32)
-        wr_raw_scales = reused("wr_raw_scales", [P, H // 4], I32, 71680)
-        wg_raw_scales = held("wg_raw_scales", [P, H // 4], I32)
+        wr_raw_scales = reused("wr_raw_scales", [P, H // 4], I32, 98304)
+        wg_raw_scales = reused("wg_raw_scales", [P, H // 4], I32, 90112)
         wr_raw = held("wr_raw", [P, H // 2], I32)
-        wg_raw = reused("wg_raw", [P, H], I32, 90112)
+        wg_raw = held("wg_raw", [P, H], I32)
         ws_raw = [reused("ws_raw%d" % b, [P, PACK, HALF], F32, 12288 * b) for b in range(PASSES)]
         wm_raw = [held("wm_raw%d" % b, [P, PACK, N], F32) for b in range(PASSES)]
         rows = reused("rows", [P, PASSES * P], F32, 20480)
         identity = held("identity", [P, P], F32)
 
-        nc.vector.memset(table_scales[:], 0)
+        nc.gpsimd.memset(table_scales[:], 0)
         nc.gpsimd.memset(rows[:], 0.0)
         nc.vector.memset(wr_raw_scales[:], 0)
         nc.vector.memset(wg_raw_scales[:], 0)
@@ -82,8 +82,9 @@ def tile_list_scheduled_gain_mixing_kernel(
         make_identity(nc, identity[:])
         nc.sync.dma_start(lists[0][:], offs)
         nc.sync.dma_start(lists[1][:], offs2)
-        nc.sync.dma_start(wr_raw[:], wr_words[0].bitcast(I32))
         load_scale_rows(table_scales, tab_scales)
+        nc.sync.dma_start(wr_raw[:], wr_words[0].bitcast(I32))
+        nc.sync.dma_start(wg_raw[:], wg_words[0].rearrange("p n t -> p (n t)").bitcast(I32))
         nc.sync.dma_start(table_words[:], tab_words[0].rearrange("p n t -> p (n t)").bitcast(I32))
         load_scale_rows(wr_raw_scales, wr_scales)
         load_ws(0)
@@ -91,7 +92,6 @@ def tile_list_scheduled_gain_mixing_kernel(
         load_limits(HI, hi)
         load_ws(1)
         nc.sync.dma_start(lists[2][:], offs3)
-        nc.sync.dma_start(wg_raw[:], wg_words[0].rearrange("p n t -> p (n t)").bitcast(I32))
         load_scale_rows(wg_raw_scales, wg_scales)
         for b in range(PASSES):
             wm_rows = wm[b * HALF : (b + 1) * HALF, :].rearrange("(q t i) n -> t q i n", t=PACK, i=8)
@@ -117,17 +117,23 @@ def tile_list_scheduled_gain_mixing_kernel(
             nc.vector.tensor_copy(gain_scales[c][:], table_scales[:].bitcast(U8).indirect(offsets))
 
         def gather_words(picked, offsets):
-            nc.vector.tensor_copy(picked[:], table_words[:].bitcast(U32).indirect(offsets))
+            nc.vector.tensor_copy(picked, table_words[:].bitcast(U32).indirect(offsets))
 
-        def reorder_columns(moved, raw, run):
-            nc.vector.tensor_copy(
+        def reorder_columns(engine, moved, raw, run):
+            engine.tensor_copy(
                 moved[:].rearrange("p (b t q e) -> p b t q e", b=PASSES, t=PACK, e=run),
                 raw[:].rearrange("p (b q t e) -> p b t q e", b=PASSES, t=PACK, e=run),
             )
 
+        def reorder_wg(b):
+            nc.gpsimd.tensor_copy(
+                wg_codes[b][:].rearrange("p (t q e) -> p t q e", t=PACK, e=8),
+                wg_raw[:, b * HALF : (b + 1) * HALF].rearrange("p (q t e) -> p t q e", t=PACK, e=8),
+            )
+
         wr_codes = held("wr_codes", [P, H // 2], I32)
         wr_planes = held("wr_planes", [P, H // 4], I32)
-        wg_codes = reused("wg_codes", [P, H], I32, 12352)
+        wg_codes = [held("wg_codes0", [P, HALF], I32), reused("wg_codes1", [P, HALF], I32, 98304)]
         wg_planes = reused("wg_planes", [P, H // 4], I32, 16640)
         ws_codes = [held("ws_codes%d" % b, [P, HALF], U32) for b in range(PASSES)]
         ws_scales = held("ws_scales", [P, H], U8)
@@ -184,7 +190,7 @@ def tile_list_scheduled_gain_mixing_kernel(
             b, t = divmod(u, PACK)
             cols = slice(u * P, (u + 1) * P)
             picks = slice(c * CHUNK, (c + 1) * CHUNK)
-            tag, bufs = ("mix", 3) if b == 0 and c == 1 and t > 0 else ("first", 5)
+            tag, bufs = ("mix", 3) if c == 1 and t > 0 else ("first", 5)
             acc = psum.tile([P, CHUNK], F32, name="demand", tag=tag, bufs=bufs)
             nc.tensor.matmul_mx(
                 out=acc[:],
@@ -223,7 +229,7 @@ def tile_list_scheduled_gain_mixing_kernel(
                 cols = slice((PACK * b + t) * P, (PACK * b + t + 1) * P)
                 nc.tensor.matmul_mx(
                     out=gain[:, t, :],
-                    lhsT=wg_codes[:, cols].bitcast(FP8X4),
+                    lhsT=wg_codes[b][:, t * P : (t + 1) * P].bitcast(FP8X4),
                     lhsT_scale=wg_planes[:].bitcast(U8)[:, cols],
                     rhs=gain_words[:, j0 : j0 + UNIT].bitcast(FP8X4),
                     rhs_scale=gain_scales[j0 // CHUNK][:, j0 % CHUNK : j0 % CHUNK + UNIT],
@@ -243,7 +249,7 @@ def tile_list_scheduled_gain_mixing_kernel(
             )
 
         h = [held("h%d" % g, [P, PASSES * PACK * width], BF16) for g, (first, width) in enumerate(GROUPS)]
-        h_offsets = (41984, 44032, 53248, 46080, 47104)
+        h_offsets = (41984, 44032, 53248, 46080)
         h_codes = [
             reused("h_codes%d" % g, [P, PASSES * width], U32, h_offsets[g]) for g, (first, width) in enumerate(GROUPS)
         ]
@@ -270,57 +276,72 @@ def tile_list_scheduled_gain_mixing_kernel(
                 if order[k][1] == g:
                     product(k)
 
-        def quantize_h(g, first_pass, passes):
-            width = GROUPS[g][1]
-            start, stop = first_pass * width, (first_pass + passes) * width
+        def quantize_h(g, start, stop):
             nc.vector.quantize_mx(
                 out=h_codes[g][:, start:stop].bitcast(FP8X4),
                 scales=h_scales[g][:, start:stop],
                 in_=h[g][:, PACK * start : PACK * stop],
             )
 
+        def mix_pass(total, g, n, b, first, last, start, stop):
+            width = GROUPS[g][1]
+            cols = slice(b * N + n * P, b * N + (n + 1) * P)
+            nc.tensor.matmul_mx(
+                out=total[:, first:last],
+                lhsT=wm_codes[:, cols].bitcast(FP8X4),
+                lhsT_scale=wm_scales[:, cols],
+                rhs=h_codes[g][:, b * width + first : b * width + last].bitcast(FP8X4),
+                rhs_scale=h_scales[g][:, b * width + first : b * width + last],
+                start=start,
+                stop=stop,
+            )
+
         def mix(g):
             first, width = GROUPS[g]
             result = held("result%d" % g, [P, N_TILES, width], F32)
-            tag, bufs = ("first", 5) if g == len(GROUPS) - 2 else ("mix", 3)
-            sums = [psum.tile([P, width], F32, name="mix", tag=tag, bufs=bufs) for n in range(N_TILES)]
-            steps = [(n, b) for n in range(N_TILES) for b in range(PASSES)]
-            if g >= len(GROUPS) - 2:
-                steps = sorted(steps, key=lambda step: step[1])
-            for n, b in steps:
-                cols = slice(b * N + n * P, b * N + (n + 1) * P)
-                nc.tensor.matmul_mx(
-                    out=sums[n][:],
-                    lhsT=wm_codes[:, cols].bitcast(FP8X4),
-                    lhsT_scale=wm_scales[:, cols],
-                    rhs=h_codes[g][:, b * width : (b + 1) * width].bitcast(FP8X4),
-                    rhs_scale=h_scales[g][:, b * width : (b + 1) * width],
-                    start=(b == 0),
-                    stop=(b == PASSES - 1),
-                )
+            sums = [psum.tile([P, width], F32, name="mix", tag="mix", bufs=3) for n in range(N_TILES)]
             for n in range(N_TILES):
-                trim_column = trims[:, n : n + 1]
-                if g >= len(GROUPS) - 2 and (g + n) % 2 == 1:
-                    nc.vector.tensor_scalar(result[:, n, :], sums[n][:], trim_column, None, ALU.add)
-                else:
-                    nc.scalar.activation(result[:, n, :], sums[n][:], ACT.Identity, bias=trim_column)
+                for b in range(PASSES):
+                    mix_pass(sums[n], g, n, b, 0, width, b == 0, b == PASSES - 1)
+            for n in range(N_TILES):
+                nc.scalar.activation(result[:, n, :], sums[n][:], ACT.Identity, bias=trims[:, n : n + 1])
             nc.sync.dma_start(out[:, first : first + width].rearrange("(n p) j -> p n j", p=P), result[:])
 
-        reorder_columns(wr_codes, wr_raw, 4)
+        def mix_last(g):
+            first, width = GROUPS[g]
+            sums = [psum.tile([P, width], F32, name="mix", tag="first", bufs=5) for n in range(N_TILES)]
+            for n in range(N_TILES):
+                mix_pass(sums[n], g, n, 0, 0, width, True, False)
+            for j0 in range(0, width, UNIT):
+                for n in range(N_TILES):
+                    mix_pass(sums[n], g, n, 1, j0, j0 + UNIT, False, j0 + UNIT == width)
+            for n in range(N_TILES):
+                result = held("last_result%d" % n, [P, width], F32)
+                if n % 2 == 0:
+                    nc.vector.tensor_scalar(result[:], sums[n][:], trims[:, n : n + 1], None, ALU.add)
+                else:
+                    nc.scalar.activation(result[:], sums[n][:], ACT.Identity, bias=trims[:, n : n + 1])
+                nc.sync.dma_start(out[n * P : (n + 1) * P, first : first + width], result[:])
+
+        reorder_columns(nc.gpsimd, wr_codes, wr_raw, 4)
+        reorder_wg(0)
         for i in range(2):
             gather_scales(i)
-        gather_words(demand_words[1], lists[1][:])
-        reorder_columns(wr_planes, wr_raw_scales, 2)
-        gather_words(demand_words[0], lists[0][:])
+        for c in range(CHUNKS):
+            gather_words(
+                demand_words[1][:, c * CHUNK : (c + 1) * CHUNK], lists[1][:, c * CHUNK // 16 : (c + 1) * CHUNK // 16]
+            )
+        reorder_columns(nc.gpsimd, wr_planes, wr_raw_scales, 2)
+        reorder_wg(1)
+        gather_words(demand_words[0][:], lists[0][:])
         round_ws(0)
         round_ws(1)
         quantize_ws(0)
         gather_gain_scales(0)
         quantize_ws(1)
-        reorder_columns(wg_planes, wg_raw_scales, 2)
-        reorder_columns(wg_codes, wg_raw, 8)
+        reorder_columns(nc.vector, wg_planes, wg_raw_scales, 2)
         gather_gain_scales(1)
-        gather_words(gain_words, lists[2][:])
+        gather_words(gain_words[:], lists[2][:])
         rows_turned = psum.tile([P, PASSES, P], F32, name="rows_turned", tag="mix", bufs=3)
         for b in range(PASSES):
             nc.tensor.transpose(rows_turned[:, b, :], rows[:, b * P : (b + 1) * P], identity[:])
@@ -343,27 +364,24 @@ def tile_list_scheduled_gain_mixing_kernel(
         for k in range(AHEAD):
             queue_gain()
         for k in range(len(places)):
-            if k % 2 == 0 and PACK + 1 + k // 2 < TILES:
-                demand(PACK + 1 + k // 2, 1)
-                clamp(nc.gpsimd, PACK + 1 + k // 2, 1)
+            if PACK + 1 + k < TILES:
+                demand(PACK + 1 + k, 1)
+                clamp(nc.gpsimd, PACK + 1 + k, 1)
             product(k)
         round_wm(0)
         round_wm(1)
         units(0)
         units(1)
-        quantize_h(0, 0, PASSES)
-        quantize_h(1, 0, PASSES)
+        quantize_h(0, 0, 512)
         quantize_wm()
+        quantize_h(1, 0, 512)
         mix(0)
         mix(1)
         units(2)
-        quantize_h(3, 0, 1)
-        quantize_h(4, 0, 1)
-        quantize_h(2, 0, PASSES)
+        quantize_h(3, 0, 256)
+        quantize_h(2, 0, 512)
         mix(2)
         units(3)
-        units(4)
-        quantize_h(3, 1, 1)
-        quantize_h(4, 1, 1)
-        mix(3)
-        mix(4)
+        quantize_h(3, 256, 384)
+        quantize_h(3, 384, 512)
+        mix_last(3)

@@ -51,13 +51,13 @@ def tile_list_scheduled_gain_mixing_kernel(
         lists = [held("list%d" % i, [P, S // 16], U16) for i in range(3)]
         table_words = held("table_words", [P, T], I32)
         table_scales = held("table_scales", [P, T // 4], I32)
-        wr_raw_scales = reused("wr_raw_scales", [P, H // 4], I32, 98304)
-        wg_raw_scales = reused("wg_raw_scales", [P, H // 4], I32, 90112)
+        wr_raw_scales = held("wr_raw_scales", [P, H // 4], I32)
+        wg_raw_scales = held("wg_raw_scales", [P, H // 4], I32)
         wr_raw = held("wr_raw", [P, H // 2], I32)
-        wg_raw = held("wg_raw", [P, H], I32)
+        wg_raw = [held("wg_raw%d" % b, [P, HALF], I32) for b in range(PASSES)]
         ws_raw = [reused("ws_raw%d" % b, [P, PACK, HALF], F32, 12288 * b) for b in range(PASSES)]
         wm_raw = [held("wm_raw%d" % b, [P, PACK, N], F32) for b in range(PASSES)]
-        rows = reused("rows", [P, PASSES * P], F32, 20480)
+        rows = held("rows", [P, PASSES * P], F32)
         identity = held("identity", [P, P], F32)
 
         nc.gpsimd.memset(table_scales[:], 0)
@@ -73,6 +73,10 @@ def tile_list_scheduled_gain_mixing_kernel(
         def load_ws(b):
             nc.sync.dma_start(ws_raw[b][:], ws[:, b * HALF : (b + 1) * HALF].rearrange("(p j) c -> p j c", j=PACK))
 
+        def load_wg(b):
+            words = wg_words[0, :, b * HALF : (b + 1) * HALF, :]
+            nc.sync.dma_start(wg_raw[b][:], words.rearrange("p n t -> p (n t)").bitcast(I32))
+
         def load_limits(first, vector):
             nc.sync.dma_start(
                 rows[first : first + PACK, :].rearrange("t (q i) -> t q i", i=8),
@@ -84,14 +88,15 @@ def tile_list_scheduled_gain_mixing_kernel(
         nc.sync.dma_start(lists[1][:], offs2)
         load_scale_rows(table_scales, tab_scales)
         nc.sync.dma_start(wr_raw[:], wr_words[0].bitcast(I32))
-        nc.sync.dma_start(wg_raw[:], wg_words[0].rearrange("p n t -> p (n t)").bitcast(I32))
         nc.sync.dma_start(table_words[:], tab_words[0].rearrange("p n t -> p (n t)").bitcast(I32))
-        load_scale_rows(wr_raw_scales, wr_scales)
-        load_ws(0)
         load_limits(LO, lo)
         load_limits(HI, hi)
+        load_scale_rows(wr_raw_scales, wr_scales)
+        load_ws(0)
+        load_wg(0)
         load_ws(1)
         nc.sync.dma_start(lists[2][:], offs3)
+        load_wg(1)
         load_scale_rows(wg_raw_scales, wg_scales)
         for b in range(PASSES):
             wm_rows = wm[b * HALF : (b + 1) * HALF, :].rearrange("(q t i) n -> t q i n", t=PACK, i=8)
@@ -101,13 +106,13 @@ def tile_list_scheduled_gain_mixing_kernel(
         with nc.allow_non_contiguous_dma(reason="one trim value for each partition and output tile"):
             nc.sync.dma_start(trims[:], trim.rearrange("(n p) -> p n", p=P))
 
-        columns = reused("columns", [P, PASSES, ROWS], F32, 16448)
+        columns = held("columns", [P, PASSES, ROWS], F32)
 
-        ws_grouped = [reused("ws_grouped%d" % b, [P, PACK, HALF], BF16, 81408 + 4608 * b) for b in range(PASSES)]
+        ws_grouped = [reused("ws_grouped%d" % b, [P, PACK, HALF], BF16, 81408 + 8704 * b) for b in range(PASSES)]
         demand_words = [reused("words0", [P, S], U32, 71680), held("words1", [P, S], U32)]
-        gain_words = reused("gain_words", [P, S], U32, 85504)
+        gain_words = reused("gain_words", [P, S], U32, 90112 + 256 - 4096)
         picked_scales = [held("scales%d" % i, [P, S], U8) for i in range(2)]
-        gain_scales = [reused("scales2_0", [P, CHUNK], U8, 81920), reused("scales2_1", [P, CHUNK], U8, 85504 + 4096)]
+        gain_scales = [reused("scales2_0", [P, CHUNK], U8, 84992), reused("scales2_1", [P, CHUNK], U8, 90112 + 256)]
 
         def gather_scales(i):
             nc.vector.tensor_copy(picked_scales[i][:], table_scales[:].bitcast(U8).indirect(lists[i][:]))
@@ -125,16 +130,16 @@ def tile_list_scheduled_gain_mixing_kernel(
                 raw[:].rearrange("p (b q t e) -> p b t q e", b=PASSES, t=PACK, e=run),
             )
 
-        def reorder_wg(b):
-            nc.gpsimd.tensor_copy(
+        def reorder_wg(engine, b):
+            engine.tensor_copy(
                 wg_codes[b][:].rearrange("p (t q e) -> p t q e", t=PACK, e=8),
-                wg_raw[:, b * HALF : (b + 1) * HALF].rearrange("p (q t e) -> p t q e", t=PACK, e=8),
+                wg_raw[b][:].rearrange("p (q t e) -> p t q e", t=PACK, e=8),
             )
 
         wr_codes = held("wr_codes", [P, H // 2], I32)
         wr_planes = held("wr_planes", [P, H // 4], I32)
-        wg_codes = [held("wg_codes0", [P, HALF], I32), reused("wg_codes1", [P, HALF], I32, 98304)]
-        wg_planes = reused("wg_planes", [P, H // 4], I32, 16640)
+        wg_codes = [held("wg_codes0", [P, HALF], I32), reused("wg_codes1", [P, HALF], I32, 90112 + 1792)]
+        wg_planes = reused("wg_planes", [P, H // 4], I32, 90112 + 768)
         ws_codes = [held("ws_codes%d" % b, [P, HALF], U32) for b in range(PASSES)]
         ws_scales = held("ws_scales", [P, H], U8)
 
@@ -171,26 +176,27 @@ def tile_list_scheduled_gain_mixing_kernel(
                     in_=wm_grouped[:, PACK * first : PACK * last],
                 )
 
-        demand0 = [reused("demand0_%d" % c, [P, PACK, CHUNK], F32, 18432 + 8192 * c) for c in range(CHUNKS)]
-        demand1_vector = reused("demand1_vector", [P, SHARE, CHUNK], F32, 57344)
-        demand1_gpsimd = held("demand1_gpsimd", [P, PACK - SHARE, CHUNK], F32)
-        demand1_last = reused("demand1_last", [P, PACK, CHUNK], F32, 40960)
-        clamped0 = [reused("clamped0_0", [P, PACK, CHUNK], F32, 90112), held("clamped0_1", [P, PACK, CHUNK], F32)]
-        clamped1 = [held("clamped1_0", [P, PACK, CHUNK], F32), reused("clamped1_1", [P, PACK, CHUNK], F32, 57344)]
+        demand_early = reused("demand_early", [P, SHARE, S], F32, 18432)
+        demand_vector = reused("demand_vector", [P, PACK - SHARE, S], F32, 0)
+        demand_middle = held("demand_middle", [P, S], F32)
+        demand_late = reused("demand_late", [P, PACK - 1, S], F32, 40960)
+        clamped = [
+            reused("clamped0", [P, PACK, S], F32, 90112 + 3840),
+            reused("clamped1", [P, PACK, S], F32, 0),
+        ]
 
-        def demand_rows(u, c):
-            b, t = divmod(u, PACK)
-            if b == 0:
-                return demand0[c][:, t, :]
-            if c == 1:
-                return demand1_last[:, t, :]
-            return demand1_vector[:, t, :] if t < SHARE else demand1_gpsimd[:, t - SHARE, :]
+        def demand_rows(u):
+            if u < SHARE:
+                return demand_early[:, u, :]
+            if u < PACK:
+                return demand_vector[:, u - SHARE, :]
+            return demand_middle[:] if u == PACK else demand_late[:, u - PACK - 1, :]
 
-        def demand(u, c):
-            b, t = divmod(u, PACK)
+        open_sums = {}
+
+        def open_demand(u, c, tag, bufs):
             cols = slice(u * P, (u + 1) * P)
             picks = slice(c * CHUNK, (c + 1) * CHUNK)
-            tag, bufs = ("mix", 3) if c == 1 and t > 0 else ("first", 5)
             acc = psum.tile([P, CHUNK], F32, name="demand", tag=tag, bufs=bufs)
             nc.tensor.matmul_mx(
                 out=acc[:],
@@ -201,6 +207,13 @@ def tile_list_scheduled_gain_mixing_kernel(
                 start=True,
                 stop=False,
             )
+            open_sums[u, c] = acc
+
+        def close_demand(u, c):
+            b, t = divmod(u, PACK)
+            cols = slice(u * P, (u + 1) * P)
+            picks = slice(c * CHUNK, (c + 1) * CHUNK)
+            acc = open_sums[u, c]
             nc.tensor.matmul_mx(
                 out=acc[:],
                 lhsT=ws_codes[b][:, t * P : (t + 1) * P].bitcast(FP8X4),
@@ -210,13 +223,17 @@ def tile_list_scheduled_gain_mixing_kernel(
                 start=False,
                 stop=True,
             )
-            nc.scalar.copy(demand_rows(u, c), acc[:])
+            nc.scalar.copy(demand_rows(u)[:, picks], acc[:])
 
-        def clamp(engine, u, c):
+        def demand(u, c, tag, bufs):
+            open_demand(u, c, tag, bufs)
+            close_demand(u, c)
+
+        def clamp(engine, u, first, last):
             b, t = divmod(u, PACK)
             engine.tensor_scalar(
-                (clamped0, clamped1)[b][c][:, t, :],
-                demand_rows(u, c),
+                clamped[b][:, t, first:last],
+                demand_rows(u)[:, first:last],
                 columns[:, b, HI + t : HI + t + 1],
                 columns[:, b, LO + t : LO + t + 1],
                 ALU.min,
@@ -239,8 +256,7 @@ def tile_list_scheduled_gain_mixing_kernel(
             return gain
 
         def multiply(gain, h_tile, word, j0, b):
-            c, within = divmod(j0, CHUNK)
-            source = (clamped0, clamped1)[b][c][:, :, within : within + UNIT]
+            source = clamped[b][:, :, j0 : j0 + UNIT]
             nc.vector.tensor_tensor(
                 h_tile[:, PACK * word : PACK * (word + UNIT)].rearrange("p (h l t) -> p h t l", l=4, t=PACK),
                 source.rearrange("p t (h l) -> p h t l", l=4),
@@ -324,7 +340,6 @@ def tile_list_scheduled_gain_mixing_kernel(
                 nc.sync.dma_start(out[n * P : (n + 1) * P, first : first + width], result[:])
 
         reorder_columns(nc.gpsimd, wr_codes, wr_raw, 4)
-        reorder_wg(0)
         for i in range(2):
             gather_scales(i)
         for c in range(CHUNKS):
@@ -332,41 +347,41 @@ def tile_list_scheduled_gain_mixing_kernel(
                 demand_words[1][:, c * CHUNK : (c + 1) * CHUNK], lists[1][:, c * CHUNK // 16 : (c + 1) * CHUNK // 16]
             )
         reorder_columns(nc.gpsimd, wr_planes, wr_raw_scales, 2)
-        reorder_wg(1)
+        reorder_wg(nc.gpsimd, 0)
         gather_words(demand_words[0][:], lists[0][:])
         round_ws(0)
         round_ws(1)
         quantize_ws(0)
         gather_gain_scales(0)
         quantize_ws(1)
-        reorder_columns(nc.vector, wg_planes, wg_raw_scales, 2)
         gather_gain_scales(1)
         gather_words(gain_words[:], lists[2][:])
+        reorder_columns(nc.vector, wg_planes, wg_raw_scales, 2)
+        reorder_wg(nc.vector, 1)
         rows_turned = psum.tile([P, PASSES, P], F32, name="rows_turned", tag="mix", bufs=3)
         for b in range(PASSES):
             nc.tensor.transpose(rows_turned[:, b, :], rows[:, b * P : (b + 1) * P], identity[:])
         nc.scalar.copy(columns[:], rows_turned[:, :, 0:ROWS])
+        for c in range(CHUNKS):
+            for t in range(PACK):
+                early = 2 * t + c < 5
+                open_demand(t, c, "first" if early else "mix", 5 if early else 3)
         for t in range(PACK):
-            demand(t, 0)
-        for t in range(PACK):
-            clamp(nc.gpsimd, t, 0)
-        for t in range(PACK):
-            demand(t, 1)
-            clamp(nc.vector, t, 1)
-        for u in range(PACK, PACK + SHARE):
-            demand(u, 0)
-            clamp(nc.vector, u, 0)
-        demand(PACK, 1)
-        clamp(nc.gpsimd, PACK, 1)
-        for u in range(PACK + SHARE, TILES):
-            demand(u, 0)
-            clamp(nc.gpsimd, u, 0)
+            for c in range(CHUNKS):
+                close_demand(t, c)
+            clamp(nc.gpsimd if t < SHARE else nc.vector, t, 0, S)
+        for c in range(CHUNKS):
+            demand(PACK, c, "first", 5)
+        clamp(nc.vector, PACK, 0, S)
+        for u in range(PACK + 1, TILES):
+            demand(u, 0, "first", 5)
+            clamp(nc.gpsimd, u, 0, CHUNK)
         for k in range(AHEAD):
             queue_gain()
         for k in range(len(places)):
             if PACK + 1 + k < TILES:
-                demand(PACK + 1 + k, 1)
-                clamp(nc.gpsimd, PACK + 1 + k, 1)
+                demand(PACK + 1 + k, 1, "mix", 3)
+                clamp(nc.gpsimd, PACK + 1 + k, CHUNK, S)
             product(k)
         round_wm(0)
         round_wm(1)

@@ -65,10 +65,10 @@ def tile_list_scheduled_gain_mixing_kernel(
         nc.vector.memset(wr_raw_scales[:], 0)
         nc.vector.memset(wg_raw_scales[:], 0)
 
-        def load_scale_rows(plane, scales):
+        def load_scale_rows(plane, scales, queues):
             by_row = scales[0].rearrange("(q r) n -> r q n", r=4)
             for r in range(4):
-                nc.sync.dma_start(plane[r:P:32, :], by_row[r].bitcast(I32))
+                queues[r % len(queues)].dma_start(plane[r:P:32, :], by_row[r].bitcast(I32))
 
         def load_ws(b):
             nc.sync.dma_start(ws_raw[b][:], ws[:, b * HALF : (b + 1) * HALF].rearrange("(p j) c -> p j c", j=PACK))
@@ -86,18 +86,18 @@ def tile_list_scheduled_gain_mixing_kernel(
         make_identity(nc, identity[:])
         nc.sync.dma_start(lists[0][:], offs)
         nc.sync.dma_start(lists[1][:], offs2)
-        load_scale_rows(table_scales, tab_scales)
+        load_scale_rows(table_scales, tab_scales, (nc.sync, nc.scalar))
         nc.sync.dma_start(wr_raw[:], wr_words[0].bitcast(I32))
         nc.sync.dma_start(table_words[:], tab_words[0].rearrange("p n t -> p (n t)").bitcast(I32))
         load_limits(LO, lo)
         load_limits(HI, hi)
-        load_scale_rows(wr_raw_scales, wr_scales)
+        load_scale_rows(wr_raw_scales, wr_scales, (nc.sync,))
         load_ws(0)
         load_wg(0)
         load_ws(1)
         nc.sync.dma_start(lists[2][:], offs3)
         load_wg(1)
-        load_scale_rows(wg_raw_scales, wg_scales)
+        load_scale_rows(wg_raw_scales, wg_scales, (nc.sync,))
         for b in range(PASSES):
             wm_rows = wm[b * HALF : (b + 1) * HALF, :].rearrange("(q t i) n -> t q i n", t=PACK, i=8)
             for t in range(PACK):
@@ -177,12 +177,12 @@ def tile_list_scheduled_gain_mixing_kernel(
                 )
 
         demand_early = reused("demand_early", [P, SHARE, S], F32, 18432)
-        demand_vector = reused("demand_vector", [P, PACK - SHARE, S], F32, 0)
+        demand_vector = reused("demand_vector", [P, PACK - SHARE, S], F32, 10240)
         demand_middle = held("demand_middle", [P, S], F32)
         demand_late = reused("demand_late", [P, PACK - 1, S], F32, 40960)
         clamped = [
             reused("clamped0", [P, PACK, S], F32, 90112 + 3840),
-            reused("clamped1", [P, PACK, S], F32, 0),
+            reused("clamped1", [P, PACK, S], F32, 2048),
         ]
 
         def demand_rows(u):

@@ -21,16 +21,21 @@ P = 128
 PACK = 4
 HALF = 512
 PASSES = H // HALF
-TILES = H // P
 CHUNK = 512
 CHUNKS = S // CHUNK
 UNIT = 128
+GROUP = 256
+GROUPS = S // GROUP
 N_TILES = N // P
-GROUPS = ((0, 256), (256, 256), (512, 256), (768, 256))
 LO, HI = 0, PACK
-ROWS = 8
+EARLY = 2
 AHEAD = 3
-SHARE = 2
+MAIN_BANKS, SIDE_BANKS = ("main", 5), ("side", 3)
+
+RAW_WS = (0, 12288)
+LATE_DEMAND = 40960
+STATE_WORDS = 71680
+ROUNDED_WS = (81408, 90112)
 
 
 def tile_list_scheduled_gain_mixing_kernel(
@@ -45,8 +50,11 @@ def tile_list_scheduled_gain_mixing_kernel(
         def held(name, shape, dtype):
             return keep.tile(shape, dtype, name=name, align_bytes=64)
 
-        def reused(name, shape, dtype, offset):
+        def placed(name, shape, dtype, offset):
             return shared.tile(shape, dtype, name=name, align_bytes=64, offset=offset)
+
+        def bank(name, shape, ring):
+            return psum.tile(shape, F32, name=name, tag=ring[0], bufs=ring[1])
 
         lists = [held("list%d" % i, [P, S // 16], U16) for i in range(3)]
         table_words = held("table_words", [P, T], I32)
@@ -55,20 +63,20 @@ def tile_list_scheduled_gain_mixing_kernel(
         wg_raw_scales = held("wg_raw_scales", [P, H // 4], I32)
         wr_raw = held("wr_raw", [P, H // 2], I32)
         wg_raw = [held("wg_raw%d" % b, [P, HALF], I32) for b in range(PASSES)]
-        ws_raw = [reused("ws_raw%d" % b, [P, PACK, HALF], F32, 12288 * b) for b in range(PASSES)]
+        ws_raw = [placed("ws_raw%d" % b, [P, PACK, HALF], F32, RAW_WS[b]) for b in range(PASSES)]
         wm_raw = [held("wm_raw%d" % b, [P, PACK, N], F32) for b in range(PASSES)]
-        rows = held("rows", [P, PASSES * P], F32)
+        limit_rows = held("limit_rows", [P, PASSES * P], F32)
         identity = held("identity", [P, P], F32)
 
         nc.gpsimd.memset(table_scales[:], 0)
-        nc.gpsimd.memset(rows[:], 0.0)
+        nc.gpsimd.memset(limit_rows[:], 0.0)
         nc.vector.memset(wr_raw_scales[:], 0)
         nc.vector.memset(wg_raw_scales[:], 0)
 
-        def load_scale_rows(plane, scales, queues):
+        def load_scale_rows(scale_tile, scales, queues):
             by_row = scales[0].rearrange("(q r) n -> r q n", r=4)
             for r in range(4):
-                queues[r % len(queues)].dma_start(plane[r:P:32, :], by_row[r].bitcast(I32))
+                queues[r % len(queues)].dma_start(scale_tile[r:P:32, :], by_row[r].bitcast(I32))
 
         def load_ws(b):
             nc.sync.dma_start(ws_raw[b][:], ws[:, b * HALF : (b + 1) * HALF].rearrange("(p j) c -> p j c", j=PACK))
@@ -79,7 +87,7 @@ def tile_list_scheduled_gain_mixing_kernel(
 
         def load_limits(first, vector):
             nc.sync.dma_start(
-                rows[first : first + PACK, :].rearrange("t (q i) -> t q i", i=8),
+                limit_rows[first : first + PACK, :].rearrange("t (q i) -> t q i", i=8),
                 vector.rearrange("(q t i) -> t q i", t=PACK, i=8),
             )
 
@@ -106,40 +114,46 @@ def tile_list_scheduled_gain_mixing_kernel(
         with nc.allow_non_contiguous_dma(reason="one trim value for each partition and output tile"):
             nc.sync.dma_start(trims[:], trim.rearrange("(n p) -> p n", p=P))
 
-        columns = held("columns", [P, PASSES, ROWS], F32)
+        limits = held("limits", [P, PASSES, 2 * PACK], F32)
 
-        ws_grouped = [reused("ws_grouped%d" % b, [P, PACK, HALF], BF16, 81408 + 8704 * b) for b in range(PASSES)]
-        demand_words = [reused("words0", [P, S], U32, 71680), held("words1", [P, S], U32)]
-        gain_words = reused("gain_words", [P, S], U32, 90112 + 256 - 4096)
-        picked_scales = [held("scales%d" % i, [P, S], U8) for i in range(2)]
-        gain_scales = [reused("scales2_0", [P, CHUNK], U8, 84992), reused("scales2_1", [P, CHUNK], U8, 90112 + 256)]
+        overhang = 256
+        after_ws1 = ROUNDED_WS[1] + overhang
+        ws_rounded = [placed("ws_rounded%d" % b, [P, PACK, HALF], BF16, ROUNDED_WS[b]) for b in range(PASSES)]
+        state_words = placed("state_words", [P, S], U32, STATE_WORDS)
+        reference_words = held("reference_words", [P, S], U32)
+        gain_words = placed("gain_words", [P, S], U32, after_ws1 - 4 * S)
+        state_scales = held("state_scales", [P, S], U8)
+        reference_scales = held("reference_scales", [P, S], U8)
+        gain_scales = [
+            placed("gain_scales0", [P, CHUNK], U8, ROUNDED_WS[0] + 2 * PACK * HALF - CHUNK),
+            placed("gain_scales1", [P, CHUNK], U8, after_ws1),
+        ]
 
-        def gather_scales(i):
-            nc.vector.tensor_copy(picked_scales[i][:], table_scales[:].bitcast(U8).indirect(lists[i][:]))
+        def chunk_of(entries, c):
+            return entries[:, c * CHUNK // 16 : (c + 1) * CHUNK // 16]
 
-        def gather_gain_scales(c):
-            offsets = lists[2][:, c * CHUNK // 16 : (c + 1) * CHUNK // 16]
-            nc.vector.tensor_copy(gain_scales[c][:], table_scales[:].bitcast(U8).indirect(offsets))
+        def gather_scales(picked, offsets):
+            nc.vector.tensor_copy(picked, table_scales[:].bitcast(U8).indirect(offsets))
 
         def gather_words(picked, offsets):
             nc.vector.tensor_copy(picked, table_words[:].bitcast(U32).indirect(offsets))
 
-        def reorder_columns(engine, moved, raw, run):
+        def regroup(engine, moved, raw, run):
             engine.tensor_copy(
                 moved[:].rearrange("p (b t q e) -> p b t q e", b=PASSES, t=PACK, e=run),
                 raw[:].rearrange("p (b q t e) -> p b t q e", b=PASSES, t=PACK, e=run),
             )
 
-        def reorder_wg(engine, b):
+        def regroup_wg(engine, b):
             engine.tensor_copy(
                 wg_codes[b][:].rearrange("p (t q e) -> p t q e", t=PACK, e=8),
                 wg_raw[b][:].rearrange("p (q t e) -> p t q e", t=PACK, e=8),
             )
 
         wr_codes = held("wr_codes", [P, H // 2], I32)
-        wr_planes = held("wr_planes", [P, H // 4], I32)
-        wg_codes = [held("wg_codes0", [P, HALF], I32), reused("wg_codes1", [P, HALF], I32, 90112 + 1792)]
-        wg_planes = reused("wg_planes", [P, H // 4], I32, 90112 + 768)
+        wr_scale_tile = held("wr_scale_tile", [P, H // 4], I32)
+        wg_codes = [held("wg_codes0", [P, HALF], I32), placed("wg_codes1", [P, HALF], I32, after_ws1 + CHUNK + H)]
+        wg_scale_tile = placed("wg_scale_tile", [P, H // 4], I32, after_ws1 + CHUNK)
         ws_codes = [held("ws_codes%d" % b, [P, HALF], U32) for b in range(PASSES)]
         ws_scales = held("ws_scales", [P, H], U8)
 
@@ -147,256 +161,252 @@ def tile_list_scheduled_gain_mixing_kernel(
             source = ws_raw[b][:].rearrange("p j (q t h l) -> p t q h j l", t=PACK, h=2, l=4)
             for t in range(PACK):
                 nc.scalar.copy(
-                    ws_grouped[b][:, t, :].rearrange("p (q h l j) -> p q h j l", h=2, l=4, j=PACK), source[:, t]
+                    ws_rounded[b][:, t, :].rearrange("p (q h l j) -> p q h j l", h=2, l=4, j=PACK), source[:, t]
                 )
 
         def quantize_ws(b):
-            cols = slice(b * HALF, (b + 1) * HALF)
             nc.vector.quantize_mx(
                 out=ws_codes[b][:].bitcast(FP8X4),
-                scales=ws_scales[:, cols],
-                in_=ws_grouped[b][:].rearrange("p t c -> p (t c)"),
+                scales=ws_scales[:, b * HALF : (b + 1) * HALF],
+                in_=ws_rounded[b][:].rearrange("p t c -> p (t c)"),
             )
 
-        wm_codes = reused("wm_codes", [P, PASSES * N], U32, 38912)
+        wm_codes = placed("wm_codes", [P, PASSES * N], U32, LATE_DEMAND - 2048)
         wm_scales = held("wm_scales", [P, PASSES * N], U8)
-        wm_grouped = reused("wm_grouped", [P, PASSES * N * PACK], BF16, 71680)
+        wm_rounded = placed("wm_rounded", [P, PASSES * N * PACK], BF16, STATE_WORDS)
 
         def round_wm(b):
             nc.scalar.copy(
-                wm_grouped[:, b * N * PACK : (b + 1) * N * PACK].rearrange("p (h l t) -> p h t l", l=4, t=PACK),
+                wm_rounded[:, b * N * PACK : (b + 1) * N * PACK].rearrange("p (h l t) -> p h t l", l=4, t=PACK),
                 wm_raw[b][:].rearrange("p t (h l) -> p h t l", l=4),
             )
 
         def quantize_wm():
-            for first, last in ((0, 512), (512, 768)):
+            for first, last in ((0, 512), (512, PASSES * N)):
                 nc.vector.quantize_mx(
                     out=wm_codes[:, first:last].bitcast(FP8X4),
                     scales=wm_scales[:, first:last],
-                    in_=wm_grouped[:, PACK * first : PACK * last],
+                    in_=wm_rounded[:, PACK * first : PACK * last],
                 )
 
-        demand_early = reused("demand_early", [P, SHARE, S], F32, 18432)
-        demand_vector = reused("demand_vector", [P, PACK - SHARE, S], F32, 10240)
+        split = RAW_WS[1] + 6144
+        demand_early = placed("demand_early", [P, EARLY, S], F32, split)
+        demand_vector = placed("demand_vector", [P, PACK - EARLY, S], F32, split - 4 * S * (PACK - EARLY))
         demand_middle = held("demand_middle", [P, S], F32)
-        demand_late = reused("demand_late", [P, PACK - 1, S], F32, 40960)
+        demand_late = placed("demand_late", [P, PACK - 1, S], F32, LATE_DEMAND)
         clamped = [
-            reused("clamped0", [P, PACK, S], F32, 90112 + 3840),
-            reused("clamped1", [P, PACK, S], F32, 2048),
+            placed("clamped0", [P, CHUNKS, PACK, CHUNK], F32, after_ws1 + CHUNK + H + 4 * HALF),
+            placed("clamped1", [P, CHUNKS, PACK, CHUNK], F32, split - 4 * S * PACK),
         ]
 
         def demand_rows(u):
-            if u < SHARE:
+            if u < EARLY:
                 return demand_early[:, u, :]
             if u < PACK:
-                return demand_vector[:, u - SHARE, :]
+                return demand_vector[:, u - EARLY, :]
             return demand_middle[:] if u == PACK else demand_late[:, u - PACK - 1, :]
 
         open_sums = {}
 
-        def open_demand(u, c, tag, bufs):
-            cols = slice(u * P, (u + 1) * P)
+        def open_demand(u, c, ring):
             picks = slice(c * CHUNK, (c + 1) * CHUNK)
-            acc = psum.tile([P, CHUNK], F32, name="demand", tag=tag, bufs=bufs)
+            total = bank("demand", [P, CHUNK], ring)
             nc.tensor.matmul_mx(
-                out=acc[:],
+                out=total[:],
                 lhsT=wr_codes[:].bitcast(U8)[:, 2 * u * P : 2 * (u + 1) * P].bitcast(FP4X4),
-                lhsT_scale=wr_planes[:].bitcast(U8)[:, cols],
-                rhs=demand_words[1][:, picks].bitcast(FP8X4),
-                rhs_scale=picked_scales[1][:, picks],
+                lhsT_scale=wr_scale_tile[:].bitcast(U8)[:, u * P : (u + 1) * P],
+                rhs=reference_words[:, picks].bitcast(FP8X4),
+                rhs_scale=reference_scales[:, picks],
                 start=True,
                 stop=False,
             )
-            open_sums[u, c] = acc
+            open_sums[u, c] = total
 
         def close_demand(u, c):
             b, t = divmod(u, PACK)
-            cols = slice(u * P, (u + 1) * P)
             picks = slice(c * CHUNK, (c + 1) * CHUNK)
-            acc = open_sums[u, c]
+            total = open_sums[u, c]
             nc.tensor.matmul_mx(
-                out=acc[:],
+                out=total[:],
                 lhsT=ws_codes[b][:, t * P : (t + 1) * P].bitcast(FP8X4),
-                lhsT_scale=ws_scales[:, cols],
-                rhs=demand_words[0][:, picks].bitcast(FP8X4),
-                rhs_scale=picked_scales[0][:, picks],
+                lhsT_scale=ws_scales[:, u * P : (u + 1) * P],
+                rhs=state_words[:, picks].bitcast(FP8X4),
+                rhs_scale=state_scales[:, picks],
                 start=False,
                 stop=True,
             )
-            nc.scalar.copy(demand_rows(u)[:, picks], acc[:])
+            nc.scalar.copy(demand_rows(u)[:, picks], total[:])
 
-        def demand(u, c, tag, bufs):
-            open_demand(u, c, tag, bufs)
+        def demand(u, c, ring):
+            open_demand(u, c, ring)
             close_demand(u, c)
 
-        def clamp(engine, u, first, last):
+        def clamp(engine, u, first_chunk, chunks):
             b, t = divmod(u, PACK)
+            rows = demand_rows(u)[:, first_chunk * CHUNK : (first_chunk + chunks) * CHUNK]
             engine.tensor_scalar(
-                clamped[b][:, t, first:last],
-                demand_rows(u)[:, first:last],
-                columns[:, b, HI + t : HI + t + 1],
-                columns[:, b, LO + t : LO + t + 1],
+                clamped[b][:, first_chunk : first_chunk + chunks, t, :],
+                rows.rearrange("p (c j) -> p c j", j=CHUNK),
+                limits[:, b, HI + t : HI + t + 1],
+                limits[:, b, LO + t : LO + t + 1],
                 ALU.min,
                 ALU.max,
             )
 
-        def gain_unit(j0, b):
-            gain = psum.tile([P, PACK, UNIT], F32, name="gain", tag="first", bufs=5)
-            for t in range(PACK):
-                cols = slice((PACK * b + t) * P, (PACK * b + t + 1) * P)
-                nc.tensor.matmul_mx(
-                    out=gain[:, t, :],
-                    lhsT=wg_codes[b][:, t * P : (t + 1) * P].bitcast(FP8X4),
-                    lhsT_scale=wg_planes[:].bitcast(U8)[:, cols],
-                    rhs=gain_words[:, j0 : j0 + UNIT].bitcast(FP8X4),
-                    rhs_scale=gain_scales[j0 // CHUNK][:, j0 % CHUNK : j0 % CHUNK + UNIT],
-                    start=True,
-                    stop=True,
-                )
-            return gain
-
-        def multiply(gain, h_tile, word, j0, b):
-            source = clamped[b][:, :, j0 : j0 + UNIT]
-            nc.vector.tensor_tensor(
-                h_tile[:, PACK * word : PACK * (word + UNIT)].rearrange("p (h l t) -> p h t l", l=4, t=PACK),
-                source.rearrange("p t (h l) -> p h t l", l=4),
-                gain[:].rearrange("p t (h l) -> p h t l", l=4),
-                ALU.mult,
-            )
-
-        h = [held("h%d" % g, [P, PASSES * PACK * width], BF16) for g, (first, width) in enumerate(GROUPS)]
-        h_offsets = (41984, 44032, 53248, 46080)
+        h = [held("h%d" % g, [P, PASSES * PACK * GROUP], BF16) for g in range(GROUPS)]
         h_codes = [
-            reused("h_codes%d" % g, [P, PASSES * width], U32, h_offsets[g]) for g, (first, width) in enumerate(GROUPS)
+            placed("h_codes%d" % g, [P, PASSES * GROUP], U32, LATE_DEMAND + 1024 + 4 * PASSES * GROUP * g)
+            for g in range(GROUPS)
         ]
-        h_scales = [held("h_scales%d" % g, [P, PASSES * width], U8) for g, (first, width) in enumerate(GROUPS)]
+        h_scales = [held("h_scales%d" % g, [P, PASSES * GROUP], U8) for g in range(GROUPS)]
 
-        places = [(g, j0) for g, (first, width) in enumerate(GROUPS) for j0 in range(first, first + width, UNIT)]
-        middle = CHUNK // UNIT
-        order = [(0, g, j0) for g, j0 in places[middle:] + places[:middle]] + [(1, g, j0) for g, j0 in places]
+        starts = list(range(0, S, UNIT))
+        order = [(0, j0) for j0 in starts[CHUNK // UNIT :] + starts[: CHUNK // UNIT]] + [(1, j0) for j0 in starts]
         gains = []
 
         def queue_gain():
             if len(gains) < len(order):
-                b, g, j0 = order[len(gains)]
-                gains.append(gain_unit(j0, b))
+                b, j0 = order[len(gains)]
+                c, within = divmod(j0, CHUNK)
+                gain = bank("gain", [P, PACK, UNIT], MAIN_BANKS)
+                for t in range(PACK):
+                    u = PACK * b + t
+                    nc.tensor.matmul_mx(
+                        out=gain[:, t, :],
+                        lhsT=wg_codes[b][:, t * P : (t + 1) * P].bitcast(FP8X4),
+                        lhsT_scale=wg_scale_tile[:].bitcast(U8)[:, u * P : (u + 1) * P],
+                        rhs=gain_words[:, j0 : j0 + UNIT].bitcast(FP8X4),
+                        rhs_scale=gain_scales[c][:, within : within + UNIT],
+                        start=True,
+                        stop=True,
+                    )
+                gains.append(gain)
 
         def product(k):
-            b, g, j0 = order[k]
-            first, width = GROUPS[g]
-            multiply(gains[k], h[g], b * width + j0 - first, j0, b)
+            b, j0 = order[k]
+            c, within = divmod(j0, CHUNK)
+            g, word = j0 // GROUP, b * GROUP + j0 % GROUP
+            nc.vector.tensor_tensor(
+                h[g][:, PACK * word : PACK * (word + UNIT)].rearrange("p (h l t) -> p h t l", l=4, t=PACK),
+                clamped[b][:, c, :, within : within + UNIT].rearrange("p t (h l) -> p h t l", l=4),
+                gains[k][:].rearrange("p t (h l) -> p h t l", l=4),
+                ALU.mult,
+            )
             queue_gain()
 
-        def units(g):
-            for k in range(len(places), len(order)):
-                if order[k][1] == g:
-                    product(k)
+        def finish_group(g):
+            for j0 in range(g * GROUP, (g + 1) * GROUP, UNIT):
+                product(order.index((1, j0)))
 
-        def quantize_h(g, start, stop):
+        def quantize_h(g, first, last):
             nc.vector.quantize_mx(
-                out=h_codes[g][:, start:stop].bitcast(FP8X4),
-                scales=h_scales[g][:, start:stop],
-                in_=h[g][:, PACK * start : PACK * stop],
+                out=h_codes[g][:, first:last].bitcast(FP8X4),
+                scales=h_scales[g][:, first:last],
+                in_=h[g][:, PACK * first : PACK * last],
             )
 
         def mix_pass(total, g, n, b, first, last, start, stop):
-            width = GROUPS[g][1]
             cols = slice(b * N + n * P, b * N + (n + 1) * P)
+            words = slice(b * GROUP + first, b * GROUP + last)
             nc.tensor.matmul_mx(
                 out=total[:, first:last],
                 lhsT=wm_codes[:, cols].bitcast(FP8X4),
                 lhsT_scale=wm_scales[:, cols],
-                rhs=h_codes[g][:, b * width + first : b * width + last].bitcast(FP8X4),
-                rhs_scale=h_scales[g][:, b * width + first : b * width + last],
+                rhs=h_codes[g][:, words].bitcast(FP8X4),
+                rhs_scale=h_scales[g][:, words],
                 start=start,
                 stop=stop,
             )
 
         def mix(g):
-            first, width = GROUPS[g]
-            result = held("result%d" % g, [P, N_TILES, width], F32)
-            sums = [psum.tile([P, width], F32, name="mix", tag="mix", bufs=3) for n in range(N_TILES)]
+            result = held("result%d" % g, [P, N_TILES, GROUP], F32)
+            sums = [bank("mix", [P, GROUP], SIDE_BANKS) for n in range(N_TILES)]
             for n in range(N_TILES):
                 for b in range(PASSES):
-                    mix_pass(sums[n], g, n, b, 0, width, b == 0, b == PASSES - 1)
+                    mix_pass(sums[n], g, n, b, 0, GROUP, b == 0, b == PASSES - 1)
             for n in range(N_TILES):
                 nc.scalar.activation(result[:, n, :], sums[n][:], ACT.Identity, bias=trims[:, n : n + 1])
-            nc.sync.dma_start(out[:, first : first + width].rearrange("(n p) j -> p n j", p=P), result[:])
+            nc.sync.dma_start(out[:, g * GROUP : (g + 1) * GROUP].rearrange("(n p) j -> p n j", p=P), result[:])
 
         def mix_last(g):
-            first, width = GROUPS[g]
-            sums = [psum.tile([P, width], F32, name="mix", tag="first", bufs=5) for n in range(N_TILES)]
+            sums = [bank("mix", [P, GROUP], MAIN_BANKS) for n in range(N_TILES)]
             for n in range(N_TILES):
-                mix_pass(sums[n], g, n, 0, 0, width, True, False)
-            for j0 in range(0, width, UNIT):
+                mix_pass(sums[n], g, n, 0, 0, GROUP, True, False)
+            for first in range(0, GROUP, UNIT):
                 for n in range(N_TILES):
-                    mix_pass(sums[n], g, n, 1, j0, j0 + UNIT, False, j0 + UNIT == width)
+                    mix_pass(sums[n], g, n, 1, first, first + UNIT, False, first + UNIT == GROUP)
             for n in range(N_TILES):
-                result = held("last_result%d" % n, [P, width], F32)
+                result = held("last_result%d" % n, [P, GROUP], F32)
                 if n % 2 == 0:
                     nc.vector.tensor_scalar(result[:], sums[n][:], trims[:, n : n + 1], None, ALU.add)
                 else:
                     nc.scalar.activation(result[:], sums[n][:], ACT.Identity, bias=trims[:, n : n + 1])
-                nc.sync.dma_start(out[n * P : (n + 1) * P, first : first + width], result[:])
+                nc.sync.dma_start(out[n * P : (n + 1) * P, g * GROUP : (g + 1) * GROUP], result[:])
 
-        reorder_columns(nc.gpsimd, wr_codes, wr_raw, 4)
-        for i in range(2):
-            gather_scales(i)
+        regroup(nc.gpsimd, wr_codes, wr_raw, 4)
+        gather_scales(state_scales[:], lists[0][:])
+        gather_scales(reference_scales[:], lists[1][:])
         for c in range(CHUNKS):
-            gather_words(
-                demand_words[1][:, c * CHUNK : (c + 1) * CHUNK], lists[1][:, c * CHUNK // 16 : (c + 1) * CHUNK // 16]
-            )
-        reorder_columns(nc.gpsimd, wr_planes, wr_raw_scales, 2)
-        reorder_wg(nc.gpsimd, 0)
-        gather_words(demand_words[0][:], lists[0][:])
+            gather_words(reference_words[:, c * CHUNK : (c + 1) * CHUNK], chunk_of(lists[1], c))
+        regroup(nc.gpsimd, wr_scale_tile, wr_raw_scales, 2)
+        regroup_wg(nc.gpsimd, 0)
+        gather_words(state_words[:], lists[0][:])
         round_ws(0)
         round_ws(1)
         quantize_ws(0)
-        gather_gain_scales(0)
+        gather_scales(gain_scales[0][:], chunk_of(lists[2], 0))
         quantize_ws(1)
-        gather_gain_scales(1)
+        gather_scales(gain_scales[1][:], chunk_of(lists[2], 1))
         gather_words(gain_words[:], lists[2][:])
-        reorder_columns(nc.vector, wg_planes, wg_raw_scales, 2)
-        reorder_wg(nc.vector, 1)
-        rows_turned = psum.tile([P, PASSES, P], F32, name="rows_turned", tag="mix", bufs=3)
+        regroup(nc.vector, wg_scale_tile, wg_raw_scales, 2)
+        regroup_wg(nc.vector, 1)
+
+        limits_turned = bank("limits_turned", [P, PASSES, P], SIDE_BANKS)
         for b in range(PASSES):
-            nc.tensor.transpose(rows_turned[:, b, :], rows[:, b * P : (b + 1) * P], identity[:])
-        nc.scalar.copy(columns[:], rows_turned[:, :, 0:ROWS])
+            nc.tensor.transpose(limits_turned[:, b, :], limit_rows[:, b * P : (b + 1) * P], identity[:])
+        nc.scalar.copy(limits[:], limits_turned[:, :, 0 : 2 * PACK])
+
         for c in range(CHUNKS):
             for t in range(PACK):
-                early = 2 * t + c < 5
-                open_demand(t, c, "first" if early else "mix", 5 if early else 3)
+                open_demand(t, c, MAIN_BANKS if CHUNKS * t + c < MAIN_BANKS[1] else SIDE_BANKS)
         for t in range(PACK):
             for c in range(CHUNKS):
                 close_demand(t, c)
-            clamp(nc.gpsimd if t < SHARE else nc.vector, t, 0, S)
+            clamp(nc.gpsimd if t < EARLY else nc.vector, t, 0, CHUNKS)
+
+        demand(PACK, 0, MAIN_BANKS)
+        clamp(nc.vector, PACK, 0, 1)
+        demand(PACK + 1, 0, MAIN_BANKS)
+        clamp(nc.gpsimd, PACK + 1, 0, 1)
         for c in range(CHUNKS):
-            demand(PACK, c, "first", 5)
-        clamp(nc.vector, PACK, 0, S)
-        for u in range(PACK + 1, TILES):
-            demand(u, 0, "first", 5)
-            clamp(nc.gpsimd, u, 0, CHUNK)
+            demand(PACK + 2, c, MAIN_BANKS)
+        clamp(nc.gpsimd, PACK + 2, 0, CHUNKS)
+        demand(PACK + 3, 0, MAIN_BANKS)
+        demand(PACK + 3, 1, SIDE_BANKS)
+        clamp(nc.gpsimd, PACK + 3, 0, CHUNKS)
         for k in range(AHEAD):
             queue_gain()
-        for k in range(len(places)):
-            if PACK + 1 + k < TILES:
-                demand(PACK + 1 + k, 1, "mix", 3)
-                clamp(nc.gpsimd, PACK + 1 + k, CHUNK, S)
+        second_chunks_left = (PACK, PACK + 1)
+        for k in range(len(starts)):
+            if k < len(second_chunks_left):
+                demand(second_chunks_left[k], 1, SIDE_BANKS)
+                clamp(nc.gpsimd, second_chunks_left[k], 1, 1)
             product(k)
+
         round_wm(0)
         round_wm(1)
-        units(0)
-        units(1)
-        quantize_h(0, 0, 512)
+        finish_group(0)
+        finish_group(1)
+        quantize_h(0, 0, PASSES * GROUP)
         quantize_wm()
-        quantize_h(1, 0, 512)
+        quantize_h(1, 0, PASSES * GROUP)
         mix(0)
         mix(1)
-        units(2)
-        quantize_h(3, 0, 256)
-        quantize_h(2, 0, 512)
+        finish_group(2)
+        quantize_h(3, 0, GROUP)
+        quantize_h(2, 0, PASSES * GROUP)
         mix(2)
-        units(3)
-        quantize_h(3, 256, 384)
-        quantize_h(3, 384, 512)
+        finish_group(3)
+        quantize_h(3, GROUP, GROUP + UNIT)
+        quantize_h(3, GROUP + UNIT, PASSES * GROUP)
         mix_last(3)

@@ -27,15 +27,11 @@ UNIT = 128
 GROUP = 256
 GROUPS = S // GROUP
 N_TILES = N // P
-LO, HI = 0, PACK
-EARLY = 2
-AHEAD = 3
-MAIN_BANKS, SIDE_BANKS = ("main", 5), ("side", 3)
+LO, HI = 0, 1
+DEMAND_BANKS, GAIN_BANKS = ("demand", 4), ("gain", 4)
 
-RAW_WS = (0, 12288)
-LATE_DEMAND = 40960
-STATE_WORDS = 71680
-ROUNDED_WS = (81408, 90112)
+ROUNDED_WS = (8192, 49152)
+LATE_DEMAND = 61440
 
 
 def tile_list_scheduled_gain_mixing_kernel(
@@ -61,11 +57,13 @@ def tile_list_scheduled_gain_mixing_kernel(
         table_scales = held("table_scales", [P, T // 4], I32)
         wr_raw_scales = held("wr_raw_scales", [P, H // 4], I32)
         wg_raw_scales = held("wg_raw_scales", [P, H // 4], I32)
-        wr_raw = held("wr_raw", [P, H // 2], I32)
-        wg_raw = [held("wg_raw%d" % b, [P, HALF], I32) for b in range(PASSES)]
-        ws_raw = [placed("ws_raw%d" % b, [P, PACK, HALF], F32, RAW_WS[b]) for b in range(PASSES)]
+        wr_raw = [held("wr_raw%d" % b, [P, HALF // 2], I32) for b in range(PASSES)]
+        wg_raw = held("wg_raw", [P, H], I32)
+        ws_pieces = [(0, 0, HALF // 2), (0, HALF // 2, HALF), (1, 0, HALF)]
+        ws_raw = [held("ws_raw%d" % i, [P, PACK, z - a], F32) for i, (b, a, z) in enumerate(ws_pieces)]
         wm_raw = [held("wm_raw%d" % b, [P, PACK, N], F32) for b in range(PASSES)]
-        limit_rows = held("limit_rows", [P, PASSES * P], F32)
+        limits_raw = held("limits_raw", [2, H], F32)
+        limit_rows = held("limit_rows", [P, H], F32)
         identity = held("identity", [P, P], F32)
 
         nc.gpsimd.memset(table_scales[:], 0)
@@ -78,33 +76,31 @@ def tile_list_scheduled_gain_mixing_kernel(
             for r in range(4):
                 queues[r % len(queues)].dma_start(scale_tile[r:P:32, :], by_row[r].bitcast(I32))
 
-        def load_ws(b):
-            nc.sync.dma_start(ws_raw[b][:], ws[:, b * HALF : (b + 1) * HALF].rearrange("(p j) c -> p j c", j=PACK))
+        def load_ws(i):
+            b, a, z = ws_pieces[i]
+            nc.sync.dma_start(ws_raw[i][:], ws[:, b * HALF + a : b * HALF + z].rearrange("(p j) c -> p j c", j=PACK))
 
-        def load_wg(b):
-            words = wg_words[0, :, b * HALF : (b + 1) * HALF, :]
-            nc.sync.dma_start(wg_raw[b][:], words.rearrange("p n t -> p (n t)").bitcast(I32))
+        def load_limits(row, vector):
+            nc.sync.dma_start(limits_raw[row : row + 1, :], vector.rearrange("(o r) -> o r", o=1))
 
-        def load_limits(first, vector):
-            nc.sync.dma_start(
-                limit_rows[first : first + PACK, :].rearrange("t (q i) -> t q i", i=8),
-                vector.rearrange("(q t i) -> t q i", t=PACK, i=8),
-            )
+        def load_wr(b):
+            nc.sync.dma_start(wr_raw[b][:], wr_words[0, :, b * 2 * HALF : (b + 1) * 2 * HALF].bitcast(I32))
 
         make_identity(nc, identity[:])
-        nc.sync.dma_start(lists[0][:], offs)
         nc.sync.dma_start(lists[1][:], offs2)
         load_scale_rows(table_scales, tab_scales, (nc.sync, nc.scalar))
-        nc.sync.dma_start(wr_raw[:], wr_words[0].bitcast(I32))
-        nc.sync.dma_start(table_words[:], tab_words[0].rearrange("p n t -> p (n t)").bitcast(I32))
         load_limits(LO, lo)
         load_limits(HI, hi)
-        load_scale_rows(wr_raw_scales, wr_scales, (nc.sync,))
+        nc.sync.dma_start(table_words[:], tab_words[0].rearrange("p n t -> p (n t)").bitcast(I32))
+        nc.sync.dma_start(lists[0][:], offs)
         load_ws(0)
-        load_wg(0)
+        load_wr(0)
+        load_scale_rows(wr_raw_scales, wr_scales, (nc.sync,))
+        load_wr(1)
         load_ws(1)
+        load_ws(2)
+        nc.sync.dma_start(wg_raw[:], wg_words[0].rearrange("p n t -> p (n t)").bitcast(I32))
         nc.sync.dma_start(lists[2][:], offs3)
-        load_wg(1)
         load_scale_rows(wg_raw_scales, wg_scales, (nc.sync,))
         for b in range(PASSES):
             wm_rows = wm[b * HALF : (b + 1) * HALF, :].rearrange("(q t i) n -> t q i n", t=PACK, i=8)
@@ -114,19 +110,24 @@ def tile_list_scheduled_gain_mixing_kernel(
         with nc.allow_non_contiguous_dma(reason="one trim value for each partition and output tile"):
             nc.sync.dma_start(trims[:], trim.rearrange("(n p) -> p n", p=P))
 
-        limits = held("limits", [P, PASSES, 2 * PACK], F32)
+        limits = held("limits", [P, PASSES, PACK, 2], F32)
 
-        overhang = 256
-        after_ws1 = ROUNDED_WS[1] + overhang
-        ws_rounded = [placed("ws_rounded%d" % b, [P, PACK, HALF], BF16, ROUNDED_WS[b]) for b in range(PASSES)]
-        state_words = placed("state_words", [P, S], U32, STATE_WORDS)
-        reference_words = held("reference_words", [P, S], U32)
-        gain_words = placed("gain_words", [P, S], U32, after_ws1 - 4 * S)
-        state_scales = held("state_scales", [P, S], U8)
+        r0, r1 = ROUNDED_WS
+        ws_rounded = [
+            [placed("ws_rounded%d_%d" % (b, v), [P, 2, HALF], BF16, ROUNDED_WS[b] + 2048 * v) for v in range(2)]
+            for b in range(PASSES)
+        ]
+        state_words = [held("state_words0", [P, CHUNK], U32), placed("state_words1", [P, CHUNK], U32, r0 + 3072)]
+        reference_words = [
+            held("reference_words0", [P, CHUNK], U32),
+            placed("reference_words1", [P, CHUNK], U32, r0 + 512),
+        ]
+        gain_words = [held("gain_words0", [P, CHUNK], U32), placed("gain_words1", [P, CHUNK], U32, r1 + 4096 - 64)]
+        state_scales = [held("state_scales0", [P, CHUNK], U8), placed("state_scales1", [P, CHUNK], U8, r0)]
         reference_scales = held("reference_scales", [P, S], U8)
         gain_scales = [
-            placed("gain_scales0", [P, CHUNK], U8, ROUNDED_WS[0] + 2 * PACK * HALF - CHUNK),
-            placed("gain_scales1", [P, CHUNK], U8, after_ws1),
+            held("gain_scales0", [P, CHUNK], U8),
+            placed("gain_scales1", [P, CHUNK], U8, r1 + 2048),
         ]
 
         def chunk_of(entries, c):
@@ -138,42 +139,45 @@ def tile_list_scheduled_gain_mixing_kernel(
         def gather_words(picked, offsets):
             nc.vector.tensor_copy(picked, table_words[:].bitcast(U32).indirect(offsets))
 
-        def regroup(engine, moved, raw, run):
-            engine.tensor_copy(
-                moved[:].rearrange("p (b t q e) -> p b t q e", b=PASSES, t=PACK, e=run),
-                raw[:].rearrange("p (b q t e) -> p b t q e", b=PASSES, t=PACK, e=run),
+        def regrouped(moved, raw, run, b):
+            words = slice(b * 64 * run, (b + 1) * 64 * run)
+            return (
+                moved.rearrange("p (t q e) -> p t q e", t=PACK, e=run),
+                raw[:, words].rearrange("p (q t e) -> p t q e", t=PACK, e=run),
             )
 
-        def regroup_wg(engine, b):
-            engine.tensor_copy(
-                wg_codes[b][:].rearrange("p (t q e) -> p t q e", t=PACK, e=8),
-                wg_raw[b][:].rearrange("p (q t e) -> p t q e", t=PACK, e=8),
-            )
-
-        wr_codes = held("wr_codes", [P, H // 2], I32)
-        wr_scale_tile = held("wr_scale_tile", [P, H // 4], I32)
-        wg_codes = [held("wg_codes0", [P, HALF], I32), placed("wg_codes1", [P, HALF], I32, after_ws1 + CHUNK + H)]
-        wg_scale_tile = placed("wg_scale_tile", [P, H // 4], I32, after_ws1 + CHUNK)
+        wr_codes = [held("wr_codes%d" % b, [P, HALF // 2], I32) for b in range(PASSES)]
+        wr_scale_tile = [held("wr_scale_tile%d" % b, [P, HALF // 4], I32) for b in range(PASSES)]
+        wg_codes = [held("wg_codes%d" % b, [P, HALF], I32) for b in range(PASSES)]
+        wg_scale_tile = [held("wg_scale_tile%d" % b, [P, HALF // 4], I32) for b in range(PASSES)]
         ws_codes = [held("ws_codes%d" % b, [P, HALF], U32) for b in range(PASSES)]
-        ws_scales = held("ws_scales", [P, H], U8)
+        ws_scales = [held("ws_scales%d" % b, [P, HALF], U8) for b in range(PASSES)]
 
-        def round_ws(b):
-            source = ws_raw[b][:].rearrange("p j (q t h l) -> p t q h j l", t=PACK, h=2, l=4)
-            for t in range(PACK):
-                nc.scalar.copy(
-                    ws_rounded[b][:, t, :].rearrange("p (q h l j) -> p q h j l", h=2, l=4, j=PACK), source[:, t]
-                )
+        def regroup_wr(move, b):
+            move(*regrouped(wr_codes[b][:].bitcast(U32), wr_raw[b][:].bitcast(U32), 4, 0))
+            move(*regrouped(wr_scale_tile[b][:].bitcast(U32), wr_raw_scales[:].bitcast(U32), 2, b))
 
-        def quantize_ws(b):
-            nc.vector.quantize_mx(
-                out=ws_codes[b][:].bitcast(FP8X4),
-                scales=ws_scales[:, b * HALF : (b + 1) * HALF],
-                in_=ws_rounded[b][:].rearrange("p t c -> p (t c)"),
+        def regroup_wg(b):
+            nc.scalar.copy(*regrouped(wg_codes[b][:].bitcast(U32), wg_raw[:].bitcast(U32), 8, b))
+            nc.scalar.copy(*regrouped(wg_scale_tile[b][:].bitcast(U32), wg_raw_scales[:].bitcast(U32), 2, b))
+
+        def round_ws(i, t):
+            b, a, z = ws_pieces[i]
+            source = ws_raw[i][:].rearrange("p j (q t h l) -> p t q h j l", t=PACK, h=2, l=4)
+            nc.scalar.copy(
+                ws_rounded[b][t // 2][:, t % 2, a:z].rearrange("p (q h l j) -> p q h j l", h=2, l=4, j=PACK), source[:, t]
             )
 
-        wm_codes = placed("wm_codes", [P, PASSES * N], U32, LATE_DEMAND - 2048)
+        def quantize_ws(b, v):
+            nc.vector.quantize_mx(
+                out=ws_codes[b][:, 2 * v * P : 2 * (v + 1) * P].bitcast(FP8X4),
+                scales=ws_scales[b][:, 2 * v * P : 2 * (v + 1) * P],
+                in_=ws_rounded[b][v][:].rearrange("p t c -> p (t c)"),
+            )
+
+        wm_codes = placed("wm_codes", [P, PASSES * N], U32, LATE_DEMAND)
         wm_scales = held("wm_scales", [P, PASSES * N], U8)
-        wm_rounded = placed("wm_rounded", [P, PASSES * N * PACK], BF16, STATE_WORDS)
+        wm_rounded = placed("wm_rounded", [P, PASSES * N * PACK], BF16, r0 + 3072 + 2048 - 64)
 
         def round_wm(b):
             nc.scalar.copy(
@@ -189,93 +193,80 @@ def tile_list_scheduled_gain_mixing_kernel(
                     in_=wm_rounded[:, PACK * first : PACK * last],
                 )
 
-        split = RAW_WS[1] + 6144
-        demand_early = placed("demand_early", [P, EARLY, S], F32, split)
-        demand_vector = placed("demand_vector", [P, PACK - EARLY, S], F32, split - 4 * S * (PACK - EARLY))
-        demand_middle = held("demand_middle", [P, S], F32)
-        demand_late = placed("demand_late", [P, PACK - 1, S], F32, LATE_DEMAND)
-        clamped = [
-            placed("clamped0", [P, CHUNKS, PACK, CHUNK], F32, after_ws1 + CHUNK + H + 4 * HALF),
-            placed("clamped1", [P, CHUNKS, PACK, CHUNK], F32, split - 4 * S * PACK),
+        demand_early = [
+            [placed("demand%d_%d" % (t, c), [P, CHUNK], F32, r1 + 1024 - 4096 * (CHUNKS * t + c)) for c in range(CHUNKS)]
+            for t in range(PACK)
         ]
+        demand_late = placed("demand_late", [P, 3 * S], F32, LATE_DEMAND)
+        clamped = [held("clamped%d" % b, [P, CHUNKS, PACK, CHUNK], F32) for b in range(PASSES)]
 
-        def demand_rows(u):
-            if u < EARLY:
-                return demand_early[:, u, :]
+        def staged(u, c):
             if u < PACK:
-                return demand_vector[:, u - EARLY, :]
-            return demand_middle[:] if u == PACK else demand_late[:, u - PACK - 1, :]
+                return demand_early[u][c][:]
+            first = (u - PACK) * S + c * CHUNK if u < PACK + 2 else 2 * S + (u - PACK - 2) * CHUNK
+            return demand_late[:, first : first + CHUNK]
 
         open_sums = {}
 
-        def open_demand(u, c, ring):
-            picks = slice(c * CHUNK, (c + 1) * CHUNK)
-            total = bank("demand", [P, CHUNK], ring)
+        def open_demand(u, c, ring=DEMAND_BANKS):
+            open_sums[u, c] = bank("demand", [P, CHUNK], ring)
             nc.tensor.matmul_mx(
-                out=total[:],
-                lhsT=wr_codes[:].bitcast(U8)[:, 2 * u * P : 2 * (u + 1) * P].bitcast(FP4X4),
-                lhsT_scale=wr_scale_tile[:].bitcast(U8)[:, u * P : (u + 1) * P],
-                rhs=reference_words[:, picks].bitcast(FP8X4),
-                rhs_scale=reference_scales[:, picks],
+                out=open_sums[u, c][:],
+                lhsT=wr_codes[u // PACK][:].bitcast(U8)[:, 2 * (u % PACK) * P : 2 * (u % PACK + 1) * P].bitcast(FP4X4),
+                lhsT_scale=wr_scale_tile[u // PACK][:].bitcast(U8)[:, (u % PACK) * P : (u % PACK + 1) * P],
+                rhs=reference_words[c][:].bitcast(FP8X4),
+                rhs_scale=reference_scales[:, c * CHUNK : (c + 1) * CHUNK],
                 start=True,
                 stop=False,
             )
-            open_sums[u, c] = total
 
         def close_demand(u, c):
             b, t = divmod(u, PACK)
-            picks = slice(c * CHUNK, (c + 1) * CHUNK)
-            total = open_sums[u, c]
             nc.tensor.matmul_mx(
-                out=total[:],
+                out=open_sums[u, c][:],
                 lhsT=ws_codes[b][:, t * P : (t + 1) * P].bitcast(FP8X4),
-                lhsT_scale=ws_scales[:, u * P : (u + 1) * P],
-                rhs=state_words[:, picks].bitcast(FP8X4),
-                rhs_scale=state_scales[:, picks],
+                lhsT_scale=ws_scales[b][:, t * P : (t + 1) * P],
+                rhs=state_words[c][:].bitcast(FP8X4),
+                rhs_scale=state_scales[c][:],
                 start=False,
                 stop=True,
             )
-            nc.scalar.copy(demand_rows(u)[:, picks], total[:])
 
-        def demand(u, c, ring):
-            open_demand(u, c, ring)
-            close_demand(u, c)
+        def stage(u, c):
+            nc.scalar.copy(staged(u, c), open_sums[u, c][:])
 
-        def clamp(engine, u, first_chunk, chunks):
+        def clamp(engine, u, first_chunk, chunks, rows):
             b, t = divmod(u, PACK)
-            rows = demand_rows(u)[:, first_chunk * CHUNK : (first_chunk + chunks) * CHUNK]
             engine.tensor_scalar(
                 clamped[b][:, first_chunk : first_chunk + chunks, t, :],
                 rows.rearrange("p (c j) -> p c j", j=CHUNK),
-                limits[:, b, HI + t : HI + t + 1],
-                limits[:, b, LO + t : LO + t + 1],
+                limits[:, b, t, HI : HI + 1],
+                limits[:, b, t, LO : LO + 1],
                 ALU.min,
                 ALU.max,
             )
 
         h = [held("h%d" % g, [P, PASSES * PACK * GROUP], BF16) for g in range(GROUPS)]
         h_codes = [
-            placed("h_codes%d" % g, [P, PASSES * GROUP], U32, LATE_DEMAND + 1024 + 4 * PASSES * GROUP * g)
+            placed("h_codes%d" % g, [P, PASSES * GROUP], U32, LATE_DEMAND + 3072 + 4 * PASSES * GROUP * g)
             for g in range(GROUPS)
         ]
         h_scales = [held("h_scales%d" % g, [P, PASSES * GROUP], U8) for g in range(GROUPS)]
 
-        starts = list(range(0, S, UNIT))
-        order = [(0, j0) for j0 in starts[CHUNK // UNIT :] + starts[: CHUNK // UNIT]] + [(1, j0) for j0 in starts]
+        order = [(b, j0) for b in range(PASSES) for j0 in range(0, S, UNIT)]
         gains = []
 
         def queue_gain():
             if len(gains) < len(order):
                 b, j0 = order[len(gains)]
                 c, within = divmod(j0, CHUNK)
-                gain = bank("gain", [P, PACK, UNIT], MAIN_BANKS)
+                gain = bank("gain", [P, PACK, UNIT], GAIN_BANKS)
                 for t in range(PACK):
-                    u = PACK * b + t
                     nc.tensor.matmul_mx(
                         out=gain[:, t, :],
                         lhsT=wg_codes[b][:, t * P : (t + 1) * P].bitcast(FP8X4),
-                        lhsT_scale=wg_scale_tile[:].bitcast(U8)[:, u * P : (u + 1) * P],
-                        rhs=gain_words[:, j0 : j0 + UNIT].bitcast(FP8X4),
+                        lhsT_scale=wg_scale_tile[b][:].bitcast(U8)[:, t * P : (t + 1) * P],
+                        rhs=gain_words[c][:, within : within + UNIT].bitcast(FP8X4),
                         rhs_scale=gain_scales[c][:, within : within + UNIT],
                         start=True,
                         stop=True,
@@ -320,7 +311,7 @@ def tile_list_scheduled_gain_mixing_kernel(
 
         def mix(g):
             result = held("result%d" % g, [P, N_TILES, GROUP], F32)
-            sums = [bank("mix", [P, GROUP], SIDE_BANKS) for n in range(N_TILES)]
+            sums = [bank("mix", [P, GROUP], DEMAND_BANKS) for n in range(N_TILES)]
             for n in range(N_TILES):
                 for b in range(PASSES):
                     mix_pass(sums[n], g, n, b, 0, GROUP, b == 0, b == PASSES - 1)
@@ -329,7 +320,7 @@ def tile_list_scheduled_gain_mixing_kernel(
             nc.sync.dma_start(out[:, g * GROUP : (g + 1) * GROUP].rearrange("(n p) j -> p n j", p=P), result[:])
 
         def mix_last(g):
-            sums = [bank("mix", [P, GROUP], MAIN_BANKS) for n in range(N_TILES)]
+            sums = [bank("mix", [P, GROUP], GAIN_BANKS) for n in range(N_TILES)]
             for n in range(N_TILES):
                 mix_pass(sums[n], g, n, 0, 0, GROUP, True, False)
             for first in range(0, GROUP, UNIT):
@@ -343,54 +334,77 @@ def tile_list_scheduled_gain_mixing_kernel(
                     nc.scalar.activation(result[:], sums[n][:], ACT.Identity, bias=trims[:, n : n + 1])
                 nc.sync.dma_start(out[n * P : (n + 1) * P, g * GROUP : (g + 1) * GROUP], result[:])
 
-        regroup(nc.gpsimd, wr_codes, wr_raw, 4)
-        gather_scales(state_scales[:], lists[0][:])
         gather_scales(reference_scales[:], lists[1][:])
-        for c in range(CHUNKS):
-            gather_words(reference_words[:, c * CHUNK : (c + 1) * CHUNK], chunk_of(lists[1], c))
-        regroup(nc.gpsimd, wr_scale_tile, wr_raw_scales, 2)
-        regroup_wg(nc.gpsimd, 0)
-        gather_words(state_words[:], lists[0][:])
-        round_ws(0)
-        round_ws(1)
-        quantize_ws(0)
-        gather_scales(gain_scales[0][:], chunk_of(lists[2], 0))
-        quantize_ws(1)
-        gather_scales(gain_scales[1][:], chunk_of(lists[2], 1))
-        gather_words(gain_words[:], lists[2][:])
-        regroup(nc.vector, wg_scale_tile, wg_raw_scales, 2)
-        regroup_wg(nc.vector, 1)
-
-        limits_turned = bank("limits_turned", [P, PASSES, P], SIDE_BANKS)
+        gather_words(reference_words[0][:], chunk_of(lists[1], 0))
+        gather_scales(state_scales[0][:], chunk_of(lists[0], 0))
+        gather_words(state_words[0][:], chunk_of(lists[0], 0))
         for b in range(PASSES):
-            nc.tensor.transpose(limits_turned[:, b, :], limit_rows[:, b * P : (b + 1) * P], identity[:])
-        nc.scalar.copy(limits[:], limits_turned[:, :, 0 : 2 * PACK])
-
-        for c in range(CHUNKS):
+            nc.gpsimd.tensor_scalar(
+                limit_rows[0:2, b * HALF : (b + 1) * HALF].rearrange("p (t q i) -> p t q i", t=PACK, i=8),
+                limits_raw[:, b * HALF : (b + 1) * HALF].rearrange("p (q t i) -> p t q i", t=PACK, i=8),
+                1.0,
+                0.0,
+                ALU.mult,
+                ALU.add,
+            )
+            limits_turned = bank("limits_turned", [P, PACK, P], GAIN_BANKS)
             for t in range(PACK):
-                open_demand(t, c, MAIN_BANKS if CHUNKS * t + c < MAIN_BANKS[1] else SIDE_BANKS)
+                u = PACK * b + t
+                nc.tensor.transpose(limits_turned[:, t, :], limit_rows[:, u * P : (u + 1) * P], identity[:])
+            nc.scalar.copy(limits[:, b, :, :], limits_turned[:, :, 0:2])
         for t in range(PACK):
-            for c in range(CHUNKS):
-                close_demand(t, c)
-            clamp(nc.gpsimd if t < EARLY else nc.vector, t, 0, CHUNKS)
+            round_ws(0, t)
+        regroup_wr(nc.scalar.copy, 0)
+        regroup_wr(nc.gpsimd.tensor_copy, 1)
+        for t in range(PACK):
+            round_ws(1, t)
+        quantize_ws(0, 0)
+        gather_scales(state_scales[1][:], chunk_of(lists[0], 1))
+        quantize_ws(0, 1)
+        gather_words(reference_words[1][:], chunk_of(lists[1], 1))
+        gather_words(state_words[1][:], chunk_of(lists[0], 1))
+        gather_scales(gain_scales[0][:], chunk_of(lists[2], 0))
+        gather_words(gain_words[0][:], chunk_of(lists[2], 0))
 
-        demand(PACK, 0, MAIN_BANKS)
-        clamp(nc.vector, PACK, 0, 1)
-        demand(PACK + 1, 0, MAIN_BANKS)
-        clamp(nc.gpsimd, PACK + 1, 0, 1)
-        for c in range(CHUNKS):
-            demand(PACK + 2, c, MAIN_BANKS)
-        clamp(nc.gpsimd, PACK + 2, 0, CHUNKS)
-        demand(PACK + 3, 0, MAIN_BANKS)
-        demand(PACK + 3, 1, SIDE_BANKS)
-        clamp(nc.gpsimd, PACK + 3, 0, CHUNKS)
-        for k in range(AHEAD):
+        for t in range(PACK):
+            open_demand(t, 0)
+        for t in range(PACK):
+            close_demand(t, 0)
+            stage(t, 0)
+            clamp(nc.gpsimd, t, 0, 1, staged(t, 0))
+            round_ws(2, t)
+        quantize_ws(1, 0)
+        quantize_ws(1, 1)
+        gather_words(gain_words[1][:], chunk_of(lists[2], 1))
+        gather_scales(gain_scales[1][:], chunk_of(lists[2], 1))
+        for t in range(PACK):
+            open_demand(t, 1)
+            close_demand(t, 1)
+            stage(t, 1)
+            clamp(nc.gpsimd, t, 1, 1, staged(t, 1))
+        regroup_wg(0)
+        for u in (PACK + 2, PACK + 3):
+            open_demand(u, 0, GAIN_BANKS)
+            close_demand(u, 0)
+            clamp(nc.vector, u, 0, 1, open_sums[u, 0][:])
+        for k in range(2):
             queue_gain()
-        second_chunks_left = (PACK, PACK + 1)
-        for k in range(len(starts)):
-            if k < len(second_chunks_left):
-                demand(second_chunks_left[k], 1, SIDE_BANKS)
-                clamp(nc.gpsimd, second_chunks_left[k], 1, 1)
+        for u in (PACK, PACK + 1):
+            for c in range(CHUNKS):
+                open_demand(u, c)
+                close_demand(u, c)
+                stage(u, c)
+            clamp(nc.gpsimd, u, 0, CHUNKS, demand_late[:, (u - PACK) * S : (u - PACK + 1) * S])
+        regroup_wg(1)
+        for k in range(GAIN_BANKS[1] - 2):
+            queue_gain()
+        for u in (PACK + 2, PACK + 3):
+            open_demand(u, 1)
+            close_demand(u, 1)
+            stage(u, 1)
+            clamp(nc.gpsimd, u, 1, 1, staged(u, 1))
+
+        for k in range(S // UNIT):
             product(k)
 
         round_wm(0)

@@ -30,8 +30,10 @@ N_TILES = N // P
 LO, HI = 0, 1
 DEMAND_BANKS, GAIN_BANKS = ("demand", 4), ("gain", 4)
 
-ROUNDED_WS = (8192, 49152)
-LATE_DEMAND = 61440
+RAW_WR = 0
+ROUNDED_WS = (2048, 6144, 22528 + 2048 - 64)
+LATE_DEMAND = 53248
+EARLY_DEMAND = 22528
 
 
 def tile_list_scheduled_gain_mixing_kernel(
@@ -57,7 +59,7 @@ def tile_list_scheduled_gain_mixing_kernel(
         table_scales = held("table_scales", [P, T // 4], I32)
         wr_raw_scales = held("wr_raw_scales", [P, H // 4], I32)
         wg_raw_scales = held("wg_raw_scales", [P, H // 4], I32)
-        wr_raw = [held("wr_raw%d" % b, [P, HALF // 2], I32) for b in range(PASSES)]
+        wr_raw = [placed("wr_raw0", [P, HALF // 2], I32, RAW_WR), held("wr_raw1", [P, HALF // 2], I32)]
         wg_raw = held("wg_raw", [P, H], I32)
         ws_pieces = [(0, 0, HALF // 2), (0, HALF // 2, HALF), (1, 0, HALF)]
         ws_raw = [held("ws_raw%d" % i, [P, PACK, z - a], F32) for i, (b, a, z) in enumerate(ws_pieces)]
@@ -88,19 +90,19 @@ def tile_list_scheduled_gain_mixing_kernel(
 
         make_identity(nc, identity[:])
         nc.sync.dma_start(lists[1][:], offs2)
-        load_scale_rows(table_scales, tab_scales, (nc.sync, nc.scalar))
-        load_limits(LO, lo)
-        load_limits(HI, hi)
-        nc.sync.dma_start(table_words[:], tab_words[0].rearrange("p n t -> p (n t)").bitcast(I32))
         nc.sync.dma_start(lists[0][:], offs)
-        load_ws(0)
+        load_scale_rows(table_scales, tab_scales, (nc.sync, nc.scalar))
+        nc.sync.dma_start(table_words[:], tab_words[0].rearrange("p n t -> p (n t)").bitcast(I32))
         load_wr(0)
         load_scale_rows(wr_raw_scales, wr_scales, (nc.sync,))
-        load_wr(1)
+        load_ws(0)
+        load_limits(LO, lo)
+        load_limits(HI, hi)
         load_ws(1)
+        load_wr(1)
         load_ws(2)
-        nc.sync.dma_start(wg_raw[:], wg_words[0].rearrange("p n t -> p (n t)").bitcast(I32))
         nc.sync.dma_start(lists[2][:], offs3)
+        nc.sync.dma_start(wg_raw[:], wg_words[0].rearrange("p n t -> p (n t)").bitcast(I32))
         load_scale_rows(wg_raw_scales, wg_scales, (nc.sync,))
         for b in range(PASSES):
             wm_rows = wm[b * HALF : (b + 1) * HALF, :].rearrange("(q t i) n -> t q i n", t=PACK, i=8)
@@ -110,25 +112,28 @@ def tile_list_scheduled_gain_mixing_kernel(
         with nc.allow_non_contiguous_dma(reason="one trim value for each partition and output tile"):
             nc.sync.dma_start(trims[:], trim.rearrange("(n p) -> p n", p=P))
 
-        limits = held("limits", [P, PASSES, PACK, 2], F32)
+        limits = [held("limits%d" % b, [P, PACK, 2], F32) for b in range(PASSES)]
 
-        r0, r1 = ROUNDED_WS
+        r0, r1, r2 = ROUNDED_WS
+        ws_parts = [(0, 0, 2), (0, 2, PACK), (1, 0, PACK)]
         ws_rounded = [
-            [placed("ws_rounded%d_%d" % (b, v), [P, 2, HALF], BF16, ROUNDED_WS[b] + 2048 * v) for v in range(2)]
-            for b in range(PASSES)
+            placed("ws_rounded%d" % v, [P, z - a, HALF], BF16, ROUNDED_WS[v]) for v, (b, a, z) in enumerate(ws_parts)
         ]
-        state_words = [held("state_words0", [P, CHUNK], U32), placed("state_words1", [P, CHUNK], U32, r0 + 3072)]
+        state_words = [held("state_words0", [P, CHUNK], U32), placed("state_words1", [P, CHUNK], U32, r1 + 2048 - 64)]
         reference_words = [
             held("reference_words0", [P, CHUNK], U32),
-            placed("reference_words1", [P, CHUNK], U32, r0 + 512),
+            placed("reference_words1", [P, CHUNK], U32, r1 - 2048 + 64),
         ]
-        gain_words = [held("gain_words0", [P, CHUNK], U32), placed("gain_words1", [P, CHUNK], U32, r1 + 4096 - 64)]
+        gain_words = [
+            placed("gain_words0", [P, CHUNK], U32, EARLY_DEMAND - 2048 + 64),
+            placed("gain_words1", [P, CHUNK], U32, r2 + 1024),
+        ]
         state_scales = [held("state_scales0", [P, CHUNK], U8), placed("state_scales1", [P, CHUNK], U8, r0)]
-        reference_scales = held("reference_scales", [P, S], U8)
-        gain_scales = [
-            held("gain_scales0", [P, CHUNK], U8),
-            placed("gain_scales1", [P, CHUNK], U8, r1 + 2048),
+        reference_scales = [
+            held("reference_scales0", [P, CHUNK], U8),
+            placed("reference_scales1", [P, CHUNK], U8, RAW_WR),
         ]
+        gain_scales = placed("gain_scales", [P, S], U8, r1 + 512)
 
         def chunk_of(entries, c):
             return entries[:, c * CHUNK // 16 : (c + 1) * CHUNK // 16]
@@ -148,8 +153,9 @@ def tile_list_scheduled_gain_mixing_kernel(
 
         wr_codes = [held("wr_codes%d" % b, [P, HALF // 2], I32) for b in range(PASSES)]
         wr_scale_tile = [held("wr_scale_tile%d" % b, [P, HALF // 4], I32) for b in range(PASSES)]
-        wg_codes = [held("wg_codes%d" % b, [P, HALF], I32) for b in range(PASSES)]
-        wg_scale_tile = [held("wg_scale_tile%d" % b, [P, HALF // 4], I32) for b in range(PASSES)]
+        wg_at = [EARLY_DEMAND + 6144 + 3072 * 3, EARLY_DEMAND + 6144 + 3072 * 6]
+        wg_codes = [placed("wg_codes%d" % b, [P, HALF], I32, wg_at[b] + 512) for b in range(PASSES)]
+        wg_scale_tile = [placed("wg_scale_tile%d" % b, [P, HALF // 4], I32, wg_at[b]) for b in range(PASSES)]
         ws_codes = [held("ws_codes%d" % b, [P, HALF], U32) for b in range(PASSES)]
         ws_scales = [held("ws_scales%d" % b, [P, HALF], U8) for b in range(PASSES)]
 
@@ -161,23 +167,25 @@ def tile_list_scheduled_gain_mixing_kernel(
             nc.scalar.copy(*regrouped(wg_codes[b][:].bitcast(U32), wg_raw[:].bitcast(U32), 8, b))
             nc.scalar.copy(*regrouped(wg_scale_tile[b][:].bitcast(U32), wg_raw_scales[:].bitcast(U32), 2, b))
 
-        def round_ws(i, t):
+        def round_ws(i, v, first, last):
             b, a, z = ws_pieces[i]
-            source = ws_raw[i][:].rearrange("p j (q t h l) -> p t q h j l", t=PACK, h=2, l=4)
+            rows = slice(first - ws_parts[v][1], last - ws_parts[v][1])
             nc.scalar.copy(
-                ws_rounded[b][t // 2][:, t % 2, a:z].rearrange("p (q h l j) -> p q h j l", h=2, l=4, j=PACK), source[:, t]
+                ws_rounded[v][:, rows, a:z].rearrange("p t (q l j) -> p t q j l", l=8, j=PACK),
+                ws_raw[i][:].rearrange("p j (q t l) -> p t q j l", t=PACK, l=8)[:, first:last],
             )
 
-        def quantize_ws(b, v):
+        def quantize_ws(v):
+            b, a, z = ws_parts[v]
             nc.vector.quantize_mx(
-                out=ws_codes[b][:, 2 * v * P : 2 * (v + 1) * P].bitcast(FP8X4),
-                scales=ws_scales[b][:, 2 * v * P : 2 * (v + 1) * P],
-                in_=ws_rounded[b][v][:].rearrange("p t c -> p (t c)"),
+                out=ws_codes[b][:, a * P : z * P].bitcast(FP8X4),
+                scales=ws_scales[b][:, a * P : z * P],
+                in_=ws_rounded[v][:].rearrange("p t c -> p (t c)"),
             )
 
         wm_codes = placed("wm_codes", [P, PASSES * N], U32, LATE_DEMAND)
         wm_scales = held("wm_scales", [P, PASSES * N], U8)
-        wm_rounded = placed("wm_rounded", [P, PASSES * N * PACK], BF16, r0 + 3072 + 2048 - 64)
+        wm_rounded = placed("wm_rounded", [P, PASSES * N * PACK], BF16, r1 + 2048 + 2048 - 128)
 
         def round_wm(b):
             nc.scalar.copy(
@@ -194,7 +202,7 @@ def tile_list_scheduled_gain_mixing_kernel(
                 )
 
         demand_early = [
-            [placed("demand%d_%d" % (t, c), [P, CHUNK], F32, r1 + 1024 - 4096 * (CHUNKS * t + c)) for c in range(CHUNKS)]
+            [placed("demand%d_%d" % (t, c), [P, CHUNK], F32, EARLY_DEMAND + (6144 if t + c else 0) + 3072 * (PACK * c + t)) for c in range(CHUNKS)]
             for t in range(PACK)
         ]
         demand_late = placed("demand_late", [P, 3 * S], F32, LATE_DEMAND)
@@ -215,7 +223,7 @@ def tile_list_scheduled_gain_mixing_kernel(
                 lhsT=wr_codes[u // PACK][:].bitcast(U8)[:, 2 * (u % PACK) * P : 2 * (u % PACK + 1) * P].bitcast(FP4X4),
                 lhsT_scale=wr_scale_tile[u // PACK][:].bitcast(U8)[:, (u % PACK) * P : (u % PACK + 1) * P],
                 rhs=reference_words[c][:].bitcast(FP8X4),
-                rhs_scale=reference_scales[:, c * CHUNK : (c + 1) * CHUNK],
+                rhs_scale=reference_scales[c][:],
                 start=True,
                 stop=False,
             )
@@ -240,8 +248,8 @@ def tile_list_scheduled_gain_mixing_kernel(
             engine.tensor_scalar(
                 clamped[b][:, first_chunk : first_chunk + chunks, t, :],
                 rows.rearrange("p (c j) -> p c j", j=CHUNK),
-                limits[:, b, t, HI : HI + 1],
-                limits[:, b, t, LO : LO + 1],
+                limits[b][:, t, HI : HI + 1],
+                limits[b][:, t, LO : LO + 1],
                 ALU.min,
                 ALU.max,
             )
@@ -259,15 +267,14 @@ def tile_list_scheduled_gain_mixing_kernel(
         def queue_gain():
             if len(gains) < len(order):
                 b, j0 = order[len(gains)]
-                c, within = divmod(j0, CHUNK)
                 gain = bank("gain", [P, PACK, UNIT], GAIN_BANKS)
                 for t in range(PACK):
                     nc.tensor.matmul_mx(
                         out=gain[:, t, :],
                         lhsT=wg_codes[b][:, t * P : (t + 1) * P].bitcast(FP8X4),
                         lhsT_scale=wg_scale_tile[b][:].bitcast(U8)[:, t * P : (t + 1) * P],
-                        rhs=gain_words[c][:, within : within + UNIT].bitcast(FP8X4),
-                        rhs_scale=gain_scales[c][:, within : within + UNIT],
+                        rhs=gain_words[j0 // CHUNK][:, j0 % CHUNK : j0 % CHUNK + UNIT].bitcast(FP8X4),
+                        rhs_scale=gain_scales[:, j0 : j0 + UNIT],
                         start=True,
                         stop=True,
                     )
@@ -334,11 +341,7 @@ def tile_list_scheduled_gain_mixing_kernel(
                     nc.scalar.activation(result[:], sums[n][:], ACT.Identity, bias=trims[:, n : n + 1])
                 nc.sync.dma_start(out[n * P : (n + 1) * P, g * GROUP : (g + 1) * GROUP], result[:])
 
-        gather_scales(reference_scales[:], lists[1][:])
-        gather_words(reference_words[0][:], chunk_of(lists[1], 0))
-        gather_scales(state_scales[0][:], chunk_of(lists[0], 0))
-        gather_words(state_words[0][:], chunk_of(lists[0], 0))
-        for b in range(PASSES):
+        def regroup_limits(b):
             nc.gpsimd.tensor_scalar(
                 limit_rows[0:2, b * HALF : (b + 1) * HALF].rearrange("p (t q i) -> p t q i", t=PACK, i=8),
                 limits_raw[:, b * HALF : (b + 1) * HALF].rearrange("p (q t i) -> p t q i", t=PACK, i=8),
@@ -347,48 +350,59 @@ def tile_list_scheduled_gain_mixing_kernel(
                 ALU.mult,
                 ALU.add,
             )
-            limits_turned = bank("limits_turned", [P, PACK, P], GAIN_BANKS)
+
+        def turn_limits(b):
+            turned = bank("limits_turned", [P, PACK, P], GAIN_BANKS)
             for t in range(PACK):
                 u = PACK * b + t
-                nc.tensor.transpose(limits_turned[:, t, :], limit_rows[:, u * P : (u + 1) * P], identity[:])
-            nc.scalar.copy(limits[:, b, :, :], limits_turned[:, :, 0:2])
-        for t in range(PACK):
-            round_ws(0, t)
+                nc.tensor.transpose(turned[:, t, :], limit_rows[:, u * P : (u + 1) * P], identity[:])
+            nc.scalar.copy(limits[b][:], turned[:, :, 0:2])
+
+        gather_scales(reference_scales[0][:], chunk_of(lists[1], 0))
+        gather_scales(state_scales[0][:], chunk_of(lists[0], 0))
+        gather_words(reference_words[0][:], chunk_of(lists[1], 0))
+        gather_words(state_words[0][:], chunk_of(lists[0], 0))
         regroup_wr(nc.scalar.copy, 0)
+        gather_scales(reference_scales[1][:], chunk_of(lists[1], 1))
+        round_ws(0, 0, 0, 2)
+        round_ws(0, 1, 2, PACK)
+        for b in range(PASSES):
+            regroup_limits(b)
         regroup_wr(nc.gpsimd.tensor_copy, 1)
-        for t in range(PACK):
-            round_ws(1, t)
-        quantize_ws(0, 0)
+        round_ws(1, 0, 0, 2)
+        quantize_ws(0)
         gather_scales(state_scales[1][:], chunk_of(lists[0], 1))
-        quantize_ws(0, 1)
+        round_ws(1, 1, 2, PACK)
+        quantize_ws(1)
         gather_words(reference_words[1][:], chunk_of(lists[1], 1))
         gather_words(state_words[1][:], chunk_of(lists[0], 1))
-        gather_scales(gain_scales[0][:], chunk_of(lists[2], 0))
-        gather_words(gain_words[0][:], chunk_of(lists[2], 0))
+        gather_scales(gain_scales[:], lists[2][:])
 
         for t in range(PACK):
             open_demand(t, 0)
+        turn_limits(0)
         for t in range(PACK):
             close_demand(t, 0)
             stage(t, 0)
             clamp(nc.gpsimd, t, 0, 1, staged(t, 0))
-            round_ws(2, t)
-        quantize_ws(1, 0)
-        quantize_ws(1, 1)
-        gather_words(gain_words[1][:], chunk_of(lists[2], 1))
-        gather_scales(gain_scales[1][:], chunk_of(lists[2], 1))
+            if t >= 2:
+                round_ws(2, 2, t - 2, t - 1)
+        gather_words(gain_words[0][:], chunk_of(lists[2], 0))
+        turn_limits(1)
         for t in range(PACK):
             open_demand(t, 1)
             close_demand(t, 1)
             stage(t, 1)
             clamp(nc.gpsimd, t, 1, 1, staged(t, 1))
+            if t < 2:
+                round_ws(2, 2, t + 2, t + 3)
+        quantize_ws(2)
+        gather_words(gain_words[1][:], chunk_of(lists[2], 1))
         regroup_wg(0)
         for u in (PACK + 2, PACK + 3):
             open_demand(u, 0, GAIN_BANKS)
             close_demand(u, 0)
             clamp(nc.vector, u, 0, 1, open_sums[u, 0][:])
-        for k in range(2):
-            queue_gain()
         for u in (PACK, PACK + 1):
             for c in range(CHUNKS):
                 open_demand(u, c)
@@ -396,13 +410,14 @@ def tile_list_scheduled_gain_mixing_kernel(
                 stage(u, c)
             clamp(nc.gpsimd, u, 0, CHUNKS, demand_late[:, (u - PACK) * S : (u - PACK + 1) * S])
         regroup_wg(1)
-        for k in range(GAIN_BANKS[1] - 2):
-            queue_gain()
+        queue_gain()
+        queue_gain()
         for u in (PACK + 2, PACK + 3):
             open_demand(u, 1)
             close_demand(u, 1)
             stage(u, 1)
             clamp(nc.gpsimd, u, 1, 1, staged(u, 1))
+            queue_gain()
 
         for k in range(S // UNIT):
             product(k)

@@ -31,7 +31,7 @@ LO, HI = 0, 1
 DEMAND_BANKS, GAIN_BANKS = ("demand", 4), ("gain", 4)
 
 RAW_WR = 0
-ROUNDED_WS = (2048, 6144, 22528 + 2048 - 64)
+ROUNDED_WS = (2048, 6144, 22528 + 2048)
 LATE_DEMAND = 53248
 EARLY_DEMAND = 22528
 
@@ -61,7 +61,7 @@ def tile_list_scheduled_gain_mixing_kernel(
         wg_raw_scales = held("wg_raw_scales", [P, H // 4], I32)
         wr_raw = [placed("wr_raw0", [P, HALF // 2], I32, RAW_WR), held("wr_raw1", [P, HALF // 2], I32)]
         wg_raw = held("wg_raw", [P, H], I32)
-        ws_pieces = [(0, 0, HALF // 2), (0, HALF // 2, HALF), (1, 0, HALF)]
+        ws_pieces = [(b, a, a + HALF // 2) for b in range(PASSES) for a in (0, HALF // 2)]
         ws_raw = [held("ws_raw%d" % i, [P, PACK, z - a], F32) for i, (b, a, z) in enumerate(ws_pieces)]
         wm_raw = [held("wm_raw%d" % b, [P, PACK, N], F32) for b in range(PASSES)]
         limits_raw = held("limits_raw", [2, H], F32)
@@ -95,12 +95,13 @@ def tile_list_scheduled_gain_mixing_kernel(
         nc.sync.dma_start(table_words[:], tab_words[0].rearrange("p n t -> p (n t)").bitcast(I32))
         load_wr(0)
         load_scale_rows(wr_raw_scales, wr_scales, (nc.sync,))
+        load_wr(1)
         load_ws(0)
         load_limits(LO, lo)
         load_limits(HI, hi)
         load_ws(1)
-        load_wr(1)
         load_ws(2)
+        load_ws(3)
         nc.sync.dma_start(lists[2][:], offs3)
         nc.sync.dma_start(wg_raw[:], wg_words[0].rearrange("p n t -> p (n t)").bitcast(I32))
         load_scale_rows(wg_raw_scales, wg_scales, (nc.sync,))
@@ -124,16 +125,13 @@ def tile_list_scheduled_gain_mixing_kernel(
             held("reference_words0", [P, CHUNK], U32),
             placed("reference_words1", [P, CHUNK], U32, r1 - 2048 + 64),
         ]
-        gain_words = [
-            placed("gain_words0", [P, CHUNK], U32, EARLY_DEMAND - 2048 + 64),
-            placed("gain_words1", [P, CHUNK], U32, r2 + 1024),
-        ]
+        gain_words = [placed("gain_words%d" % c, [P, CHUNK], U32, r2 + 1024 + 2048 * c) for c in range(CHUNKS)]
         state_scales = [held("state_scales0", [P, CHUNK], U8), placed("state_scales1", [P, CHUNK], U8, r0)]
         reference_scales = [
             held("reference_scales0", [P, CHUNK], U8),
             placed("reference_scales1", [P, CHUNK], U8, RAW_WR),
         ]
-        gain_scales = placed("gain_scales", [P, S], U8, r1 + 512)
+        gain_scales = [placed("gain_scales0", [P, CHUNK], U8, r1 + 512), placed("gain_scales1", [P, CHUNK], U8, r2)]
 
         def chunk_of(entries, c):
             return entries[:, c * CHUNK // 16 : (c + 1) * CHUNK // 16]
@@ -173,6 +171,17 @@ def tile_list_scheduled_gain_mixing_kernel(
             nc.scalar.copy(
                 ws_rounded[v][:, rows, a:z].rearrange("p t (q l j) -> p t q j l", l=8, j=PACK),
                 ws_raw[i][:].rearrange("p j (q t l) -> p t q j l", t=PACK, l=8)[:, first:last],
+            )
+
+        def round_ws_on_gpsimd(i, v):
+            b, a, z = ws_pieces[i]
+            nc.gpsimd.tensor_scalar(
+                ws_rounded[v][:, :, a:z].rearrange("p t (q l j) -> p q t l j", l=8, j=PACK),
+                ws_raw[i][:].rearrange("p j (q t l) -> p q t l j", t=PACK, l=8),
+                1.0,
+                0.0,
+                ALU.mult,
+                ALU.add,
             )
 
         def quantize_ws(v):
@@ -274,7 +283,7 @@ def tile_list_scheduled_gain_mixing_kernel(
                         lhsT=wg_codes[b][:, t * P : (t + 1) * P].bitcast(FP8X4),
                         lhsT_scale=wg_scale_tile[b][:].bitcast(U8)[:, t * P : (t + 1) * P],
                         rhs=gain_words[j0 // CHUNK][:, j0 % CHUNK : j0 % CHUNK + UNIT].bitcast(FP8X4),
-                        rhs_scale=gain_scales[:, j0 : j0 + UNIT],
+                        rhs_scale=gain_scales[j0 // CHUNK][:, j0 % CHUNK : j0 % CHUNK + UNIT],
                         start=True,
                         stop=True,
                     )
@@ -376,8 +385,9 @@ def tile_list_scheduled_gain_mixing_kernel(
         quantize_ws(1)
         gather_words(reference_words[1][:], chunk_of(lists[1], 1))
         gather_words(state_words[1][:], chunk_of(lists[0], 1))
-        gather_scales(gain_scales[:], lists[2][:])
+        gather_scales(gain_scales[0][:], chunk_of(lists[2], 0))
 
+        round_ws_on_gpsimd(2, 2)
         for t in range(PACK):
             open_demand(t, 0)
         turn_limits(0)
@@ -385,19 +395,18 @@ def tile_list_scheduled_gain_mixing_kernel(
             close_demand(t, 0)
             stage(t, 0)
             clamp(nc.gpsimd, t, 0, 1, staged(t, 0))
-            if t >= 2:
-                round_ws(2, 2, t - 2, t - 1)
-        gather_words(gain_words[0][:], chunk_of(lists[2], 0))
+            if t in (1, 2):
+                round_ws(3, 2, 2 * (t - 1), 2 * t)
+        quantize_ws(2)
+        for c in range(CHUNKS):
+            gather_words(gain_words[c][:], chunk_of(lists[2], c))
+        gather_scales(gain_scales[1][:], chunk_of(lists[2], 1))
         turn_limits(1)
         for t in range(PACK):
             open_demand(t, 1)
             close_demand(t, 1)
             stage(t, 1)
             clamp(nc.gpsimd, t, 1, 1, staged(t, 1))
-            if t < 2:
-                round_ws(2, 2, t + 2, t + 3)
-        quantize_ws(2)
-        gather_words(gain_words[1][:], chunk_of(lists[2], 1))
         regroup_wg(0)
         for u in (PACK + 2, PACK + 3):
             open_demand(u, 0, GAIN_BANKS)
@@ -417,7 +426,8 @@ def tile_list_scheduled_gain_mixing_kernel(
             close_demand(u, 1)
             stage(u, 1)
             clamp(nc.gpsimd, u, 1, 1, staged(u, 1))
-            queue_gain()
+        queue_gain()
+        queue_gain()
 
         for k in range(S // UNIT):
             product(k)

@@ -30,7 +30,7 @@ N_TILES = N // P
 LO, HI = 0, 1
 DEMAND_BANKS, GAIN_BANKS = ("demand", 4), ("gain", 4)
 
-RAW_WR = 0
+RAW_WS = 16384
 ROUNDED_WS = (2048, 6144, 22528 + 2048)
 LATE_DEMAND = 53248
 EARLY_DEMAND = 22528
@@ -59,10 +59,11 @@ def tile_list_scheduled_gain_mixing_kernel(
         table_scales = held("table_scales", [P, T // 4], I32)
         wr_raw_scales = held("wr_raw_scales", [P, H // 4], I32)
         wg_raw_scales = held("wg_raw_scales", [P, H // 4], I32)
-        wr_raw = [placed("wr_raw0", [P, HALF // 2], I32, RAW_WR), held("wr_raw1", [P, HALF // 2], I32)]
+        wr_raw = held("wr_raw", [P, H // 2], I32)
         wg_raw = held("wg_raw", [P, H], I32)
         ws_pieces = [(b, a, a + HALF // 2) for b in range(PASSES) for a in (0, HALF // 2)]
-        ws_raw = [held("ws_raw%d" % i, [P, PACK, z - a], F32) for i, (b, a, z) in enumerate(ws_pieces)]
+        ws_raw = [placed("ws_raw0", [P, PACK, HALF // 2], F32, RAW_WS)]
+        ws_raw.extend(held("ws_raw%d" % i, [P, PACK, HALF // 2], F32) for i in range(1, 4))
         wm_raw = [held("wm_raw%d" % b, [P, PACK, N], F32) for b in range(PASSES)]
         limits_raw = held("limits_raw", [2, H], F32)
         limit_rows = held("limit_rows", [P, H], F32)
@@ -85,20 +86,16 @@ def tile_list_scheduled_gain_mixing_kernel(
         def load_limits(row, vector):
             nc.sync.dma_start(limits_raw[row : row + 1, :], vector.rearrange("(o r) -> o r", o=1))
 
-        def load_wr(b):
-            nc.sync.dma_start(wr_raw[b][:], wr_words[0, :, b * 2 * HALF : (b + 1) * 2 * HALF].bitcast(I32))
-
         make_identity(nc, identity[:])
         nc.sync.dma_start(lists[1][:], offs2)
         nc.sync.dma_start(lists[0][:], offs)
         load_scale_rows(table_scales, tab_scales, (nc.sync, nc.scalar))
         nc.sync.dma_start(table_words[:], tab_words[0].rearrange("p n t -> p (n t)").bitcast(I32))
-        load_wr(0)
-        load_scale_rows(wr_raw_scales, wr_scales, (nc.sync,))
-        load_wr(1)
+        nc.sync.dma_start(wr_raw[:], wr_words[0].bitcast(I32))
         load_ws(0)
         load_limits(LO, lo)
         load_limits(HI, hi)
+        load_scale_rows(wr_raw_scales, wr_scales, (nc.sync,))
         load_ws(1)
         load_ws(2)
         load_ws(3)
@@ -123,14 +120,14 @@ def tile_list_scheduled_gain_mixing_kernel(
         state_words = [held("state_words0", [P, CHUNK], U32), placed("state_words1", [P, CHUNK], U32, r1 + 2048 - 64)]
         reference_words = [
             held("reference_words0", [P, CHUNK], U32),
-            placed("reference_words1", [P, CHUNK], U32, r1 - 2048 + 64),
+            placed("reference_words1", [P, CHUNK], U32, r0 - 1024),
         ]
-        gain_words = [placed("gain_words%d" % c, [P, CHUNK], U32, r2 + 1024 + 2048 * c) for c in range(CHUNKS)]
-        state_scales = [held("state_scales0", [P, CHUNK], U8), placed("state_scales1", [P, CHUNK], U8, r0)]
-        reference_scales = [
-            held("reference_scales0", [P, CHUNK], U8),
-            placed("reference_scales1", [P, CHUNK], U8, RAW_WR),
+        gain_words = [
+            placed("gain_words0", [P, CHUNK], U32, r1 - 2048 + 64),
+            placed("gain_words1", [P, CHUNK], U32, r2 + 1024),
         ]
+        state_scales = [held("state_scales0", [P, CHUNK], U8), placed("state_scales1", [P, CHUNK], U8, RAW_WS)]
+        reference_scales = held("reference_scales", [P, S], U8)
         gain_scales = [placed("gain_scales0", [P, CHUNK], U8, r1 + 512), placed("gain_scales1", [P, CHUNK], U8, r2)]
 
         def chunk_of(entries, c):
@@ -158,8 +155,10 @@ def tile_list_scheduled_gain_mixing_kernel(
         ws_scales = [held("ws_scales%d" % b, [P, HALF], U8) for b in range(PASSES)]
 
         def regroup_wr(move, b):
-            move(*regrouped(wr_codes[b][:].bitcast(U32), wr_raw[b][:].bitcast(U32), 4, 0))
-            move(*regrouped(wr_scale_tile[b][:].bitcast(U32), wr_raw_scales[:].bitcast(U32), 2, b))
+            move(*regrouped(wr_codes[b][:].bitcast(U32), wr_raw[:].bitcast(U32), 4, b))
+
+        def regroup_wr_scales(b):
+            nc.gpsimd.tensor_copy(*regrouped(wr_scale_tile[b][:], wr_raw_scales[:], 2, b))
 
         def regroup_wg(b):
             nc.scalar.copy(*regrouped(wg_codes[b][:].bitcast(U32), wg_raw[:].bitcast(U32), 8, b))
@@ -171,17 +170,6 @@ def tile_list_scheduled_gain_mixing_kernel(
             nc.scalar.copy(
                 ws_rounded[v][:, rows, a:z].rearrange("p t (q l j) -> p t q j l", l=8, j=PACK),
                 ws_raw[i][:].rearrange("p j (q t l) -> p t q j l", t=PACK, l=8)[:, first:last],
-            )
-
-        def round_ws_on_gpsimd(i, v):
-            b, a, z = ws_pieces[i]
-            nc.gpsimd.tensor_scalar(
-                ws_rounded[v][:, :, a:z].rearrange("p t (q l j) -> p q t l j", l=8, j=PACK),
-                ws_raw[i][:].rearrange("p j (q t l) -> p q t l j", t=PACK, l=8),
-                1.0,
-                0.0,
-                ALU.mult,
-                ALU.add,
             )
 
         def quantize_ws(v):
@@ -232,7 +220,7 @@ def tile_list_scheduled_gain_mixing_kernel(
                 lhsT=wr_codes[u // PACK][:].bitcast(U8)[:, 2 * (u % PACK) * P : 2 * (u % PACK + 1) * P].bitcast(FP4X4),
                 lhsT_scale=wr_scale_tile[u // PACK][:].bitcast(U8)[:, (u % PACK) * P : (u % PACK + 1) * P],
                 rhs=reference_words[c][:].bitcast(FP8X4),
-                rhs_scale=reference_scales[c][:],
+                rhs_scale=reference_scales[:, c * CHUNK : (c + 1) * CHUNK],
                 start=True,
                 stop=False,
             )
@@ -367,30 +355,31 @@ def tile_list_scheduled_gain_mixing_kernel(
                 nc.tensor.transpose(turned[:, t, :], limit_rows[:, u * P : (u + 1) * P], identity[:])
             nc.scalar.copy(limits[b][:], turned[:, :, 0:2])
 
-        gather_scales(reference_scales[0][:], chunk_of(lists[1], 0))
+        gather_scales(reference_scales[:], lists[1][:])
         gather_scales(state_scales[0][:], chunk_of(lists[0], 0))
         gather_words(reference_words[0][:], chunk_of(lists[1], 0))
         gather_words(state_words[0][:], chunk_of(lists[0], 0))
         regroup_wr(nc.scalar.copy, 0)
-        gather_scales(reference_scales[1][:], chunk_of(lists[1], 1))
         round_ws(0, 0, 0, 2)
         round_ws(0, 1, 2, PACK)
+        gather_scales(state_scales[1][:], chunk_of(lists[0], 1))
+        regroup_wr(nc.gpsimd.tensor_copy, 1)
         for b in range(PASSES):
             regroup_limits(b)
-        regroup_wr(nc.gpsimd.tensor_copy, 1)
+            regroup_wr_scales(b)
         round_ws(1, 0, 0, 2)
         quantize_ws(0)
-        gather_scales(state_scales[1][:], chunk_of(lists[0], 1))
+        gather_words(reference_words[1][:], chunk_of(lists[1], 1))
         round_ws(1, 1, 2, PACK)
         quantize_ws(1)
-        gather_words(reference_words[1][:], chunk_of(lists[1], 1))
         gather_words(state_words[1][:], chunk_of(lists[0], 1))
         gather_scales(gain_scales[0][:], chunk_of(lists[2], 0))
+        gather_words(gain_words[0][:], chunk_of(lists[2], 0))
 
-        round_ws_on_gpsimd(2, 2)
+        turn_limits(0)
         for t in range(PACK):
             open_demand(t, 0)
-        turn_limits(0)
+        round_ws(2, 2, 0, PACK)
         for t in range(PACK):
             close_demand(t, 0)
             stage(t, 0)
@@ -398,8 +387,7 @@ def tile_list_scheduled_gain_mixing_kernel(
             if t in (1, 2):
                 round_ws(3, 2, 2 * (t - 1), 2 * t)
         quantize_ws(2)
-        for c in range(CHUNKS):
-            gather_words(gain_words[c][:], chunk_of(lists[2], c))
+        gather_words(gain_words[1][:], chunk_of(lists[2], 1))
         gather_scales(gain_scales[1][:], chunk_of(lists[2], 1))
         turn_limits(1)
         for t in range(PACK):
@@ -426,8 +414,7 @@ def tile_list_scheduled_gain_mixing_kernel(
             close_demand(u, 1)
             stage(u, 1)
             clamp(nc.gpsimd, u, 1, 1, staged(u, 1))
-        queue_gain()
-        queue_gain()
+            queue_gain()
 
         for k in range(S // UNIT):
             product(k)

@@ -30,10 +30,9 @@ N_TILES = N // P
 LO, HI = 0, 1
 DEMAND_BANKS, GAIN_BANKS = ("demand", 4), ("gain", 4)
 
-RAW_WS = 16384
-ROUNDED_WS = (2048, 6144, 22528 + 2048)
-LATE_DEMAND = 53248
-EARLY_DEMAND = 22528
+RAW_WS = (0, 8192, 20480)
+LATE_DEMAND = 57344
+EARLY_DEMAND = 32768
 
 
 def tile_list_scheduled_gain_mixing_kernel(
@@ -62,8 +61,12 @@ def tile_list_scheduled_gain_mixing_kernel(
         wr_raw = held("wr_raw", [P, H // 2], I32)
         wg_raw = held("wg_raw", [P, H], I32)
         ws_pieces = [(b, a, a + HALF // 2) for b in range(PASSES) for a in (0, HALF // 2)]
-        ws_raw = [placed("ws_raw0", [P, PACK, HALF // 2], F32, RAW_WS)]
-        ws_raw.extend(held("ws_raw%d" % i, [P, PACK, HALF // 2], F32) for i in range(1, 4))
+        ws_raw = [
+            placed("ws_raw0", [P, PACK, HALF // 2], F32, RAW_WS[0]),
+            placed("ws_raw1", [P, PACK, HALF // 2], F32, RAW_WS[1]),
+            held("ws_raw2", [P, PACK, HALF // 2], F32),
+            placed("ws_raw3", [P, PACK, HALF // 2], F32, RAW_WS[2]),
+        ]
         wm_raw = [held("wm_raw%d" % b, [P, PACK, N], F32) for b in range(PASSES)]
         limits_raw = held("limits_raw", [2, H], F32)
         limit_rows = held("limit_rows", [P, H], F32)
@@ -112,21 +115,18 @@ def tile_list_scheduled_gain_mixing_kernel(
 
         limits = [held("limits%d" % b, [P, PACK, 2], F32) for b in range(PASSES)]
 
-        r0, r1, r2 = ROUNDED_WS
-        ws_parts = [(0, 0, 2), (0, 2, PACK), (1, 0, PACK)]
-        ws_rounded = [
-            placed("ws_rounded%d" % v, [P, z - a, HALF], BF16, ROUNDED_WS[v]) for v, (b, a, z) in enumerate(ws_parts)
-        ]
-        state_words = [held("state_words0", [P, CHUNK], U32), placed("state_words1", [P, CHUNK], U32, r1 + 2048 - 64)]
+        r0, r1, r2 = RAW_WS
+        ws_rounded = [held("ws_rounded%d" % b, [P, PACK, HALF], BF16) for b in range(PASSES)]
+        state_words = [held("state_words0", [P, CHUNK], U32), placed("state_words1", [P, CHUNK], U32, r1 + 3072)]
         reference_words = [
             held("reference_words0", [P, CHUNK], U32),
-            placed("reference_words1", [P, CHUNK], U32, r0 - 1024),
+            placed("reference_words1", [P, CHUNK], U32, r1 + 1024),
         ]
         gain_words = [
-            placed("gain_words0", [P, CHUNK], U32, r1 - 2048 + 64),
+            placed("gain_words0", [P, CHUNK], U32, r1 - 1536),
             placed("gain_words1", [P, CHUNK], U32, r2 + 1024),
         ]
-        state_scales = [held("state_scales0", [P, CHUNK], U8), placed("state_scales1", [P, CHUNK], U8, RAW_WS)]
+        state_scales = [held("state_scales0", [P, CHUNK], U8), placed("state_scales1", [P, CHUNK], U8, r0)]
         reference_scales = held("reference_scales", [P, S], U8)
         gain_scales = [placed("gain_scales0", [P, CHUNK], U8, r1 + 512), placed("gain_scales1", [P, CHUNK], U8, r2)]
 
@@ -148,7 +148,7 @@ def tile_list_scheduled_gain_mixing_kernel(
 
         wr_codes = [held("wr_codes%d" % b, [P, HALF // 2], I32) for b in range(PASSES)]
         wr_scale_tile = [held("wr_scale_tile%d" % b, [P, HALF // 4], I32) for b in range(PASSES)]
-        wg_at = [EARLY_DEMAND + 6144 + 3072 * 3, EARLY_DEMAND + 6144 + 3072 * 6]
+        wg_at = [EARLY_DEMAND + 3072 * 2, EARLY_DEMAND + 3072 * 5]
         wg_codes = [placed("wg_codes%d" % b, [P, HALF], I32, wg_at[b] + 512) for b in range(PASSES)]
         wg_scale_tile = [placed("wg_scale_tile%d" % b, [P, HALF // 4], I32, wg_at[b]) for b in range(PASSES)]
         ws_codes = [held("ws_codes%d" % b, [P, HALF], U32) for b in range(PASSES)]
@@ -164,25 +164,23 @@ def tile_list_scheduled_gain_mixing_kernel(
             nc.scalar.copy(*regrouped(wg_codes[b][:].bitcast(U32), wg_raw[:].bitcast(U32), 8, b))
             nc.scalar.copy(*regrouped(wg_scale_tile[b][:].bitcast(U32), wg_raw_scales[:].bitcast(U32), 2, b))
 
-        def round_ws(i, v, first, last):
+        def round_ws(i, first, last):
             b, a, z = ws_pieces[i]
-            rows = slice(first - ws_parts[v][1], last - ws_parts[v][1])
             nc.scalar.copy(
-                ws_rounded[v][:, rows, a:z].rearrange("p t (q l j) -> p t q j l", l=8, j=PACK),
+                ws_rounded[b][:, first:last, a:z].rearrange("p t (q l j) -> p t q j l", l=8, j=PACK),
                 ws_raw[i][:].rearrange("p j (q t l) -> p t q j l", t=PACK, l=8)[:, first:last],
             )
 
-        def quantize_ws(v):
-            b, a, z = ws_parts[v]
+        def quantize_ws(b):
             nc.vector.quantize_mx(
-                out=ws_codes[b][:, a * P : z * P].bitcast(FP8X4),
-                scales=ws_scales[b][:, a * P : z * P],
-                in_=ws_rounded[v][:].rearrange("p t c -> p (t c)"),
+                out=ws_codes[b][:].bitcast(FP8X4),
+                scales=ws_scales[b][:],
+                in_=ws_rounded[b][:].rearrange("p t c -> p (t c)"),
             )
 
         wm_codes = placed("wm_codes", [P, PASSES * N], U32, LATE_DEMAND)
         wm_scales = held("wm_scales", [P, PASSES * N], U8)
-        wm_rounded = placed("wm_rounded", [P, PASSES * N * PACK], BF16, r1 + 2048 + 2048 - 128)
+        wm_rounded = placed("wm_rounded", [P, PASSES * N * PACK], BF16, r1 + 3072 + 2048 - 64)
 
         def round_wm(b):
             nc.scalar.copy(
@@ -190,25 +188,27 @@ def tile_list_scheduled_gain_mixing_kernel(
                 wm_raw[b][:].rearrange("p t (h l) -> p h t l", l=4),
             )
 
-        def quantize_wm():
-            for first, last in ((0, 512), (512, PASSES * N)):
-                nc.vector.quantize_mx(
-                    out=wm_codes[:, first:last].bitcast(FP8X4),
-                    scales=wm_scales[:, first:last],
-                    in_=wm_rounded[:, PACK * first : PACK * last],
-                )
+        def quantize_wm(b):
+            nc.vector.quantize_mx(
+                out=wm_codes[:, b * N : (b + 1) * N].bitcast(FP8X4),
+                scales=wm_scales[:, b * N : (b + 1) * N],
+                in_=wm_rounded[:, PACK * b * N : PACK * (b + 1) * N],
+            )
 
         demand_early = [
-            [placed("demand%d_%d" % (t, c), [P, CHUNK], F32, EARLY_DEMAND + (6144 if t + c else 0) + 3072 * (PACK * c + t)) for c in range(CHUNKS)]
-            for t in range(PACK)
+            [placed("demand%d_%d" % (t, c), [P, CHUNK], F32, EARLY_DEMAND + 3072 * (PACK * c + t)) for c in range(CHUNKS)]
+            for t in range(PACK - 1)
         ]
-        demand_late = placed("demand_late", [P, 3 * S], F32, LATE_DEMAND)
+        demand_wide = held("demand_wide", [P, S], F32)
+        demand_late = placed("demand_late", [P, 3 * S + CHUNK], F32, LATE_DEMAND)
         clamped = [held("clamped%d" % b, [P, CHUNKS, PACK, CHUNK], F32) for b in range(PASSES)]
 
         def staged(u, c):
-            if u < PACK:
+            if u < PACK - 1:
                 return demand_early[u][c][:]
-            first = (u - PACK) * S + c * CHUNK if u < PACK + 2 else 2 * S + (u - PACK - 2) * CHUNK
+            if u < PACK:
+                return demand_wide[:, c * CHUNK : (c + 1) * CHUNK]
+            first = (u - PACK) * S + c * CHUNK if u < PACK + 3 else 3 * S
             return demand_late[:, first : first + CHUNK]
 
         open_sums = {}
@@ -239,6 +239,11 @@ def tile_list_scheduled_gain_mixing_kernel(
 
         def stage(u, c):
             nc.scalar.copy(staged(u, c), open_sums[u, c][:])
+
+        def demand(u, c):
+            open_demand(u, c)
+            close_demand(u, c)
+            stage(u, c)
 
         def clamp(engine, u, first_chunk, chunks, rows):
             b, t = divmod(u, PACK)
@@ -316,8 +321,8 @@ def tile_list_scheduled_gain_mixing_kernel(
         def mix(g):
             result = held("result%d" % g, [P, N_TILES, GROUP], F32)
             sums = [bank("mix", [P, GROUP], DEMAND_BANKS) for n in range(N_TILES)]
-            for n in range(N_TILES):
-                for b in range(PASSES):
+            for b in range(PASSES):
+                for n in range(N_TILES):
                     mix_pass(sums[n], g, n, b, 0, GROUP, b == 0, b == PASSES - 1)
             for n in range(N_TILES):
                 nc.scalar.activation(result[:, n, :], sums[n][:], ACT.Identity, bias=trims[:, n : n + 1])
@@ -360,18 +365,15 @@ def tile_list_scheduled_gain_mixing_kernel(
         gather_words(reference_words[0][:], chunk_of(lists[1], 0))
         gather_words(state_words[0][:], chunk_of(lists[0], 0))
         regroup_wr(nc.scalar.copy, 0)
-        round_ws(0, 0, 0, 2)
-        round_ws(0, 1, 2, PACK)
+        round_ws(0, 0, PACK)
         gather_scales(state_scales[1][:], chunk_of(lists[0], 1))
         regroup_wr(nc.gpsimd.tensor_copy, 1)
         for b in range(PASSES):
             regroup_limits(b)
             regroup_wr_scales(b)
-        round_ws(1, 0, 0, 2)
+        round_ws(1, 0, PACK)
         quantize_ws(0)
         gather_words(reference_words[1][:], chunk_of(lists[1], 1))
-        round_ws(1, 1, 2, PACK)
-        quantize_ws(1)
         gather_words(state_words[1][:], chunk_of(lists[0], 1))
         gather_scales(gain_scales[0][:], chunk_of(lists[2], 0))
         gather_words(gain_words[0][:], chunk_of(lists[2], 0))
@@ -379,53 +381,54 @@ def tile_list_scheduled_gain_mixing_kernel(
         turn_limits(0)
         for t in range(PACK):
             open_demand(t, 0)
-        round_ws(2, 2, 0, PACK)
+        round_ws(2, 0, PACK)
         for t in range(PACK):
             close_demand(t, 0)
             stage(t, 0)
-            clamp(nc.gpsimd, t, 0, 1, staged(t, 0))
+            if t < PACK - 1:
+                clamp(nc.gpsimd, t, 0, 1, staged(t, 0))
             if t in (1, 2):
-                round_ws(3, 2, 2 * (t - 1), 2 * t)
-        quantize_ws(2)
+                round_ws(3, 2 * (t - 1), 2 * t)
+        quantize_ws(1)
         gather_words(gain_words[1][:], chunk_of(lists[2], 1))
         gather_scales(gain_scales[1][:], chunk_of(lists[2], 1))
+        demand(PACK - 1, 1)
+        clamp(nc.gpsimd, PACK - 1, 0, CHUNKS, demand_wide[:])
         turn_limits(1)
-        for t in range(PACK):
-            open_demand(t, 1)
-            close_demand(t, 1)
-            stage(t, 1)
+        for t in range(PACK - 1):
+            if t == PACK - 2:
+                regroup_wg(0)
+            demand(t, 1)
             clamp(nc.gpsimd, t, 1, 1, staged(t, 1))
-        regroup_wg(0)
-        for u in (PACK + 2, PACK + 3):
-            open_demand(u, 0, GAIN_BANKS)
-            close_demand(u, 0)
-            clamp(nc.vector, u, 0, 1, open_sums[u, 0][:])
+        open_demand(PACK + 3, 0, GAIN_BANKS)
+        close_demand(PACK + 3, 0)
+        clamp(nc.vector, PACK + 3, 0, 1, open_sums[PACK + 3, 0][:])
+        demand(PACK + 2, 0)
+        clamp(nc.gpsimd, PACK + 2, 0, 1, staged(PACK + 2, 0))
         for u in (PACK, PACK + 1):
+            if u > PACK:
+                for k in range(3):
+                    queue_gain()
             for c in range(CHUNKS):
-                open_demand(u, c)
-                close_demand(u, c)
-                stage(u, c)
+                demand(u, c)
             clamp(nc.gpsimd, u, 0, CHUNKS, demand_late[:, (u - PACK) * S : (u - PACK + 1) * S])
         regroup_wg(1)
         queue_gain()
-        queue_gain()
-        for u in (PACK + 2, PACK + 3):
-            open_demand(u, 1)
-            close_demand(u, 1)
-            stage(u, 1)
-            clamp(nc.gpsimd, u, 1, 1, staged(u, 1))
-            queue_gain()
-
         for k in range(S // UNIT):
             product(k)
+            if k in (1, 3):
+                u = PACK + 2 + k // 2
+                demand(u, 1)
+                clamp(nc.gpsimd, u, 1, 1, staged(u, 1))
 
         round_wm(0)
         round_wm(1)
         finish_group(0)
         finish_group(1)
         quantize_h(0, 0, PASSES * GROUP)
-        quantize_wm()
+        quantize_wm(0)
         quantize_h(1, 0, PASSES * GROUP)
+        quantize_wm(1)
         mix(0)
         mix(1)
         finish_group(2)

@@ -93,11 +93,11 @@ def tile_list_scheduled_gain_mixing_kernel(
         nc.sync.dma_start(lists[1][:], offs2)
         nc.sync.dma_start(lists[0][:], offs)
         load_scale_rows(table_scales, tab_scales, (nc.sync, nc.scalar))
+        load_limits(LO, lo)
         nc.sync.dma_start(table_words[:], tab_words[0].rearrange("p n t -> p (n t)").bitcast(I32))
         nc.sync.dma_start(wr_raw[:], wr_words[0].bitcast(I32))
-        load_ws(0)
-        load_limits(LO, lo)
         load_limits(HI, hi)
+        load_ws(0)
         load_scale_rows(wr_raw_scales, wr_scales, (nc.sync,))
         load_ws(1)
         load_ws(2)
@@ -157,8 +157,8 @@ def tile_list_scheduled_gain_mixing_kernel(
         def regroup_wr(move, b):
             move(*regrouped(wr_codes[b][:].bitcast(U32), wr_raw[:].bitcast(U32), 4, b))
 
-        def regroup_wr_scales(b):
-            nc.gpsimd.tensor_copy(*regrouped(wr_scale_tile[b][:], wr_raw_scales[:], 2, b))
+        def regroup_wr_scales(move, b):
+            move(*regrouped(wr_scale_tile[b][:].bitcast(U32), wr_raw_scales[:].bitcast(U32), 2, b))
 
         def regroup_wg(b):
             nc.scalar.copy(*regrouped(wg_codes[b][:].bitcast(U32), wg_raw[:].bitcast(U32), 8, b))
@@ -169,6 +169,17 @@ def tile_list_scheduled_gain_mixing_kernel(
             nc.scalar.copy(
                 ws_rounded[b][:, first:last, a:z].rearrange("p t (q l j) -> p t q j l", l=8, j=PACK),
                 ws_raw[i][:].rearrange("p j (q t l) -> p t q j l", t=PACK, l=8)[:, first:last],
+            )
+
+        def round_ws_on_gpsimd(i, first, last):
+            b, a, z = ws_pieces[i]
+            nc.gpsimd.tensor_scalar(
+                ws_rounded[b][:, first:last, a:z].rearrange("p t (q l j) -> p q t l j", l=8, j=PACK),
+                ws_raw[i][:].rearrange("p j (q t l) -> p q t l j", t=PACK, l=8)[:, :, first:last],
+                1.0,
+                0.0,
+                ALU.mult,
+                ALU.add,
             )
 
         def quantize_ws(b):
@@ -364,14 +375,15 @@ def tile_list_scheduled_gain_mixing_kernel(
         gather_scales(state_scales[0][:], chunk_of(lists[0], 0))
         gather_words(reference_words[0][:], chunk_of(lists[1], 0))
         gather_words(state_words[0][:], chunk_of(lists[0], 0))
-        regroup_wr(nc.scalar.copy, 0)
+        for b in range(PASSES):
+            regroup_wr(nc.scalar.copy, b)
+            regroup_limits(b)
         round_ws(0, 0, PACK)
         gather_scales(state_scales[1][:], chunk_of(lists[0], 1))
-        regroup_wr(nc.gpsimd.tensor_copy, 1)
-        for b in range(PASSES):
-            regroup_limits(b)
-            regroup_wr_scales(b)
-        round_ws(1, 0, PACK)
+        regroup_wr_scales(nc.gpsimd.tensor_copy, 0)
+        round_ws(1, 0, 2)
+        round_ws_on_gpsimd(1, 2, PACK)
+        regroup_wr_scales(nc.scalar.copy, 1)
         quantize_ws(0)
         gather_words(reference_words[1][:], chunk_of(lists[1], 1))
         gather_words(state_words[1][:], chunk_of(lists[0], 1))

@@ -58,7 +58,7 @@ def tile_list_scheduled_gain_mixing_kernel(
         table_scales = held("table_scales", [P, T // 4], I32)
         wr_raw_scales = held("wr_raw_scales", [P, H // 4], I32)
         wg_raw_scales = held("wg_raw_scales", [P, H // 4], I32)
-        wr_raw = held("wr_raw", [P, H // 2], I32)
+        wr_raw = [held("wr_raw%d" % b, [P, HALF // 2], I32) for b in range(PASSES)]
         wg_raw = held("wg_raw", [P, H], I32)
         ws_pieces = [(b, a, a + HALF // 2) for b in range(PASSES) for a in (0, HALF // 2)]
         ws_raw = [
@@ -86,6 +86,9 @@ def tile_list_scheduled_gain_mixing_kernel(
             b, a, z = ws_pieces[i]
             nc.sync.dma_start(ws_raw[i][:], ws[:, b * HALF + a : b * HALF + z].rearrange("(p j) c -> p j c", j=PACK))
 
+        def load_wr(b):
+            nc.sync.dma_start(wr_raw[b][:], wr_words[0, :, b * 2 * HALF : (b + 1) * 2 * HALF].bitcast(I32))
+
         def load_limits(row, vector):
             nc.sync.dma_start(limits_raw[row : row + 1, :], vector.rearrange("(o r) -> o r", o=1))
 
@@ -95,11 +98,12 @@ def tile_list_scheduled_gain_mixing_kernel(
         load_scale_rows(table_scales, tab_scales, (nc.sync, nc.scalar))
         load_limits(LO, lo)
         nc.sync.dma_start(table_words[:], tab_words[0].rearrange("p n t -> p (n t)").bitcast(I32))
-        nc.sync.dma_start(wr_raw[:], wr_words[0].bitcast(I32))
+        load_wr(0)
         load_limits(HI, hi)
         load_ws(0)
         load_scale_rows(wr_raw_scales, wr_scales, (nc.sync,))
         load_ws(1)
+        load_wr(1)
         load_ws(2)
         load_ws(3)
         nc.sync.dma_start(lists[2][:], offs3)
@@ -123,12 +127,12 @@ def tile_list_scheduled_gain_mixing_kernel(
             placed("reference_words1", [P, CHUNK], U32, r1 + 1024),
         ]
         gain_words = [
-            placed("gain_words0", [P, CHUNK], U32, r1 - 1536),
+            placed("gain_words0", [P, CHUNK], U32, r2 + 3072),
             placed("gain_words1", [P, CHUNK], U32, r2 + 1024),
         ]
         state_scales = [held("state_scales0", [P, CHUNK], U8), placed("state_scales1", [P, CHUNK], U8, r0)]
         reference_scales = held("reference_scales", [P, S], U8)
-        gain_scales = [placed("gain_scales0", [P, CHUNK], U8, r1 + 512), placed("gain_scales1", [P, CHUNK], U8, r2)]
+        gain_scales = placed("gain_scales", [P, S], U8, r1)
 
         def chunk_of(entries, c):
             return entries[:, c * CHUNK // 16 : (c + 1) * CHUNK // 16]
@@ -155,7 +159,7 @@ def tile_list_scheduled_gain_mixing_kernel(
         ws_scales = [held("ws_scales%d" % b, [P, HALF], U8) for b in range(PASSES)]
 
         def regroup_wr(move, b):
-            move(*regrouped(wr_codes[b][:].bitcast(U32), wr_raw[:].bitcast(U32), 4, b))
+            move(*regrouped(wr_codes[b][:].bitcast(U32), wr_raw[b][:].bitcast(U32), 4, 0))
 
         def regroup_wr_scales(move, b):
             move(*regrouped(wr_scale_tile[b][:].bitcast(U32), wr_raw_scales[:].bitcast(U32), 2, b))
@@ -287,7 +291,7 @@ def tile_list_scheduled_gain_mixing_kernel(
                         lhsT=wg_codes[b][:, t * P : (t + 1) * P].bitcast(FP8X4),
                         lhsT_scale=wg_scale_tile[b][:].bitcast(U8)[:, t * P : (t + 1) * P],
                         rhs=gain_words[j0 // CHUNK][:, j0 % CHUNK : j0 % CHUNK + UNIT].bitcast(FP8X4),
-                        rhs_scale=gain_scales[j0 // CHUNK][:, j0 % CHUNK : j0 % CHUNK + UNIT],
+                        rhs_scale=gain_scales[:, j0 : j0 + UNIT],
                         start=True,
                         stop=True,
                     )
@@ -329,15 +333,21 @@ def tile_list_scheduled_gain_mixing_kernel(
                 stop=stop,
             )
 
-        def mix(g):
-            result = held("result%d" % g, [P, N_TILES, GROUP], F32)
+        def mix(g, tiles_per_store):
+            results = [
+                held("result%d_%d" % (g, n), [P, tiles_per_store, GROUP], F32)
+                for n in range(0, N_TILES, tiles_per_store)
+            ]
             sums = [bank("mix", [P, GROUP], DEMAND_BANKS) for n in range(N_TILES)]
             for b in range(PASSES):
                 for n in range(N_TILES):
                     mix_pass(sums[n], g, n, b, 0, GROUP, b == 0, b == PASSES - 1)
             for n in range(N_TILES):
-                nc.scalar.activation(result[:, n, :], sums[n][:], ACT.Identity, bias=trims[:, n : n + 1])
-            nc.sync.dma_start(out[:, g * GROUP : (g + 1) * GROUP].rearrange("(n p) j -> p n j", p=P), result[:])
+                store, row = divmod(n, tiles_per_store)
+                nc.scalar.activation(results[store][:, row, :], sums[n][:], ACT.Identity, bias=trims[:, n : n + 1])
+                if row == tiles_per_store - 1:
+                    rows = out[(n - row) * P : (n + 1) * P, g * GROUP : (g + 1) * GROUP]
+                    nc.sync.dma_start(rows.rearrange("(n p) j -> p n j", p=P), results[store][:])
 
         def mix_last(g):
             sums = [bank("mix", [P, GROUP], GAIN_BANKS) for n in range(N_TILES)]
@@ -375,20 +385,20 @@ def tile_list_scheduled_gain_mixing_kernel(
         gather_scales(state_scales[0][:], chunk_of(lists[0], 0))
         gather_words(reference_words[0][:], chunk_of(lists[1], 0))
         gather_words(state_words[0][:], chunk_of(lists[0], 0))
+        regroup_wr(nc.scalar.copy, 0)
         for b in range(PASSES):
-            regroup_wr(nc.scalar.copy, b)
             regroup_limits(b)
         round_ws(0, 0, PACK)
         gather_scales(state_scales[1][:], chunk_of(lists[0], 1))
         regroup_wr_scales(nc.gpsimd.tensor_copy, 0)
         round_ws(1, 0, 2)
         round_ws_on_gpsimd(1, 2, PACK)
+        regroup_wr(nc.scalar.copy, 1)
         regroup_wr_scales(nc.scalar.copy, 1)
         quantize_ws(0)
         gather_words(reference_words[1][:], chunk_of(lists[1], 1))
         gather_words(state_words[1][:], chunk_of(lists[0], 1))
-        gather_scales(gain_scales[0][:], chunk_of(lists[2], 0))
-        gather_words(gain_words[0][:], chunk_of(lists[2], 0))
+        gather_scales(gain_scales[:], lists[2][:])
 
         turn_limits(0)
         for t in range(PACK):
@@ -402,8 +412,8 @@ def tile_list_scheduled_gain_mixing_kernel(
             if t in (1, 2):
                 round_ws(3, 2 * (t - 1), 2 * t)
         quantize_ws(1)
-        gather_words(gain_words[1][:], chunk_of(lists[2], 1))
-        gather_scales(gain_scales[1][:], chunk_of(lists[2], 1))
+        for c in range(CHUNKS):
+            gather_words(gain_words[c][:], chunk_of(lists[2], c))
         demand(PACK - 1, 1)
         clamp(nc.gpsimd, PACK - 1, 0, CHUNKS, demand_wide[:])
         turn_limits(1)
@@ -428,8 +438,8 @@ def tile_list_scheduled_gain_mixing_kernel(
         queue_gain()
         for k in range(S // UNIT):
             product(k)
-            if k in (1, 3):
-                u = PACK + 2 + k // 2
+            if k in (1, 2):
+                u = PACK + 1 + k
                 demand(u, 1)
                 clamp(nc.gpsimd, u, 1, 1, staged(u, 1))
 
@@ -439,14 +449,14 @@ def tile_list_scheduled_gain_mixing_kernel(
         finish_group(1)
         quantize_h(0, 0, PASSES * GROUP)
         quantize_wm(0)
-        quantize_h(1, 0, PASSES * GROUP)
         quantize_wm(1)
-        mix(0)
-        mix(1)
+        quantize_h(1, 0, PASSES * GROUP)
+        mix(0, N_TILES)
+        mix(1, N_TILES)
         finish_group(2)
         quantize_h(3, 0, GROUP)
         quantize_h(2, 0, PASSES * GROUP)
-        mix(2)
+        mix(2, 1)
         finish_group(3)
         quantize_h(3, GROUP, GROUP + UNIT)
         quantize_h(3, GROUP + UNIT, PASSES * GROUP)

@@ -95,7 +95,7 @@ def tile_list_scheduled_gain_mixing_kernel(
         make_identity(nc, identity[:])
         nc.sync.dma_start(lists[1][:], offs2)
         nc.sync.dma_start(lists[0][:], offs)
-        load_scale_rows(table_scales, tab_scales, (nc.sync, nc.scalar))
+        load_scale_rows(table_scales, tab_scales, (nc.scalar, nc.sync, nc.sync, nc.sync))
         load_limits(LO, lo)
         nc.sync.dma_start(table_words[:], tab_words[0].rearrange("p n t -> p (n t)").bitcast(I32))
         load_wr(0)

@@ -132,7 +132,7 @@ def tile_list_scheduled_gain_mixing_kernel(
         ]
         state_scales = [held("state_scales0", [P, CHUNK], U8), placed("state_scales1", [P, CHUNK], U8, r0)]
         reference_scales = held("reference_scales", [P, S], U8)
-        gain_scales = placed("gain_scales", [P, S], U8, r1)
+        gain_scales = placed("gain_scales", [P, S], U8, r2)
 
         def chunk_of(entries, c):
             return entries[:, c * CHUNK // 16 : (c + 1) * CHUNK // 16]
@@ -398,7 +398,6 @@ def tile_list_scheduled_gain_mixing_kernel(
         quantize_ws(0)
         gather_words(reference_words[1][:], chunk_of(lists[1], 1))
         gather_words(state_words[1][:], chunk_of(lists[0], 1))
-        gather_scales(gain_scales[:], lists[2][:])
 
         turn_limits(0)
         for t in range(PACK):
@@ -409,9 +408,10 @@ def tile_list_scheduled_gain_mixing_kernel(
             stage(t, 0)
             if t < PACK - 1:
                 clamp(nc.gpsimd, t, 0, 1, staged(t, 0))
-            if t in (1, 2):
-                round_ws(3, 2 * (t - 1), 2 * t)
-        quantize_ws(1)
+            if t == 0:
+                round_ws(3, 0, PACK)
+                quantize_ws(1)
+        gather_scales(gain_scales[:], lists[2][:])
         for c in range(CHUNKS):
             gather_words(gain_words[c][:], chunk_of(lists[2], c))
         demand(PACK - 1, 1)

@@ -33,6 +33,7 @@ DEMAND_BANKS, GAIN_BANKS = ("demand", 4), ("gain", 4)
 RAW_WS = (0, 8192, 20480)
 LATE_DEMAND = 57344
 EARLY_DEMAND = 32768
+LATE_H = 73728
 
 
 def tile_list_scheduled_gain_mixing_kernel(
@@ -271,98 +272,108 @@ def tile_list_scheduled_gain_mixing_kernel(
                 ALU.max,
             )
 
-        h = [held("h%d" % g, [P, PASSES * PACK * GROUP], BF16) for g in range(GROUPS)]
-        h_codes = [
-            placed("h_codes%d" % g, [P, PASSES * GROUP], U32, LATE_DEMAND + 3072 + 4 * PASSES * GROUP * g)
-            for g in range(GROUPS)
-        ]
-        h_scales = [held("h_scales%d" % g, [P, PASSES * GROUP], U8) for g in range(GROUPS)]
+        h_early = [held("h%d" % g, [P, PASSES * PACK * GROUP], BF16) for g in range(2)]
+        h_late = [placed("h_late0", [P, PACK * GROUP], BF16, LATE_H), held("h_late1", [P, PACK * GROUP], BF16)]
+        h_third = held("h_third", [P, PACK * GROUP], BF16)
+        h_units = [held("h_unit0", [P, PACK * UNIT], BF16), placed("h_unit1", [P, PACK * UNIT], BF16, LATE_H)]
+        h_codes = placed("h_codes", [P, PASSES * S], U32, LATE_DEMAND + 3072)
+        h_scales = held("h_scales", [P, PASSES * S], U8)
+
+        def h_rows(b, j0, width):
+            g, within = divmod(j0, GROUP)
+            if j0 < CHUNK:
+                tile, first = h_early[g], b * GROUP + within
+            elif b == 0:
+                tile, first = h_late[g - 2], within
+            elif j0 < S - GROUP:
+                tile, first = h_third, within
+            else:
+                tile, first = h_units[within // UNIT], 0
+            return tile[:, PACK * first : PACK * (first + width)]
+
+        def word_of(b, j0):
+            if j0 < CHUNK:
+                return j0 // GROUP * PASSES * GROUP + b * GROUP + j0 % GROUP
+            return S + b * CHUNK + j0 - CHUNK
 
         order = [(b, j0) for b in range(PASSES) for j0 in range(0, S, UNIT)]
+        pool_unit = order.pop()
         gains = []
+
+        def gain(b, j0, ring):
+            total = bank("gain", [P, PACK, UNIT], ring)
+            for t in range(PACK):
+                nc.tensor.matmul_mx(
+                    out=total[:, t, :],
+                    lhsT=wg_codes[b][:, t * P : (t + 1) * P].bitcast(FP8X4),
+                    lhsT_scale=wg_scale_tile[b][:].bitcast(U8)[:, t * P : (t + 1) * P],
+                    rhs=gain_words[j0 // CHUNK][:, j0 % CHUNK : j0 % CHUNK + UNIT].bitcast(FP8X4),
+                    rhs_scale=gain_scales[:, j0 : j0 + UNIT],
+                    start=True,
+                    stop=True,
+                )
+            return total
 
         def queue_gain():
             if len(gains) < len(order):
-                b, j0 = order[len(gains)]
-                gain = bank("gain", [P, PACK, UNIT], GAIN_BANKS)
-                for t in range(PACK):
-                    nc.tensor.matmul_mx(
-                        out=gain[:, t, :],
-                        lhsT=wg_codes[b][:, t * P : (t + 1) * P].bitcast(FP8X4),
-                        lhsT_scale=wg_scale_tile[b][:].bitcast(U8)[:, t * P : (t + 1) * P],
-                        rhs=gain_words[j0 // CHUNK][:, j0 % CHUNK : j0 % CHUNK + UNIT].bitcast(FP8X4),
-                        rhs_scale=gain_scales[:, j0 : j0 + UNIT],
-                        start=True,
-                        stop=True,
-                    )
-                gains.append(gain)
+                gains.append(gain(*order[len(gains)], GAIN_BANKS))
 
-        def product(k):
-            b, j0 = order[k]
+        def multiply(engine, b, j0, gain_rows):
             c, within = divmod(j0, CHUNK)
-            g, word = j0 // GROUP, b * GROUP + j0 % GROUP
-            nc.vector.tensor_tensor(
-                h[g][:, PACK * word : PACK * (word + UNIT)].rearrange("p (h l t) -> p h t l", l=4, t=PACK),
+            engine.tensor_tensor(
+                h_rows(b, j0, UNIT).rearrange("p (h l t) -> p h t l", l=4, t=PACK),
                 clamped[b][:, c, :, within : within + UNIT].rearrange("p t (h l) -> p h t l", l=4),
-                gains[k][:].rearrange("p t (h l) -> p h t l", l=4),
+                gain_rows.rearrange("p t (h l) -> p h t l", l=4),
                 ALU.mult,
             )
+
+        def product(k):
+            multiply(nc.vector, *order[k], gains[k][:])
             queue_gain()
 
-        def finish_group(g):
-            for j0 in range(g * GROUP, (g + 1) * GROUP, UNIT):
-                product(order.index((1, j0)))
-
-        def quantize_h(g, first, last):
+        def quantize_h(b, j0, width):
+            words = slice(word_of(b, j0), word_of(b, j0) + width)
             nc.vector.quantize_mx(
-                out=h_codes[g][:, first:last].bitcast(FP8X4),
-                scales=h_scales[g][:, first:last],
-                in_=h[g][:, PACK * first : PACK * last],
+                out=h_codes[:, words].bitcast(FP8X4), scales=h_scales[:, words], in_=h_rows(b, j0, width)
             )
 
-        def mix_pass(total, g, n, b, first, last, start, stop):
+        def mix_pass(total, n, b, j0, width, start, stop):
             cols = slice(b * N + n * P, b * N + (n + 1) * P)
-            words = slice(b * GROUP + first, b * GROUP + last)
+            words = slice(word_of(b, j0), word_of(b, j0) + width)
             nc.tensor.matmul_mx(
-                out=total[:, first:last],
+                out=total[:, j0 % GROUP : j0 % GROUP + width],
                 lhsT=wm_codes[:, cols].bitcast(FP8X4),
                 lhsT_scale=wm_scales[:, cols],
-                rhs=h_codes[g][:, words].bitcast(FP8X4),
-                rhs_scale=h_scales[g][:, words],
+                rhs=h_codes[:, words].bitcast(FP8X4),
+                rhs_scale=h_scales[:, words],
                 start=start,
                 stop=stop,
             )
 
-        def mix(g, tiles_per_store):
+        def open_mix(g, ring):
+            sums = [bank("mix", [P, GROUP], ring) for n in range(N_TILES)]
+            for n in range(N_TILES):
+                mix_pass(sums[n], n, 0, g * GROUP, GROUP, True, False)
+            return sums
+
+        def close_mix(g, sums):
+            for n in range(N_TILES):
+                mix_pass(sums[n], n, 1, g * GROUP, GROUP, False, True)
+
+        def store(g, sums, tiles_per_store, on_vector):
             results = [
                 held("result%d_%d" % (g, n), [P, tiles_per_store, GROUP], F32)
                 for n in range(0, N_TILES, tiles_per_store)
             ]
-            sums = [bank("mix", [P, GROUP], DEMAND_BANKS) for n in range(N_TILES)]
-            for b in range(PASSES):
-                for n in range(N_TILES):
-                    mix_pass(sums[n], g, n, b, 0, GROUP, b == 0, b == PASSES - 1)
             for n in range(N_TILES):
-                store, row = divmod(n, tiles_per_store)
-                nc.scalar.activation(results[store][:, row, :], sums[n][:], ACT.Identity, bias=trims[:, n : n + 1])
+                place, row = divmod(n, tiles_per_store)
+                if n in on_vector:
+                    nc.vector.tensor_scalar(results[place][:, row, :], sums[n][:], trims[:, n : n + 1], None, ALU.add)
+                else:
+                    nc.scalar.activation(results[place][:, row, :], sums[n][:], ACT.Identity, bias=trims[:, n : n + 1])
                 if row == tiles_per_store - 1:
                     rows = out[(n - row) * P : (n + 1) * P, g * GROUP : (g + 1) * GROUP]
-                    nc.sync.dma_start(rows.rearrange("(n p) j -> p n j", p=P), results[store][:])
-
-        def mix_last(g):
-            sums = [bank("mix", [P, GROUP], GAIN_BANKS) for n in range(N_TILES)]
-            for n in range(N_TILES):
-                mix_pass(sums[n], g, n, 0, 0, GROUP, True, False)
-            for first in range(0, GROUP, UNIT):
-                for n in range(N_TILES):
-                    mix_pass(sums[n], g, n, 1, first, first + UNIT, False, first + UNIT == GROUP)
-            for n in range(N_TILES):
-                result = held("last_result%d" % n, [P, GROUP], F32)
-                if n % 2 == 0:
-                    nc.vector.tensor_scalar(result[:], sums[n][:], trims[:, n : n + 1], None, ALU.add)
-                else:
-                    nc.scalar.activation(result[:], sums[n][:], ACT.Identity, bias=trims[:, n : n + 1])
-                nc.sync.dma_start(out[n * P : (n + 1) * P, g * GROUP : (g + 1) * GROUP], result[:])
+                    nc.sync.dma_start(rows.rearrange("(n p) j -> p n j", p=P), results[place][:])
 
         def regroup_limits(b):
             nc.gpsimd.tensor_scalar(
@@ -443,21 +454,34 @@ def tile_list_scheduled_gain_mixing_kernel(
                 demand(u, 1)
                 clamp(nc.gpsimd, u, 1, 1, staged(u, 1))
 
+        pool_gain = gain(*pool_unit, DEMAND_BANKS)
         round_wm(0)
         round_wm(1)
-        finish_group(0)
-        finish_group(1)
+        staged_gain = held("staged_gain", [P, PACK, UNIT], F32)
+        nc.scalar.copy(staged_gain[:], pool_gain[:])
+        for k in range(S // UNIT, S // UNIT + CHUNK // UNIT):
+            product(k)
         quantize_h(0, 0, PASSES * GROUP)
         quantize_wm(0)
         quantize_wm(1)
-        quantize_h(1, 0, PASSES * GROUP)
-        mix(0, N_TILES)
-        mix(1, N_TILES)
-        finish_group(2)
-        quantize_h(3, 0, GROUP)
-        quantize_h(2, 0, PASSES * GROUP)
-        mix(2, 1)
-        finish_group(3)
-        quantize_h(3, GROUP, GROUP + UNIT)
-        quantize_h(3, GROUP + UNIT, PASSES * GROUP)
-        mix_last(3)
+        quantize_h(0, GROUP, PASSES * GROUP)
+        for g in range(2):
+            sums = open_mix(g, DEMAND_BANKS)
+            close_mix(g, sums)
+            store(g, sums, N_TILES, ())
+        quantize_h(0, CHUNK, GROUP)
+        multiply(nc.gpsimd, *pool_unit, staged_gain[:])
+        third = open_mix(2, DEMAND_BANKS)
+        for k in range(S // UNIT + CHUNK // UNIT, len(order)):
+            product(k)
+        quantize_h(1, CHUNK, GROUP)
+        close_mix(2, third)
+        store(2, third, 1, ())
+        quantize_h(0, S - GROUP, GROUP)
+        quantize_h(1, S - UNIT, UNIT)
+        quantize_h(1, S - GROUP, UNIT)
+        last = [bank("mix", [P, GROUP], ring) for ring in (GAIN_BANKS, DEMAND_BANKS, DEMAND_BANKS)]
+        for n in range(N_TILES):
+            for b in range(PASSES):
+                mix_pass(last[n], n, b, S - GROUP, GROUP, b == 0, b == PASSES - 1)
+        store(3, last, 1, (0, 2))

@@ -196,20 +196,17 @@ def tile_list_scheduled_gain_mixing_kernel(
 
         wm_codes = placed("wm_codes", [P, PASSES * N], U32, LATE_DEMAND)
         wm_scales = held("wm_scales", [P, PASSES * N], U8)
-        wm_rounded = placed("wm_rounded", [P, PASSES * N * PACK], BF16, r1 + 3072 + 2048 - 64)
+        wm_rounded = placed("wm_rounded", [P, (PASSES * N - P) * PACK], BF16, r1 + 3072 + 2048 - 64)
+        wm_rounded_last = placed("wm_rounded_last", [P, P * PACK], BF16, LATE_DEMAND + 3072 + 4 * PASSES * S)
 
-        def round_wm(b):
+        def round_wm(b, width):
             nc.scalar.copy(
-                wm_rounded[:, b * N * PACK : (b + 1) * N * PACK].rearrange("p (h l t) -> p h t l", l=4, t=PACK),
-                wm_raw[b][:].rearrange("p t (h l) -> p h t l", l=4),
+                wm_rounded[:, PACK * b * N : PACK * (b * N + width)].rearrange("p (h l t) -> p h t l", l=4, t=PACK),
+                wm_raw[b][:, :, :width].rearrange("p t (h l) -> p h t l", l=4),
             )
 
-        def quantize_wm(b):
-            nc.vector.quantize_mx(
-                out=wm_codes[:, b * N : (b + 1) * N].bitcast(FP8X4),
-                scales=wm_scales[:, b * N : (b + 1) * N],
-                in_=wm_rounded[:, PACK * b * N : PACK * (b + 1) * N],
-            )
+        def quantize_wm(first, last, rounded):
+            nc.vector.quantize_mx(out=wm_codes[:, first:last].bitcast(FP8X4), scales=wm_scales[:, first:last], in_=rounded)
 
         demand_early = [
             [placed("demand%d_%d" % (t, c), [P, CHUNK], F32, EARLY_DEMAND + 3072 * (PACK * c + t)) for c in range(CHUNKS)]
@@ -455,15 +452,24 @@ def tile_list_scheduled_gain_mixing_kernel(
                 clamp(nc.gpsimd, u, 1, 1, staged(u, 1))
 
         pool_gain = gain(*pool_unit, DEMAND_BANKS)
-        round_wm(0)
-        round_wm(1)
+        round_wm(0, N)
+        round_wm(1, N - P)
+        nc.gpsimd.tensor_scalar(
+            wm_rounded_last[:].rearrange("p (n t) -> p n t", t=PACK),
+            wm_raw[1][:, :, N - P :].rearrange("p t n -> p n t"),
+            1.0,
+            0.0,
+            ALU.mult,
+            ALU.add,
+        )
         staged_gain = held("staged_gain", [P, PACK, UNIT], F32)
         nc.scalar.copy(staged_gain[:], pool_gain[:])
         for k in range(S // UNIT, S // UNIT + CHUNK // UNIT):
             product(k)
         quantize_h(0, 0, PASSES * GROUP)
-        quantize_wm(0)
-        quantize_wm(1)
+        quantize_wm(0, N, wm_rounded[:, : PACK * N])
+        quantize_wm(N, PASSES * N - P, wm_rounded[:, PACK * N :])
+        quantize_wm(PASSES * N - P, PASSES * N, wm_rounded_last[:])
         quantize_h(0, GROUP, PASSES * GROUP)
         for g in range(2):
             sums = open_mix(g, DEMAND_BANKS)
@@ -476,10 +482,10 @@ def tile_list_scheduled_gain_mixing_kernel(
             product(k)
         quantize_h(1, CHUNK, GROUP)
         close_mix(2, third)
-        store(2, third, 1, ())
         quantize_h(0, S - GROUP, GROUP)
         quantize_h(1, S - UNIT, UNIT)
         quantize_h(1, S - GROUP, UNIT)
+        store(2, third, 1, (2,))
         last = [bank("mix", [P, GROUP], ring) for ring in (GAIN_BANKS, DEMAND_BANKS, DEMAND_BANKS)]
         for n in range(N_TILES):
             for b in range(PASSES):

@@ -28,6 +28,7 @@ GROUP = 256
 GROUPS = S // GROUP
 N_TILES = N // P
 LO, HI = 0, 1
+NARROW = 2
 DEMAND_BANKS, GAIN_BANKS = ("demand", 4), ("gain", 4)
 
 RAW_WS = (0, 8192, 20480)
@@ -153,7 +154,7 @@ def tile_list_scheduled_gain_mixing_kernel(
 
         wr_codes = [held("wr_codes%d" % b, [P, HALF // 2], I32) for b in range(PASSES)]
         wr_scale_tile = [held("wr_scale_tile%d" % b, [P, HALF // 4], I32) for b in range(PASSES)]
-        wg_at = [EARLY_DEMAND + 3072 * 2, EARLY_DEMAND + 3072 * 5]
+        wg_at = [EARLY_DEMAND + 3072 * 1, EARLY_DEMAND + 3072 * 5]
         wg_codes = [placed("wg_codes%d" % b, [P, HALF], I32, wg_at[b] + 512) for b in range(PASSES)]
         wg_scale_tile = [placed("wg_scale_tile%d" % b, [P, HALF // 4], I32, wg_at[b]) for b in range(PASSES)]
         ws_codes = [held("ws_codes%d" % b, [P, HALF], U32) for b in range(PASSES)]
@@ -210,17 +211,17 @@ def tile_list_scheduled_gain_mixing_kernel(
 
         demand_early = [
             [placed("demand%d_%d" % (t, c), [P, CHUNK], F32, EARLY_DEMAND + 3072 * (PACK * c + t)) for c in range(CHUNKS)]
-            for t in range(PACK - 1)
+            for t in range(NARROW)
         ]
-        demand_wide = held("demand_wide", [P, S], F32)
+        demand_wide = {t: held("demand_wide%d" % t, [P, S], F32) for t in range(NARROW, PACK)}
         demand_late = placed("demand_late", [P, 3 * S + CHUNK], F32, LATE_DEMAND)
         clamped = [held("clamped%d" % b, [P, CHUNKS, PACK, CHUNK], F32) for b in range(PASSES)]
 
         def staged(u, c):
-            if u < PACK - 1:
+            if u < NARROW:
                 return demand_early[u][c][:]
             if u < PACK:
-                return demand_wide[:, c * CHUNK : (c + 1) * CHUNK]
+                return demand_wide[u][:, c * CHUNK : (c + 1) * CHUNK]
             first = (u - PACK) * S + c * CHUNK if u < PACK + 3 else 3 * S
             return demand_late[:, first : first + CHUNK]
 
@@ -413,20 +414,22 @@ def tile_list_scheduled_gain_mixing_kernel(
         round_ws(2, 0, PACK)
         for t in range(PACK):
             close_demand(t, 0)
-            stage(t, 0)
-            if t < PACK - 1:
-                clamp(nc.gpsimd, t, 0, 1, staged(t, 0))
-            if t == 0:
-                round_ws(3, 0, PACK)
-                quantize_ws(1)
+        stage(0, 0)
+        clamp(nc.gpsimd, 0, 0, 1, staged(0, 0))
+        round_ws(3, 0, PACK)
+        quantize_ws(1)
         gather_scales(gain_scales[:], lists[2][:])
         for c in range(CHUNKS):
             gather_words(gain_words[c][:], chunk_of(lists[2], c))
-        demand(PACK - 1, 1)
-        clamp(nc.gpsimd, PACK - 1, 0, CHUNKS, demand_wide[:])
+        stage(1, 0)
+        clamp(nc.gpsimd, 1, 0, 1, staged(1, 0))
+        for t in range(NARROW, PACK):
+            stage(t, 0)
+            demand(t, 1)
+            clamp(nc.gpsimd, t, 0, CHUNKS, demand_wide[t][:])
         turn_limits(1)
-        for t in range(PACK - 1):
-            if t == PACK - 2:
+        for t in range(NARROW):
+            if t == NARROW - 1:
                 regroup_wg(0)
             demand(t, 1)
             clamp(nc.gpsimd, t, 1, 1, staged(t, 1))

@@ -29,6 +29,7 @@ GROUPS = S // GROUP
 N_TILES = N // P
 LO, HI = 0, 1
 NARROW = 2
+DMA_ALIGN = 256
 DEMAND_BANKS, GAIN_BANKS = ("demand", 4), ("gain", 4)
 
 RAW_WS = (0, 8192, 20480)
@@ -46,31 +47,31 @@ def tile_list_scheduled_gain_mixing_kernel(
         shared = ctx.enter_context(tc.tile_pool(name="shared", bufs=1))
         psum = ctx.enter_context(tc.psum_pool(name="psum", bufs=1))
 
-        def held(name, shape, dtype):
-            return keep.tile(shape, dtype, name=name, align_bytes=64)
+        def held(name, shape, dtype, align=64):
+            return keep.tile(shape, dtype, name=name, align_bytes=align)
 
-        def placed(name, shape, dtype, offset):
-            return shared.tile(shape, dtype, name=name, align_bytes=64, offset=offset)
+        def placed(name, shape, dtype, offset, align=64):
+            return shared.tile(shape, dtype, name=name, align_bytes=align, offset=offset)
 
         def bank(name, shape, ring):
             return psum.tile(shape, F32, name=name, tag=ring[0], bufs=ring[1])
 
         lists = [held("list%d" % i, [P, S // 16], U16) for i in range(3)]
-        table_words = held("table_words", [P, T], I32)
-        table_scales = held("table_scales", [P, T // 4], I32)
-        wr_raw_scales = held("wr_raw_scales", [P, H // 4], I32)
-        wg_raw_scales = held("wg_raw_scales", [P, H // 4], I32)
-        wr_raw = [held("wr_raw%d" % b, [P, HALF // 2], I32) for b in range(PASSES)]
-        wg_raw = held("wg_raw", [P, H], I32)
+        table_words = held("table_words", [P, T], I32, DMA_ALIGN)
+        table_scales = held("table_scales", [P, T // 4], I32, DMA_ALIGN)
+        wr_raw_scales = held("wr_raw_scales", [P, H // 4], I32, DMA_ALIGN)
+        wg_raw_scales = held("wg_raw_scales", [P, H // 4], I32, DMA_ALIGN)
+        wr_raw = [held("wr_raw%d" % b, [P, HALF // 2], I32, DMA_ALIGN) for b in range(PASSES)]
+        wg_raw = held("wg_raw", [P, H], I32, DMA_ALIGN)
         ws_pieces = [(b, a, a + HALF // 2) for b in range(PASSES) for a in (0, HALF // 2)]
         ws_raw = [
-            placed("ws_raw0", [P, PACK, HALF // 2], F32, RAW_WS[0]),
-            placed("ws_raw1", [P, PACK, HALF // 2], F32, RAW_WS[1]),
-            held("ws_raw2", [P, PACK, HALF // 2], F32),
-            placed("ws_raw3", [P, PACK, HALF // 2], F32, RAW_WS[2]),
+            placed("ws_raw0", [P, PACK, HALF // 2], F32, RAW_WS[0], DMA_ALIGN),
+            placed("ws_raw1", [P, PACK, HALF // 2], F32, RAW_WS[1], DMA_ALIGN),
+            held("ws_raw2", [P, PACK, HALF // 2], F32, DMA_ALIGN),
+            placed("ws_raw3", [P, PACK, HALF // 2], F32, RAW_WS[2], DMA_ALIGN),
         ]
-        wm_raw = [held("wm_raw%d" % b, [P, PACK, N], F32) for b in range(PASSES)]
-        limits_raw = held("limits_raw", [2, H], F32)
+        wm_raw = [held("wm_raw%d" % b, [P, PACK, N], F32, DMA_ALIGN) for b in range(PASSES)]
+        limits_raw = held("limits_raw", [2, H], F32, DMA_ALIGN)
         limit_rows = held("limit_rows", [P, H], F32)
         identity = held("identity", [P, P], F32)
 
@@ -360,7 +361,7 @@ def tile_list_scheduled_gain_mixing_kernel(
 
         def store(g, sums, tiles_per_store, on_vector):
             results = [
-                held("result%d_%d" % (g, n), [P, tiles_per_store, GROUP], F32)
+                held("result%d_%d" % (g, n), [P, tiles_per_store, GROUP], F32, DMA_ALIGN)
                 for n in range(0, N_TILES, tiles_per_store)
             ]
             for n in range(N_TILES):

from contextlib import ExitStack

import concourse.mybir as mybir
from concourse.masks import make_identity

K, T, S, H, N = 512, 2048, 1024, 1024, 384
FLOPS = 2 * S * H * (3 * K + N)

F32 = mybir.dt.float32
BF16 = mybir.dt.bfloat16
I32 = mybir.dt.int32
U32 = mybir.dt.uint32
U16 = mybir.dt.uint16
U8 = mybir.dt.uint8
FP8X4 = mybir.dt.float8_e4m3fn_x4
FP4X4 = mybir.dt.float4_e2m1fn_x4
ALU = mybir.AluOpType
ACT = mybir.ActivationFunctionType

P = 128
PACK = 4
HALF = 512
PASSES = H // HALF
CHUNK = 512
CHUNKS = S // CHUNK
UNIT = 128
GROUP = 256
GROUPS = S // GROUP
N_TILES = N // P
LO, HI = 0, 1
NARROW = 2
DMA_ALIGN = 256
DEMAND_BANKS, GAIN_BANKS = ("demand", 4), ("gain", 4)

RAW_WS = (0, 8192, 20480)
LATE_DEMAND = 57344
EARLY_DEMAND = 32768
LATE_H = 73728


def tile_list_scheduled_gain_mixing_kernel(
    tc, tab_words, tab_scales, offs, offs2, offs3, ws, wr_words, wr_scales, wg_words, wg_scales, lo, hi, wm, trim, out
):
    nc = tc.nc
    with ExitStack() as ctx:
        keep = ctx.enter_context(tc.tile_pool(name="keep", bufs=1))
        shared = ctx.enter_context(tc.tile_pool(name="shared", bufs=1))
        psum = ctx.enter_context(tc.psum_pool(name="psum", bufs=1))

        def held(name, shape, dtype, align=64):
            return keep.tile(shape, dtype, name=name, align_bytes=align)

        def placed(name, shape, dtype, offset, align=64):
            return shared.tile(shape, dtype, name=name, align_bytes=align, offset=offset)

        def bank(name, shape, ring):
            return psum.tile(shape, F32, name=name, tag=ring[0], bufs=ring[1])

        lists = [held("list%d" % i, [P, S // 16], U16) for i in range(3)]
        table_words = held("table_words", [P, T], I32, DMA_ALIGN)
        table_scales = held("table_scales", [P, T // 4], I32, DMA_ALIGN)
        wr_raw_scales = held("wr_raw_scales", [P, H // 4], I32, DMA_ALIGN)
        wg_raw_scales = held("wg_raw_scales", [P, H // 4], I32, DMA_ALIGN)
        wr_raw = [held("wr_raw%d" % b, [P, HALF // 2], I32, DMA_ALIGN) for b in range(PASSES)]
        wg_raw = held("wg_raw", [P, H], I32, DMA_ALIGN)
        ws_pieces = [(b, a, a + HALF // 2) for b in range(PASSES) for a in (0, HALF // 2)]
        ws_raw = [
            placed("ws_raw0", [P, PACK, HALF // 2], F32, RAW_WS[0], DMA_ALIGN),
            placed("ws_raw1", [P, PACK, HALF // 2], F32, RAW_WS[1], DMA_ALIGN),
            held("ws_raw2", [P, PACK, HALF // 2], F32, DMA_ALIGN),
            placed("ws_raw3", [P, PACK, HALF // 2], F32, RAW_WS[2], DMA_ALIGN),
        ]
        wm_raw = [held("wm_raw%d" % b, [P, PACK, N], F32, DMA_ALIGN) for b in range(PASSES)]
        limits_raw = held("limits_raw", [2, H], F32, DMA_ALIGN)
        limit_rows = held("limit_rows", [P, H], F32)
        identity = held("identity", [P, P], F32)

        nc.gpsimd.memset(table_scales[:], 0)
        nc.gpsimd.memset(limit_rows[:], 0.0)
        nc.vector.memset(wr_raw_scales[:], 0)
        nc.vector.memset(wg_raw_scales[:], 0)

        def load_scale_rows(scale_tile, scales, queues):
            by_row = scales[0].rearrange("(q r) n -> r q n", r=4)
            for r in range(4):
                queues[r % len(queues)].dma_start(scale_tile[r:P:32, :], by_row[r].bitcast(I32))

        def load_ws(i):
            b, a, z = ws_pieces[i]
            nc.sync.dma_start(ws_raw[i][:], ws[:, b * HALF + a : b * HALF + z].rearrange("(p j) c -> p j c", j=PACK))

        def load_wr(b):
            nc.sync.dma_start(wr_raw[b][:], wr_words[0, :, b * 2 * HALF : (b + 1) * 2 * HALF].bitcast(I32))

        def load_limits(row, vector):
            nc.sync.dma_start(limits_raw[row : row + 1, :], vector.rearrange("(o r) -> o r", o=1))

        make_identity(nc, identity[:])
        nc.sync.dma_start(lists[1][:], offs2)
        nc.sync.dma_start(lists[0][:], offs)
        load_scale_rows(table_scales, tab_scales, (nc.scalar, nc.sync, nc.sync, nc.sync))
        load_limits(LO, lo)
        nc.sync.dma_start(table_words[:], tab_words[0].rearrange("p n t -> p (n t)").bitcast(I32))
        load_wr(0)
        load_limits(HI, hi)
        load_ws(0)
        load_scale_rows(wr_raw_scales, wr_scales, (nc.sync,))
        load_ws(1)
        load_wr(1)
        load_ws(2)
        load_ws(3)
        nc.sync.dma_start(lists[2][:], offs3)
        nc.sync.dma_start(wg_raw[:], wg_words[0].rearrange("p n t -> p (n t)").bitcast(I32))
        load_scale_rows(wg_raw_scales, wg_scales, (nc.sync,))
        for b in range(PASSES):
            wm_rows = wm[b * HALF : (b + 1) * HALF, :].rearrange("(q t i) n -> t q i n", t=PACK, i=8)
            for t in range(PACK):
                nc.sync.dma_start(wm_raw[b][:, t, :], wm_rows[t])
        trims = held("trims", [P, N_TILES], F32)
        with nc.allow_non_contiguous_dma(reason="one trim value for each partition and output tile"):
            nc.sync.dma_start(trims[:], trim.rearrange("(n p) -> p n", p=P))

        limits = [held("limits%d" % b, [P, PACK, 2], F32) for b in range(PASSES)]

        r0, r1, r2 = RAW_WS
        ws_rounded = [held("ws_rounded%d" % b, [P, PACK, HALF], BF16) for b in range(PASSES)]
        state_words = [held("state_words0", [P, CHUNK], U32), placed("state_words1", [P, CHUNK], U32, r1 + 3072)]
        reference_words = [
            held("reference_words0", [P, CHUNK], U32),
            placed("reference_words1", [P, CHUNK], U32, r1 + 1024),
        ]
        gain_words = [
            placed("gain_words0", [P, CHUNK], U32, r2 + 3072),
            placed("gain_words1", [P, CHUNK], U32, r2 + 1024),
        ]
        state_scales = [held("state_scales0", [P, CHUNK], U8), placed("state_scales1", [P, CHUNK], U8, r0)]
        reference_scales = held("reference_scales", [P, S], U8)
        gain_scales = placed("gain_scales", [P, S], U8, r2)

        def chunk_of(entries, c):
            return entries[:, c * CHUNK // 16 : (c + 1) * CHUNK // 16]

        def gather_scales(picked, offsets):
            nc.vector.tensor_copy(picked, table_scales[:].bitcast(U8).indirect(offsets))

        def gather_words(picked, offsets):
            nc.vector.tensor_copy(picked, table_words[:].bitcast(U32).indirect(offsets))

        def regrouped(moved, raw, run, b):
            words = slice(b * 64 * run, (b + 1) * 64 * run)
            return (
                moved.rearrange("p (t q e) -> p t q e", t=PACK, e=run),
                raw[:, words].rearrange("p (q t e) -> p t q e", t=PACK, e=run),
            )

        wr_codes = [held("wr_codes%d" % b, [P, HALF // 2], I32) for b in range(PASSES)]
        wr_scale_tile = [held("wr_scale_tile%d" % b, [P, HALF // 4], I32) for b in range(PASSES)]
        wg_at = [EARLY_DEMAND + 3072 * 1, EARLY_DEMAND + 3072 * 5]
        wg_codes = [placed("wg_codes%d" % b, [P, HALF], I32, wg_at[b] + 512) for b in range(PASSES)]
        wg_scale_tile = [placed("wg_scale_tile%d" % b, [P, HALF // 4], I32, wg_at[b]) for b in range(PASSES)]
        ws_codes = [held("ws_codes%d" % b, [P, HALF], U32) for b in range(PASSES)]
        ws_scales = [held("ws_scales%d" % b, [P, HALF], U8) for b in range(PASSES)]

        def regroup_wr(move, b):
            move(*regrouped(wr_codes[b][:].bitcast(U32), wr_raw[b][:].bitcast(U32), 4, 0))

        def regroup_wr_scales(move, b):
            move(*regrouped(wr_scale_tile[b][:].bitcast(U32), wr_raw_scales[:].bitcast(U32), 2, b))

        def regroup_wg(b):
            nc.scalar.copy(*regrouped(wg_codes[b][:].bitcast(U32), wg_raw[:].bitcast(U32), 8, b))
            nc.scalar.copy(*regrouped(wg_scale_tile[b][:].bitcast(U32), wg_raw_scales[:].bitcast(U32), 2, b))

        def round_ws(i, first, last):
            b, a, z = ws_pieces[i]
            nc.scalar.copy(
                ws_rounded[b][:, first:last, a:z].rearrange("p t (q l j) -> p t q j l", l=8, j=PACK),
                ws_raw[i][:].rearrange("p j (q t l) -> p t q j l", t=PACK, l=8)[:, first:last],
            )

        def round_ws_on_gpsimd(i, first, last):
            b, a, z = ws_pieces[i]
            nc.gpsimd.tensor_scalar(
                ws_rounded[b][:, first:last, a:z].rearrange("p t (q l j) -> p q t l j", l=8, j=PACK),
                ws_raw[i][:].rearrange("p j (q t l) -> p q t l j", t=PACK, l=8)[:, :, first:last],
                1.0,
                0.0,
                ALU.mult,
                ALU.add,
            )

        def quantize_ws(b):
            nc.vector.quantize_mx(
                out=ws_codes[b][:].bitcast(FP8X4),
                scales=ws_scales[b][:],
                in_=ws_rounded[b][:].rearrange("p t c -> p (t c)"),
            )

        wm_codes = placed("wm_codes", [P, PASSES * N], U32, LATE_DEMAND)
        wm_scales = held("wm_scales", [P, PASSES * N], U8)
        wm_rounded = placed("wm_rounded", [P, (PASSES * N - P) * PACK], BF16, r1 + 3072 + 2048 - 64)
        wm_rounded_last = placed("wm_rounded_last", [P, P * PACK], BF16, LATE_DEMAND + 3072 + 4 * PASSES * S)

        def round_wm(b, width):
            nc.scalar.copy(
                wm_rounded[:, PACK * b * N : PACK * (b * N + width)].rearrange("p (h l t) -> p h t l", l=4, t=PACK),
                wm_raw[b][:, :, :width].rearrange("p t (h l) -> p h t l", l=4),
            )

        def quantize_wm(first, last, rounded):
            nc.vector.quantize_mx(out=wm_codes[:, first:last].bitcast(FP8X4), scales=wm_scales[:, first:last], in_=rounded)

        demand_early = [
            [placed("demand%d_%d" % (t, c), [P, CHUNK], F32, EARLY_DEMAND + 3072 * (PACK * c + t)) for c in range(CHUNKS)]
            for t in range(NARROW)
        ]
        demand_wide = {t: held("demand_wide%d" % t, [P, S], F32) for t in range(NARROW, PACK)}
        demand_late = placed("demand_late", [P, 3 * S + CHUNK], F32, LATE_DEMAND)
        clamped = [held("clamped%d" % b, [P, CHUNKS, PACK, CHUNK], F32) for b in range(PASSES)]

        def staged(u, c):
            if u < NARROW:
                return demand_early[u][c][:]
            if u < PACK:
                return demand_wide[u][:, c * CHUNK : (c + 1) * CHUNK]
            first = (u - PACK) * S + c * CHUNK if u < PACK + 3 else 3 * S
            return demand_late[:, first : first + CHUNK]

        open_sums = {}

        def open_demand(u, c, ring=DEMAND_BANKS):
            open_sums[u, c] = bank("demand", [P, CHUNK], ring)
            nc.tensor.matmul_mx(
                out=open_sums[u, c][:],
                lhsT=wr_codes[u // PACK][:].bitcast(U8)[:, 2 * (u % PACK) * P : 2 * (u % PACK + 1) * P].bitcast(FP4X4),
                lhsT_scale=wr_scale_tile[u // PACK][:].bitcast(U8)[:, (u % PACK) * P : (u % PACK + 1) * P],
                rhs=reference_words[c][:].bitcast(FP8X4),
                rhs_scale=reference_scales[:, c * CHUNK : (c + 1) * CHUNK],
                start=True,
                stop=False,
            )

        def close_demand(u, c):
            b, t = divmod(u, PACK)
            nc.tensor.matmul_mx(
                out=open_sums[u, c][:],
                lhsT=ws_codes[b][:, t * P : (t + 1) * P].bitcast(FP8X4),
                lhsT_scale=ws_scales[b][:, t * P : (t + 1) * P],
                rhs=state_words[c][:].bitcast(FP8X4),
                rhs_scale=state_scales[c][:],
                start=False,
                stop=True,
            )

        def stage(u, c):
            nc.scalar.copy(staged(u, c), open_sums[u, c][:])

        def demand(u, c):
            open_demand(u, c)
            close_demand(u, c)
            stage(u, c)

        def clamp(engine, u, first_chunk, chunks, rows):
            b, t = divmod(u, PACK)
            engine.tensor_scalar(
                clamped[b][:, first_chunk : first_chunk + chunks, t, :],
                rows.rearrange("p (c j) -> p c j", j=CHUNK),
                limits[b][:, t, HI : HI + 1],
                limits[b][:, t, LO : LO + 1],
                ALU.min,
                ALU.max,
            )

        h_early = [held("h%d" % g, [P, PASSES * PACK * GROUP], BF16) for g in range(2)]
        h_late = [placed("h_late0", [P, PACK * GROUP], BF16, LATE_H), held("h_late1", [P, PACK * GROUP], BF16)]
        h_third = held("h_third", [P, PACK * GROUP], BF16)
        h_units = [held("h_unit0", [P, PACK * UNIT], BF16), placed("h_unit1", [P, PACK * UNIT], BF16, LATE_H)]
        h_codes = placed("h_codes", [P, PASSES * S], U32, LATE_DEMAND + 3072)
        h_scales = held("h_scales", [P, PASSES * S], U8)

        def h_rows(b, j0, width):
            g, within = divmod(j0, GROUP)
            if j0 < CHUNK:
                tile, first = h_early[g], b * GROUP + within
            elif b == 0:
                tile, first = h_late[g - 2], within
            elif j0 < S - GROUP:
                tile, first = h_third, within
            else:
                tile, first = h_units[within // UNIT], 0
            return tile[:, PACK * first : PACK * (first + width)]

        def word_of(b, j0):
            if j0 < CHUNK:
                return j0 // GROUP * PASSES * GROUP + b * GROUP + j0 % GROUP
            return S + b * CHUNK + j0 - CHUNK

        order = [(b, j0) for b in range(PASSES) for j0 in range(0, S, UNIT)]
        pool_unit = order.pop()
        gains = []

        def gain(b, j0, ring):
            total = bank("gain", [P, PACK, UNIT], ring)
            for t in range(PACK):
                nc.tensor.matmul_mx(
                    out=total[:, t, :],
                    lhsT=wg_codes[b][:, t * P : (t + 1) * P].bitcast(FP8X4),
                    lhsT_scale=wg_scale_tile[b][:].bitcast(U8)[:, t * P : (t + 1) * P],
                    rhs=gain_words[j0 // CHUNK][:, j0 % CHUNK : j0 % CHUNK + UNIT].bitcast(FP8X4),
                    rhs_scale=gain_scales[:, j0 : j0 + UNIT],
                    start=True,
                    stop=True,
                )
            return total

        def queue_gain():
            if len(gains) < len(order):
                gains.append(gain(*order[len(gains)], GAIN_BANKS))

        def multiply(engine, b, j0, gain_rows):
            c, within = divmod(j0, CHUNK)
            engine.tensor_tensor(
                h_rows(b, j0, UNIT).rearrange("p (h l t) -> p h t l", l=4, t=PACK),
                clamped[b][:, c, :, within : within + UNIT].rearrange("p t (h l) -> p h t l", l=4),
                gain_rows.rearrange("p t (h l) -> p h t l", l=4),
                ALU.mult,
            )

        def product(k):
            multiply(nc.vector, *order[k], gains[k][:])
            queue_gain()

        def quantize_h(b, j0, width):
            words = slice(word_of(b, j0), word_of(b, j0) + width)
            nc.vector.quantize_mx(
                out=h_codes[:, words].bitcast(FP8X4), scales=h_scales[:, words], in_=h_rows(b, j0, width)
            )

        def mix_pass(total, n, b, j0, width, start, stop):
            cols = slice(b * N + n * P, b * N + (n + 1) * P)
            words = slice(word_of(b, j0), word_of(b, j0) + width)
            nc.tensor.matmul_mx(
                out=total[:, j0 % GROUP : j0 % GROUP + width],
                lhsT=wm_codes[:, cols].bitcast(FP8X4),
                lhsT_scale=wm_scales[:, cols],
                rhs=h_codes[:, words].bitcast(FP8X4),
                rhs_scale=h_scales[:, words],
                start=start,
                stop=stop,
            )

        def open_mix(g, ring):
            sums = [bank("mix", [P, GROUP], ring) for n in range(N_TILES)]
            for n in range(N_TILES):
                mix_pass(sums[n], n, 0, g * GROUP, GROUP, True, False)
            return sums

        def close_mix(g, sums):
            for n in range(N_TILES):
                mix_pass(sums[n], n, 1, g * GROUP, GROUP, False, True)

        def store(g, sums, tiles_per_store, on_vector):
            results = [
                held("result%d_%d" % (g, n), [P, tiles_per_store, GROUP], F32, DMA_ALIGN)
                for n in range(0, N_TILES, tiles_per_store)
            ]
            for n in range(N_TILES):
                place, row = divmod(n, tiles_per_store)
                if n in on_vector:
                    nc.vector.tensor_scalar(results[place][:, row, :], sums[n][:], trims[:, n : n + 1], None, ALU.add)
                else:
                    nc.scalar.activation(results[place][:, row, :], sums[n][:], ACT.Identity, bias=trims[:, n : n + 1])
                if row == tiles_per_store - 1:
                    rows = out[(n - row) * P : (n + 1) * P, g * GROUP : (g + 1) * GROUP]
                    nc.sync.dma_start(rows.rearrange("(n p) j -> p n j", p=P), results[place][:])

        def regroup_limits(b):
            nc.gpsimd.tensor_scalar(
                limit_rows[0:2, b * HALF : (b + 1) * HALF].rearrange("p (t q i) -> p t q i", t=PACK, i=8),
                limits_raw[:, b * HALF : (b + 1) * HALF].rearrange("p (q t i) -> p t q i", t=PACK, i=8),
                1.0,
                0.0,
                ALU.mult,
                ALU.add,
            )

        def turn_limits(b):
            turned = bank("limits_turned", [P, PACK, P], GAIN_BANKS)
            for t in range(PACK):
                u = PACK * b + t
                nc.tensor.transpose(turned[:, t, :], limit_rows[:, u * P : (u + 1) * P], identity[:])
            nc.scalar.copy(limits[b][:], turned[:, :, 0:2])

        gather_scales(reference_scales[:], lists[1][:])
        gather_scales(state_scales[0][:], chunk_of(lists[0], 0))
        gather_words(reference_words[0][:], chunk_of(lists[1], 0))
        gather_words(state_words[0][:], chunk_of(lists[0], 0))
        regroup_wr(nc.scalar.copy, 0)
        for b in range(PASSES):
            regroup_limits(b)
        round_ws(0, 0, PACK)
        gather_scales(state_scales[1][:], chunk_of(lists[0], 1))
        regroup_wr_scales(nc.gpsimd.tensor_copy, 0)
        round_ws(1, 0, 2)
        round_ws_on_gpsimd(1, 2, PACK)
        regroup_wr(nc.scalar.copy, 1)
        regroup_wr_scales(nc.scalar.copy, 1)
        quantize_ws(0)
        gather_words(reference_words[1][:], chunk_of(lists[1], 1))
        gather_words(state_words[1][:], chunk_of(lists[0], 1))

        turn_limits(0)
        for t in range(PACK):
            open_demand(t, 0)
        round_ws(2, 0, PACK)
        for t in range(PACK):
            close_demand(t, 0)
        stage(0, 0)
        clamp(nc.gpsimd, 0, 0, 1, staged(0, 0))
        round_ws(3, 0, PACK)
        quantize_ws(1)
        gather_scales(gain_scales[:], lists[2][:])
        for c in range(CHUNKS):
            gather_words(gain_words[c][:], chunk_of(lists[2], c))
        stage(1, 0)
        clamp(nc.gpsimd, 1, 0, 1, staged(1, 0))
        for t in range(NARROW, PACK):
            stage(t, 0)
            demand(t, 1)
            clamp(nc.gpsimd, t, 0, CHUNKS, demand_wide[t][:])
        turn_limits(1)
        for t in range(NARROW):
            if t == NARROW - 1:
                regroup_wg(0)
            demand(t, 1)
            clamp(nc.gpsimd, t, 1, 1, staged(t, 1))
        open_demand(PACK + 3, 0, GAIN_BANKS)
        close_demand(PACK + 3, 0)
        clamp(nc.vector, PACK + 3, 0, 1, open_sums[PACK + 3, 0][:])
        demand(PACK + 2, 0)
        clamp(nc.gpsimd, PACK + 2, 0, 1, staged(PACK + 2, 0))
        for u in (PACK, PACK + 1):
            if u > PACK:
                for k in range(3):
                    queue_gain()
            for c in range(CHUNKS):
                demand(u, c)
            clamp(nc.gpsimd, u, 0, CHUNKS, demand_late[:, (u - PACK) * S : (u - PACK + 1) * S])
        regroup_wg(1)
        queue_gain()
        for k in range(S // UNIT):
            product(k)
            if k in (1, 2):
                u = PACK + 1 + k
                demand(u, 1)
                clamp(nc.gpsimd, u, 1, 1, staged(u, 1))

        pool_gain = gain(*pool_unit, DEMAND_BANKS)
        round_wm(0, N)
        round_wm(1, N - P)
        nc.gpsimd.tensor_scalar(
            wm_rounded_last[:].rearrange("p (n t) -> p n t", t=PACK),
            wm_raw[1][:, :, N - P :].rearrange("p t n -> p n t"),
            1.0,
            0.0,
            ALU.mult,
            ALU.add,
        )
        staged_gain = held("staged_gain", [P, PACK, UNIT], F32)
        nc.scalar.copy(staged_gain[:], pool_gain[:])
        for k in range(S // UNIT, S // UNIT + CHUNK // UNIT):
            product(k)
        quantize_h(0, 0, PASSES * GROUP)
        quantize_wm(0, N, wm_rounded[:, : PACK * N])
        quantize_wm(N, PASSES * N - P, wm_rounded[:, PACK * N :])
        quantize_wm(PASSES * N - P, PASSES * N, wm_rounded_last[:])
        quantize_h(0, GROUP, PASSES * GROUP)
        for g in range(2):
            sums = open_mix(g, DEMAND_BANKS)
            close_mix(g, sums)
            store(g, sums, N_TILES, ())
        quantize_h(0, CHUNK, GROUP)
        multiply(nc.gpsimd, *pool_unit, staged_gain[:])
        third = open_mix(2, DEMAND_BANKS)
        for k in range(S // UNIT + CHUNK // UNIT, len(order)):
            product(k)
        quantize_h(1, CHUNK, GROUP)
        close_mix(2, third)
        quantize_h(0, S - GROUP, GROUP)
        quantize_h(1, S - UNIT, UNIT)
        quantize_h(1, S - GROUP, UNIT)
        store(2, third, 1, (2,))
        last = [bank("mix", [P, GROUP], ring) for ring in (GAIN_BANKS, DEMAND_BANKS, DEMAND_BANKS)]
        for n in range(N_TILES):
            for b in range(PASSES):
                mix_pass(last[n], n, b, S - GROUP, GROUP, b == 0, b == PASSES - 1)
        store(3, last, 1, (0, 2))
